import numpy as np
import ml_dtypes


def mxq(x, axis, fmt="e4m3"):
    dtype, down = {"e4m3": (ml_dtypes.float8_e4m3fn, 7), "e5m2": (ml_dtypes.float8_e5m2, 14)}[fmt]
    v = np.moveaxis(np.asarray(x, np.float32).astype(ml_dtypes.bfloat16).astype(np.float64), axis, -1)
    blocks = v.reshape(v.shape[:-1] + (-1, 32))
    amax = np.abs(blocks).max(-1, keepdims=True)
    byte = np.maximum(np.where(amax > 0, np.frexp(amax)[1] - 1 + 127, 0) - down, 1)
    scale = np.exp2(byte - 127.0)
    codes = (blocks / scale).astype(np.float32).astype(dtype).astype(np.float64)
    return np.moveaxis((codes * scale).reshape(v.shape), -1, axis)


WIDE = False


def mx_kscale(k):
    if not WIDE:
        return np.ones(k)
    levels = np.array([18, -18])
    if k % 512:
        return np.exp2(np.random.permutation(np.resize(levels, k // 32))).repeat(32)
    a = np.empty((k // 512, 16))
    for p in range(k // 512):
        a[p, :8] = np.random.permutation(np.resize(levels, 8))
        for g in range(8):
            far = levels[np.abs(levels - a[p, g]) >= 10]
            a[p, g + 8] = far[np.random.randint(len(far))]
    return np.exp2(a.ravel()).repeat(32)


def f64(x):
    return np.asarray(x).astype(np.float64)


def striped(idx):
    return np.tile(np.asarray(idx).reshape(-1, 16).T, (8, 1)).astype(np.uint16)


def unstriped(offs):
    return offs[:16].T.reshape(-1).astype(np.int64)


def setup_inputs():
    n = np.random.standard_normal
    uni = np.random.uniform
    idx = np.random.permutation(2048)[:512]
    f_d = mx_kscale(512)
    f_i = np.ones(2048)
    f_i[idx] = mx_kscale(512)
    return {
        "xT": (0.35 * n((512, 512)) * f_d[:, None]).astype(np.float32),
        "dT": (n((512, 2048)) / np.sqrt(512) / f_d[:, None] * f_i[None, :]).astype(np.float32),
        "us": (uni(0.75, 1.3, (512, 1))).astype(np.float32),
        "ts": np.tile(uni(0.75, 1.3, 2048) / f_i, (128, 1)).astype(np.float32),
        "lk": (uni(0.5, 1.5, (512, 512))).astype(np.float32),
        "wt": (uni(0.75, 1.3, (512, 1))).astype(np.float32),
        "offs": striped(idx),
    }


def reference(xT, dT, us, ts, lk, wt, offs):
    idx = unstriped(offs)
    dT_i = f64(dT)[:, idx]
    ts_i = f64(ts)[:1][:, idx]
    a = mxq(f64(xT), 0, "e4m3").T @ mxq(dT_i, 0, "e4m3")
    z = f64(us) * ts_i * a
    m = (z).max(-1, keepdims=True)
    e = np.exp(z - m)
    t1 = (e).sum(-1, keepdims=True)
    f = e * f64(lk)
    t2 = (f).sum(-1, keepdims=True)
    g = f64(wt) * f64(us) * ts_i * (e / t1 - f / t2)
    out = mxq(g, 1, "e5m2") @ mxq(dT_i, 1, "e4m3").T
    return out

@@ -1,0 +1,201 @@
+from contextlib import ExitStack
+
+import concourse.mybir as mybir
+from concourse.masks import make_identity
+
+F32 = mybir.dt.float32
+BF16 = mybir.dt.bfloat16
+U32 = mybir.dt.uint32
+U16 = mybir.dt.uint16
+U8 = mybir.dt.uint8
+E4M3X4 = mybir.dt.float8_e4m3fn_x4
+E5M2X4 = mybir.dt.float8_e5m2_x4
+ALU = mybir.AluOpType
+ACT = mybir.ActivationFunctionType
+AX = mybir.AxisListType
+
+P = 128
+PACK = 4
+D = 512
+R = 512
+SLOTS = 512
+DOCS = 2048
+ROW_TILES = R // P
+KIB = 1024
+FORMS = ["A","A","A","A"]
+
+FLOPS = 2 * 2 * R * SLOTS * D
+BYTES = 4 * (D * R + D * DOCS + R * SLOTS + R * D + DOCS + 2 * R) + 2 * SLOTS * 8
+
+
+def tile_attend_grag_q_kernel(tc, xT, dT, us, ts, lk, wt, offs, out):
+    nc = tc.nc
+    with ExitStack() as ctx:
+        keep = ctx.enter_context(tc.tile_pool(name="keep", bufs=1))
+        reused = ctx.enter_context(tc.tile_pool(name="reused", bufs=1))
+        prep_ps = ctx.enter_context(tc.psum_pool(name="prep_ps", bufs=2))
+        score_ps = ctx.enter_context(tc.psum_pool(name="score_ps", bufs=2))
+        turn_ps = ctx.enter_context(tc.psum_pool(name="turn_ps", bufs=2))
+        out_ps = ctx.enter_context(tc.psum_pool(name="out_ps", bufs=2))
+
+        def placed(shape, dtype, name, kib):
+            return reused.tile(shape, dtype, name=name, align_bytes=64, offset=int(kib * KIB))
+
+        offsets = keep.tile([P, SLOTS // 16], U16, name="offsets")
+        d_planes = dT.rearrange("(p t) n -> t p n", t=PACK)
+        d_win = [keep.tile([P, DOCS], F32, name="d_win%d" % t) for t in range(PACK - 1)]
+        d_win.append(placed([P, DOCS], F32, "d_win3", 8))
+        ts_seed = keep.tile([P, DOCS // P], F32, name="ts_seed")
+        us_col = keep.tile([P, ROW_TILES], F32, name="us_col")
+        wt_col = keep.tile([P, ROW_TILES], F32, name="wt_col")
+
+        nc.sync.dma_start(ts_seed[:], ts[0].rearrange("(p c) -> p c", p=P))
+        nc.sync.dma_start(d_win[0][:], d_planes[0])
+        nc.sync.dma_start(offsets[:], offs)
+        with nc.allow_non_contiguous_dma(reason="one value a partition"):
+            nc.scalar.dma_start(us_col[:], us.rearrange("(j p) o -> p (j o)", p=P))
+            nc.scalar.dma_start(wt_col[:], wt.rearrange("(j p) o -> p (j o)", p=P))
+        for t in range(1, PACK):
+            nc.sync.dma_start(d_win[t][:], d_planes[t])
+        x_rows = xT.rearrange("(p t) r -> p t r", t=PACK)
+        x_raw = []
+        for c0, c1 in ((0, P), (P, 2 * P), (2 * P, R)):
+            chunk = keep.tile([P, PACK, c1 - c0], F32, name="x_chunk%d" % c0)
+            nc.sync.dma_start(chunk[:], x_rows[:, :, c0:c1])
+            x_raw.extend(chunk[:, :, c:c + P] for c in range(0, c1 - c0, P))
+        lk_sb = [keep.tile([P, SLOTS], F32, name="lk_sb%d" % j) for j in range(ROW_TILES)]
+        for j in range(ROW_TILES):
+            nc.sync.dma_start(lk_sb[j][:], lk[j * P:(j + 1) * P, :])
+
+        ident = keep.tile([P, P], F32, name="ident")
+        make_identity(nc, ident[:])
+        ident_bf = keep.tile([P, P], BF16, name="ident_bf")
+        nc.gpsimd.tensor_copy(ident_bf[:], ident[:])
+
+        warm = keep.tile([P, 1], F32, name="warm")
+        nc.scalar.activation(warm[:], ident[:, 0:1], ACT.Exp)
+
+        ts_win = placed([P, DOCS], F32, "ts_win", 0)
+        ts_win_v = ts_win[:].rearrange("m (p b c) -> m b p c", b=4, c=4)
+        for b in range(4):
+            bank = prep_ps.tile([P, 4, P], F32, name="prep_bank")
+            for c in range(4):
+                col = 4 * b + c
+                nc.tensor.transpose(bank[:, c, :], ts_seed[:, col:col + 1].to_broadcast([P, P]), ident[:])
+            nc.scalar.activation(ts_win_v[:, b], bank[:].rearrange("m c p -> m p c"), ACT.Copy)
+
+        coef = keep.tile([P, ROW_TILES], F32, name="coef")
+        nc.gpsimd.tensor_tensor(coef[:], us_col[:], wt_col[:], ALU.mult)
+
+        d01 = placed([P, 2 * SLOTS], BF16, "d01", 16)
+        dt_codes = keep.tile([P, D], U32, name="dt_codes", align_bytes=64)
+        dt_scales = keep.tile([P, D], U8, name="dt_scales", align_bytes=64)
+
+        def quantize_turned(grouped, half):
+            cols = slice(half * 2 * P, (half + 1) * 2 * P)
+            nc.vector.quantize_mx(out=dt_codes[:, cols].bitcast(E4M3X4), scales=dt_scales[:, cols], in_=grouped[:])
+
+        def turn_plain(plane, dst):
+            words = plane.bitcast(F32)
+            bank = prep_ps.tile([P, 4, P], F32, name="prep_bank")
+            for u in range(2):
+                nc.tensor.transpose(bank[:, u, :], words[:, u:SLOTS // 2:2], ident[:])
+            nc.scalar.copy(dst.bitcast(F32).rearrange("p (c u) -> p c u", u=2),
+                           bank[:, 0:2, :].rearrange("p u c -> p c u"))
+
+        nc.vector.tensor_copy(d01[:, 0:SLOTS], d_win[0][:].indirect(offsets[:]))
+        nc.vector.tensor_copy(d01[:, SLOTS:2 * SLOTS], d_win[1][:].indirect(offsets[:]))
+        ts_row = keep.tile([P, SLOTS], F32, name="ts_row")
+        nc.vector.tensor_copy(ts_row[:], ts_win[:].indirect(offsets[:]))
+        ts_coef = {}
+        for j in range(ROW_TILES):
+            if FORMS[j] == "A":
+                scaled = keep.tile([P, SLOTS], F32, name="ts_coef%d" % j)
+                nc.gpsimd.tensor_scalar(scaled[:], ts_row[:], coef[:, j:j + 1], 0.0, ALU.mult, ALU.add)
+                ts_coef[j] = scaled
+
+        d_grouped = placed([P, SLOTS, PACK], BF16, "d_grouped", 0)
+        dt_grouped01 = placed([P, 2 * P * PACK], BF16, "dt_grouped01", 4)
+        d2 = placed([P, SLOTS], BF16, "d2", 6)
+        dt_grouped23 = keep.tile([P, 2 * P * PACK], BF16, name="dt_grouped23", align_bytes=64)
+        for t in range(2):
+            turn_plain(d01[:, t * SLOTS:(t + 1) * SLOTS], dt_grouped01[:, t * P * PACK:(t + 1) * P * PACK])
+        nc.scalar.copy(d_grouped[:, :, 0:2], d01[:].rearrange("p (t i) -> p i t", t=2))
+        nc.vector.tensor_copy(d2[:], d_win[2][:].indirect(offsets[:]))
+        turn_plain(d2[:], dt_grouped23[:, 0:P * PACK])
+        quantize_turned(dt_grouped01, 0)
+        nc.vector.tensor_copy(d_grouped[:, :, 2], d2[:])
+        nc.vector.tensor_copy(d_grouped[:, :, 3], d_win[3][:].indirect(offsets[:]))
+
+        x_grouped_at = [16, 17, 4, 5]
+        x_codes_at = [8, 8.5, 8, 8.5]
+        z_at = [18, 20, 22, 24]
+        x_grouped = []
+        for j in range(ROW_TILES):
+            grouped = placed([P, P, PACK], BF16, "x_grouped%d" % j, x_grouped_at[j])
+            nc.scalar.copy(grouped[:].rearrange("p (c i) t -> p c t i", i=4),
+                           x_raw[j].rearrange("p t (c i) -> p c t i", i=4))
+            x_grouped.append(grouped)
+
+        def quantize_x(j):
+            codes = placed([P, P], U32, "x_codes%d" % j, x_codes_at[j])
+            scales = keep.tile([P, P], U8, name="x_scales%d" % j, align_bytes=64)
+            nc.vector.quantize_mx(out=codes[:].bitcast(E4M3X4), scales=scales[:],
+                                  in_=x_grouped[j][:].rearrange("p r t -> p (r t)"))
+            return codes, scales
+
+        d_codes = keep.tile([P, SLOTS], U32, name="d_codes", align_bytes=64)
+        d_scales = keep.tile([P, SLOTS], U8, name="d_scales", align_bytes=64)
+        nc.vector.quantize_mx(out=d_codes[:].bitcast(E4M3X4), scales=d_scales[:],
+                              in_=d_grouped[:].rearrange("p i t -> p (i t)"))
+
+        def turn_last():
+            last = prep_ps.tile([P, PACK, P], BF16, name="prep_bank")
+            for t in range(PACK):
+                nc.tensor.transpose(last[:, t, :], d_grouped[:, t:SLOTS:PACK, PACK - 1], ident_bf[:])
+            nc.scalar.copy(dt_grouped23[:, P * PACK:2 * P * PACK].rearrange("p (c t) -> p c t", t=PACK), last[:].rearrange("p t c -> p c t"))
+            quantize_turned(dt_grouped23, 1)
+
+        for j in range(ROW_TILES):
+            x_codes, x_scales = quantize_x(j)
+            a = score_ps.tile([P, SLOTS], F32, name="a")
+            nc.tensor.matmul_mx(out=a[:], lhsT=x_codes[:].bitcast(E4M3X4), lhsT_scale=x_scales[:],
+                                rhs=d_codes[:].bitcast(E4M3X4), rhs_scale=d_scales[:], start=True, stop=True)
+            z = placed([P, SLOTS], F32, "z%d" % j, z_at[j])
+            nc.vector.scalar_tensor_tensor(z[:], a[:], us_col[:, j:j + 1], ts_row[:], ALU.mult, ALU.mult)
+            neg_max = keep.tile([P, 1], F32, name="neg_max%d" % j)
+            nc.vector.tensor_reduce(neg_max[:], z[:], AX.X, ALU.max, negate=True)
+            e = keep.tile([P, SLOTS], F32, name="e%d" % j)
+            t1 = keep.tile([P, 1], F32, name="t1_%d" % j)
+            nc.scalar.activation(e[:], z[:], ACT.Exp, bias=neg_max[:], accum_out=t1[:])
+            inv1 = keep.tile([P, 1], F32, name="inv1_%d" % j)
+            nc.vector.reciprocal(inv1[:], t1[:])
+            f = keep.tile([P, SLOTS], F32, name="f%d" % j)
+            t2 = keep.tile([P, 1], F32, name="t2_%d" % j)
+            g_grouped = keep.tile([P, P * PACK], BF16, name="g_grouped%d" % j, align_bytes=64)
+            if FORMS[j] == "A":
+                nc.vector.scalar_tensor_tensor(f[:], e[:], 1.0, lk_sb[j][:], ALU.mult, ALU.mult, accum_out=t2[:])
+                ratio = keep.tile([P, 1], F32, name="ratio%d" % j)
+                nc.vector.tensor_tensor(ratio[:], t2[:], inv1[:], ALU.mult)
+                inv2 = keep.tile([P, 1], F32, name="inv2_%d" % j)
+                nc.vector.reciprocal(inv2[:], t2[:])
+                w = keep.tile([P, SLOTS], F32, name="w%d" % j)
+                nc.vector.scalar_tensor_tensor(w[:], e[:], ratio[:], f[:], ALU.mult, ALU.subtract)
+                g = keep.tile([P, SLOTS], BF16, name="g%d" % j, align_bytes=64)
+                nc.vector.scalar_tensor_tensor(g[:], w[:], inv2[:], ts_coef[j][:], ALU.mult, ALU.mult)
+                turned = turn_ps.tile([P, PACK, P], F32, name="turned")
+                g_words = g[:].bitcast(F32)
+                for u in range(2):
+                    nc.tensor.transpose(turned[:, u, :], g_words[:, u:SLOTS // 2:2], ident[:])
+                nc.scalar.copy(g_grouped[:].bitcast(F32).rearrange("p (r u) -> p r u", u=2), turned[:, 0:2, :].rearrange("p u r -> p r u"))
+            if j == 0:
+                turn_last()
+            g_codes = keep.tile([P, P], U32, name="g_codes%d" % j, align_bytes=64)
+            g_scales = keep.tile([P, P], U8, name="g_scales%d" % j, align_bytes=64)
+            nc.vector.quantize_mx(out=g_codes[:].bitcast(E5M2X4), scales=g_scales[:], in_=g_grouped[:])
+            res = out_ps.tile([P, D], F32, name="res")
+            nc.tensor.matmul_mx(out=res[:], lhsT=g_codes[:].bitcast(E5M2X4), lhsT_scale=g_scales[:],
+                                rhs=dt_codes[:].bitcast(E4M3X4), rhs_scale=dt_scales[:], start=True, stop=True)
+            staged = keep.tile([P, P, PACK], F32, name="staged%d" % j)
+            nc.scalar.copy(staged[:], res[:].rearrange("r (t c) -> r c t", t=PACK))
+            nc.sync.dma_start(out[j * P:(j + 1) * P, :], staged[:].rearrange("r c t -> r (c t)"))

@@ -22,7 +22,7 @@ SLOTS = 512
 DOCS = 2048
 ROW_TILES = R // P
 KIB = 1024
-FORMS = ["A","A","A","A"]
+FORMS = ["F","F","F","A"]
 
 FLOPS = 2 * 2 * R * SLOTS * D
 BYTES = 4 * (D * R + D * DOCS + R * SLOTS + R * D + DOCS + 2 * R) + 2 * SLOTS * 8
@@ -46,15 +46,14 @@ def tile_attend_grag_q_kernel(tc, xT, dT, us, ts, lk, wt, offs, out):
         d_win = [keep.tile([P, DOCS], F32, name="d_win%d" % t) for t in range(PACK - 1)]
         d_win.append(placed([P, DOCS], F32, "d_win3", 8))
         ts_seed = keep.tile([P, DOCS // P], F32, name="ts_seed")
-        us_col = keep.tile([P, ROW_TILES], F32, name="us_col")
-        wt_col = keep.tile([P, ROW_TILES], F32, name="wt_col")
+        uw_rows = keep.tile([P, P], F32, name="uw_rows")
+        nc.gpsimd.memset(uw_rows[:], 0.0)
 
         nc.sync.dma_start(ts_seed[:], ts[0].rearrange("(p c) -> p c", p=P))
         nc.sync.dma_start(d_win[0][:], d_planes[0])
         nc.sync.dma_start(offsets[:], offs)
-        with nc.allow_non_contiguous_dma(reason="one value a partition"):
-            nc.scalar.dma_start(us_col[:], us.rearrange("(j p) o -> p (j o)", p=P))
-            nc.scalar.dma_start(wt_col[:], wt.rearrange("(j p) o -> p (j o)", p=P))
+        nc.sync.dma_start(uw_rows[0:ROW_TILES, :], us.rearrange("(j p) o -> j (p o)", p=P))
+        nc.sync.dma_start(uw_rows[ROW_TILES:2 * ROW_TILES, :], wt.rearrange("(j p) o -> j (p o)", p=P))
         for t in range(1, PACK):
             nc.sync.dma_start(d_win[t][:], d_planes[t])
         x_rows = xT.rearrange("(p t) r -> p t r", t=PACK)
@@ -84,8 +83,16 @@ def tile_attend_grag_q_kernel(tc, xT, dT, us, ts, lk, wt, offs, out):
                 nc.tensor.transpose(bank[:, c, :], ts_seed[:, col:col + 1].to_broadcast([P, P]), ident[:])
             nc.scalar.activation(ts_win_v[:, b], bank[:].rearrange("m c p -> m p c"), ACT.Copy)
 
+        bank = prep_ps.tile([P, 4, P], F32, name="prep_bank")
+        nc.tensor.transpose(bank[:, 0, :], uw_rows[:], ident[:])
+        uw = keep.tile([P, 2 * ROW_TILES], F32, name="uw")
+        nc.scalar.copy(uw[:], bank[:, 0, 0:2 * ROW_TILES])
+        us_col = uw[:, 0:ROW_TILES]
+        wt_col = uw[:, ROW_TILES:2 * ROW_TILES]
         coef = keep.tile([P, ROW_TILES], F32, name="coef")
-        nc.gpsimd.tensor_tensor(coef[:], us_col[:], wt_col[:], ALU.mult)
+        nc.gpsimd.tensor_tensor(coef[:], us_col, wt_col, ALU.mult)
+        neg_coef = keep.tile([P, ROW_TILES], F32, name="neg_coef")
+        nc.gpsimd.tensor_scalar(neg_coef[:], coef[:], -1.0, 0.0, ALU.mult, ALU.add)
 
         d01 = placed([P, 2 * SLOTS], BF16, "d01", 16)
         dt_codes = keep.tile([P, D], U32, name="dt_codes", align_bytes=64)
@@ -107,12 +114,6 @@ def tile_attend_grag_q_kernel(tc, xT, dT, us, ts, lk, wt, offs, out):
         nc.vector.tensor_copy(d01[:, SLOTS:2 * SLOTS], d_win[1][:].indirect(offsets[:]))
         ts_row = keep.tile([P, SLOTS], F32, name="ts_row")
         nc.vector.tensor_copy(ts_row[:], ts_win[:].indirect(offsets[:]))
-        ts_coef = {}
-        for j in range(ROW_TILES):
-            if FORMS[j] == "A":
-                scaled = keep.tile([P, SLOTS], F32, name="ts_coef%d" % j)
-                nc.gpsimd.tensor_scalar(scaled[:], ts_row[:], coef[:, j:j + 1], 0.0, ALU.mult, ALU.add)
-                ts_coef[j] = scaled
 
         d_grouped = placed([P, SLOTS, PACK], BF16, "d_grouped", 0)
         dt_grouped01 = placed([P, 2 * P * PACK], BF16, "dt_grouped01", 4)
@@ -123,6 +124,11 @@ def tile_attend_grag_q_kernel(tc, xT, dT, us, ts, lk, wt, offs, out):
         nc.scalar.copy(d_grouped[:, :, 0:2], d01[:].rearrange("p (t i) -> p i t", t=2))
         nc.vector.tensor_copy(d2[:], d_win[2][:].indirect(offsets[:]))
         turn_plain(d2[:], dt_grouped23[:, 0:P * PACK])
+        bank = prep_ps.tile([P, 4, P], F32, name="prep_bank")
+        for t in range(PACK):
+            nc.tensor.transpose(bank[:, t, :], ts_row[:, t:SLOTS:PACK], ident[:])
+        ts_turned = keep.tile([P, PACK], F32, name="ts_turned")
+        nc.scalar.copy(ts_turned[:], bank[:, :, 0])
         quantize_turned(dt_grouped01, 0)
         nc.vector.tensor_copy(d_grouped[:, :, 2], d2[:])
         nc.vector.tensor_copy(d_grouped[:, :, 3], d_win[3][:].indirect(offsets[:]))
@@ -177,17 +183,34 @@ def tile_attend_grag_q_kernel(tc, xT, dT, us, ts, lk, wt, offs, out):
                 nc.vector.scalar_tensor_tensor(f[:], e[:], 1.0, lk_sb[j][:], ALU.mult, ALU.mult, accum_out=t2[:])
                 ratio = keep.tile([P, 1], F32, name="ratio%d" % j)
                 nc.vector.tensor_tensor(ratio[:], t2[:], inv1[:], ALU.mult)
-                inv2 = keep.tile([P, 1], F32, name="inv2_%d" % j)
-                nc.vector.reciprocal(inv2[:], t2[:])
                 w = keep.tile([P, SLOTS], F32, name="w%d" % j)
                 nc.vector.scalar_tensor_tensor(w[:], e[:], ratio[:], f[:], ALU.mult, ALU.subtract)
+                inv2 = keep.tile([P, 1], F32, name="inv2_%d" % j)
+                nc.vector.reciprocal(inv2[:], t2[:])
+                beta = keep.tile([P, 1], F32, name="beta%d" % j)
+                nc.vector.tensor_tensor(beta[:], inv2[:], coef[:, j:j + 1], ALU.mult)
                 g = keep.tile([P, SLOTS], BF16, name="g%d" % j, align_bytes=64)
-                nc.vector.scalar_tensor_tensor(g[:], w[:], inv2[:], ts_coef[j][:], ALU.mult, ALU.mult)
+                nc.vector.scalar_tensor_tensor(g[:], w[:], beta[:], ts_row[:], ALU.mult, ALU.mult)
                 turned = turn_ps.tile([P, PACK, P], F32, name="turned")
                 g_words = g[:].bitcast(F32)
                 for u in range(2):
                     nc.tensor.transpose(turned[:, u, :], g_words[:, u:SLOTS // 2:2], ident[:])
                 nc.scalar.copy(g_grouped[:].bitcast(F32).rearrange("p (r u) -> p r u", u=2), turned[:, 0:2, :].rearrange("p u r -> p r u"))
+            else:
+                nc.vector.scalar_tensor_tensor(f[:], e[:], 1.0, lk_sb[j][:], ALU.mult, ALU.mult, accum_out=t2[:])
+                inv2 = keep.tile([P, 1], F32, name="inv2_%d" % j)
+                nc.vector.reciprocal(inv2[:], t2[:])
+                turned = turn_ps.tile([P, PACK, P], F32, name="turned")
+                for k, (src, inv, cf) in enumerate(((e, inv1, coef), (f, inv2, neg_coef))):
+                    term = keep.tile([P, PACK, P], F32, name="term%d_%d" % (j, k))
+                    factor = keep.tile([P, 1], F32, name="factor%d_%d" % (j, k))
+                    nc.scalar.activation(factor[:], inv[:], ACT.Copy, scale=cf[:, j:j + 1])
+                    nc.scalar.activation(term[:].rearrange("p t s -> p s t"), src[:].rearrange("p (s t) -> p s t", t=PACK),
+                                         ACT.Copy, scale=factor[:])
+                    for t in range(PACK):
+                        nc.tensor.matmul(turned[:, t, :], lhsT=term[:, t, :], rhs=ident[:], is_transpose=True,
+                                         start=(k == 0 and t == 0), stop=(k == 1 and t == PACK - 1))
+                nc.vector.tensor_tensor(g_grouped[:].rearrange("p (r t) -> p r t", t=PACK), turned[:].rearrange("p t r -> p r t"), ts_turned[:].unsqueeze(1).to_broadcast([P, P, PACK]), ALU.mult)
             if j == 0:
                 turn_last()
             g_codes = keep.tile([P, P], U32, name="g_codes%d" % j, align_bytes=64)
@@ -197,5 +220,13 @@ def tile_attend_grag_q_kernel(tc, xT, dT, us, ts, lk, wt, offs, out):
             nc.tensor.matmul_mx(out=res[:], lhsT=g_codes[:].bitcast(E5M2X4), lhsT_scale=g_scales[:],
                                 rhs=dt_codes[:].bitcast(E4M3X4), rhs_scale=dt_scales[:], start=True, stop=True)
             staged = keep.tile([P, P, PACK], F32, name="staged%d" % j)
-            nc.scalar.copy(staged[:], res[:].rearrange("r (t c) -> r c t", t=PACK))
-            nc.sync.dma_start(out[j * P:(j + 1) * P, :], staged[:].rearrange("r c t -> r (c t)"))
+            res_natural = res[:].rearrange("r (t c) -> r c t", t=PACK)
+            rows = slice(j * P, (j + 1) * P)
+            if j < ROW_TILES - 1:
+                nc.scalar.copy(staged[:], res_natural)
+                nc.sync.dma_start(out[rows, :], staged[:].rearrange("r c t -> r (c t)"))
+            else:
+                for half in range(2):
+                    cs = slice(half * P // 2, (half + 1) * P // 2)
+                    nc.vector.tensor_copy(staged[:, cs, :], res_natural[:, cs, :])
+                    nc.sync.dma_start(out[rows, half * D // 2:(half + 1) * D // 2], staged[:, cs, :].rearrange("r c t -> r (c t)"))

@@ -21,8 +21,8 @@ R = 512
 SLOTS = 512
 DOCS = 2048
 ROW_TILES = R // P
+SLOT_TILES = SLOTS // P
 KIB = 1024
-FORMS = ["F","F","F","A"]
 
 FLOPS = 2 * 2 * R * SLOTS * D
 BYTES = 4 * (D * R + D * DOCS + R * SLOTS + R * D + DOCS + 2 * R) + 2 * SLOTS * 8
@@ -57,19 +57,18 @@ def tile_attend_grag_q_kernel(tc, xT, dT, us, ts, lk, wt, offs, out):
         for t in range(1, PACK):
             nc.sync.dma_start(d_win[t][:], d_planes[t])
         x_rows = xT.rearrange("(p t) r -> p t r", t=PACK)
+        x_spans = ((0, P), (P, 2 * P), (2 * P, R))
         x_raw = []
-        for c0, c1 in ((0, P), (P, 2 * P), (2 * P, R)):
+        for c0, c1 in x_spans:
             chunk = keep.tile([P, PACK, c1 - c0], F32, name="x_chunk%d" % c0)
             nc.sync.dma_start(chunk[:], x_rows[:, :, c0:c1])
-            x_raw.extend(chunk[:, :, c:c + P] for c in range(0, c1 - c0, P))
+            x_raw.append(chunk)
         lk_sb = [keep.tile([P, SLOTS], F32, name="lk_sb%d" % j) for j in range(ROW_TILES)]
         for j in range(ROW_TILES):
             nc.sync.dma_start(lk_sb[j][:], lk[j * P:(j + 1) * P, :])
 
         ident = keep.tile([P, P], F32, name="ident")
         make_identity(nc, ident[:])
-        ident_bf = keep.tile([P, P], BF16, name="ident_bf")
-        nc.gpsimd.tensor_copy(ident_bf[:], ident[:])
 
         warm = keep.tile([P, 1], F32, name="warm")
         nc.scalar.activation(warm[:], ident[:, 0:1], ACT.Exp)
@@ -83,18 +82,6 @@ def tile_attend_grag_q_kernel(tc, xT, dT, us, ts, lk, wt, offs, out):
                 nc.tensor.transpose(bank[:, c, :], ts_seed[:, col:col + 1].to_broadcast([P, P]), ident[:])
             nc.scalar.activation(ts_win_v[:, b], bank[:].rearrange("m c p -> m p c"), ACT.Copy)
 
-        bank = prep_ps.tile([P, 4, P], F32, name="prep_bank")
-        nc.tensor.transpose(bank[:, 0, :], uw_rows[:], ident[:])
-        uw = keep.tile([P, 2 * ROW_TILES], F32, name="uw")
-        nc.scalar.copy(uw[:], bank[:, 0, 0:2 * ROW_TILES])
-        us_col = uw[:, 0:ROW_TILES]
-        wt_col = uw[:, ROW_TILES:2 * ROW_TILES]
-        coef = keep.tile([P, ROW_TILES], F32, name="coef")
-        nc.gpsimd.tensor_tensor(coef[:], us_col, wt_col, ALU.mult)
-        neg_coef = keep.tile([P, ROW_TILES], F32, name="neg_coef")
-        nc.gpsimd.tensor_scalar(neg_coef[:], coef[:], -1.0, 0.0, ALU.mult, ALU.add)
-
-        d01 = placed([P, 2 * SLOTS], BF16, "d01", 16)
         dt_codes = keep.tile([P, D], U32, name="dt_codes", align_bytes=64)
         dt_scales = keep.tile([P, D], U8, name="dt_scales", align_bytes=64)
 
@@ -110,44 +97,53 @@ def tile_attend_grag_q_kernel(tc, xT, dT, us, ts, lk, wt, offs, out):
             nc.scalar.copy(dst.bitcast(F32).rearrange("p (c u) -> p c u", u=2),
                            bank[:, 0:2, :].rearrange("p u c -> p c u"))
 
-        nc.vector.tensor_copy(d01[:, 0:SLOTS], d_win[0][:].indirect(offsets[:]))
-        nc.vector.tensor_copy(d01[:, SLOTS:2 * SLOTS], d_win[1][:].indirect(offsets[:]))
+        d0 = keep.tile([P, SLOTS], BF16, name="d0", align_bytes=64)
+        nc.vector.tensor_copy(d0[:], d_win[0][:].indirect(offsets[:]))
         ts_row = keep.tile([P, SLOTS], F32, name="ts_row")
         nc.vector.tensor_copy(ts_row[:], ts_win[:].indirect(offsets[:]))
-
         d_grouped = placed([P, SLOTS, PACK], BF16, "d_grouped", 0)
-        dt_grouped01 = placed([P, 2 * P * PACK], BF16, "dt_grouped01", 4)
-        d2 = placed([P, SLOTS], BF16, "d2", 6)
-        dt_grouped23 = keep.tile([P, 2 * P * PACK], BF16, name="dt_grouped23", align_bytes=64)
-        for t in range(2):
-            turn_plain(d01[:, t * SLOTS:(t + 1) * SLOTS], dt_grouped01[:, t * P * PACK:(t + 1) * P * PACK])
-        nc.scalar.copy(d_grouped[:, :, 0:2], d01[:].rearrange("p (t i) -> p i t", t=2))
-        nc.vector.tensor_copy(d2[:], d_win[2][:].indirect(offsets[:]))
-        turn_plain(d2[:], dt_grouped23[:, 0:P * PACK])
-        bank = prep_ps.tile([P, 4, P], F32, name="prep_bank")
-        for t in range(PACK):
-            nc.tensor.transpose(bank[:, t, :], ts_row[:, t:SLOTS:PACK], ident[:])
-        ts_turned = keep.tile([P, PACK], F32, name="ts_turned")
-        nc.scalar.copy(ts_turned[:], bank[:, :, 0])
+        d1 = placed([P, SLOTS], BF16, "d1", 5)
+        dt_grouped01 = placed([P, 2 * P * PACK], BF16, "dt_grouped01", 16)
+        nc.vector.tensor_copy(d1[:], d_win[1][:].indirect(offsets[:]))
+        for t, plane in enumerate((d0, d1)):
+            turn_plain(plane[:], dt_grouped01[:, t * P * PACK:(t + 1) * P * PACK])
+            nc.scalar.copy(d_grouped[:, :, t], plane[:])
         quantize_turned(dt_grouped01, 0)
-        nc.vector.tensor_copy(d_grouped[:, :, 2], d2[:])
-        nc.vector.tensor_copy(d_grouped[:, :, 3], d_win[3][:].indirect(offsets[:]))
+        for t in (2, 3):
+            nc.vector.tensor_copy(d_grouped[:, :, t], d_win[t][:].indirect(offsets[:]))
 
-        x_grouped_at = [16, 17, 4, 5]
-        x_codes_at = [8, 8.5, 8, 8.5]
-        z_at = [18, 20, 22, 24]
-        x_grouped = []
+        bank = prep_ps.tile([P, 4, P], F32, name="prep_bank")
+        nc.tensor.transpose(bank[:, 0, :], uw_rows[:], ident[:])
+        uw = keep.tile([P, 2 * ROW_TILES], F32, name="uw")
+        nc.scalar.copy(uw[:], bank[:, 0, 0:2 * ROW_TILES])
+        neg_us = keep.tile([P, ROW_TILES], F32, name="neg_us")
+        nc.scalar.activation(neg_us[:], uw[:, 0:ROW_TILES], ACT.Copy, scale=-1.0)
+        stats = []
         for j in range(ROW_TILES):
-            grouped = placed([P, P, PACK], BF16, "x_grouped%d" % j, x_grouped_at[j])
+            st = keep.tile([P, 3], F32, name="stats%d" % j)
+            nc.scalar.activation(st[:, 2:3], uw[:, ROW_TILES + j:ROW_TILES + j + 1], ACT.Copy, scale=uw[:, j:j + 1])
+            stats.append(st)
+        bank = prep_ps.tile([P, 4, P], F32, name="prep_bank")
+        for s in range(SLOT_TILES):
+            nc.tensor.transpose(bank[:, s, :], ts_row[:, s * P:(s + 1) * P], ident[:])
+        ts_col = keep.tile([P, SLOT_TILES], F32, name="ts_col")
+        nc.scalar.copy(ts_col[:], bank[:, :, 0])
+
+        x_grouped_at = [4.5, 5.5, 16]
+        x_codes_at = [9, 8, 9]
+        x_grouped = []
+        for n, (c0, c1) in enumerate(x_spans):
+            grouped = placed([P, c1 - c0, PACK], BF16, "x_grouped%d" % n, x_grouped_at[n])
             nc.scalar.copy(grouped[:].rearrange("p (c i) t -> p c t i", i=4),
-                           x_raw[j].rearrange("p t (c i) -> p c t i", i=4))
+                           x_raw[n][:].rearrange("p t (c i) -> p c t i", i=4))
             x_grouped.append(grouped)
 
-        def quantize_x(j):
-            codes = placed([P, P], U32, "x_codes%d" % j, x_codes_at[j])
-            scales = keep.tile([P, P], U8, name="x_scales%d" % j, align_bytes=64)
+        def quantize_x(n):
+            width = x_spans[n][1] - x_spans[n][0]
+            codes = placed([P, width], U32, "x_codes%d" % n, x_codes_at[n])
+            scales = keep.tile([P, width], U8, name="x_scales%d" % n, align_bytes=64)
             nc.vector.quantize_mx(out=codes[:].bitcast(E4M3X4), scales=scales[:],
-                                  in_=x_grouped[j][:].rearrange("p r t -> p (r t)"))
+                                  in_=x_grouped[n][:].rearrange("p r t -> p (r t)"))
             return codes, scales
 
         d_codes = keep.tile([P, SLOTS], U32, name="d_codes", align_bytes=64)
@@ -155,67 +151,77 @@ def tile_attend_grag_q_kernel(tc, xT, dT, us, ts, lk, wt, offs, out):
         nc.vector.quantize_mx(out=d_codes[:].bitcast(E4M3X4), scales=d_scales[:],
                               in_=d_grouped[:].rearrange("p i t -> p (i t)"))
 
-        def turn_last():
-            last = prep_ps.tile([P, PACK, P], BF16, name="prep_bank")
-            for t in range(PACK):
-                nc.tensor.transpose(last[:, t, :], d_grouped[:, t:SLOTS:PACK, PACK - 1], ident_bf[:])
-            nc.scalar.copy(dt_grouped23[:, P * PACK:2 * P * PACK].rearrange("p (c t) -> p c t", t=PACK), last[:].rearrange("p t c -> p c t"))
-            quantize_turned(dt_grouped23, 1)
+        e = [keep.tile([P, SLOTS], F32, name="e%d" % j) for j in range(ROW_TILES)]
+        g_grouped = [keep.tile([P, P * PACK], BF16, name="g_grouped%d" % j, align_bytes=64) for j in range(ROW_TILES)]
 
-        for j in range(ROW_TILES):
+        def scores_by_rows(j):
             x_codes, x_scales = quantize_x(j)
-            a = score_ps.tile([P, SLOTS], F32, name="a")
+            a = score_ps.tile([P, SLOTS], F32, name="score_bank")
             nc.tensor.matmul_mx(out=a[:], lhsT=x_codes[:].bitcast(E4M3X4), lhsT_scale=x_scales[:],
                                 rhs=d_codes[:].bitcast(E4M3X4), rhs_scale=d_scales[:], start=True, stop=True)
-            z = placed([P, SLOTS], F32, "z%d" % j, z_at[j])
-            nc.vector.scalar_tensor_tensor(z[:], a[:], us_col[:, j:j + 1], ts_row[:], ALU.mult, ALU.mult)
+            z = keep.tile([P, SLOTS], F32, name="z%d" % j)
+            nc.vector.scalar_tensor_tensor(z[:], a[:], uw[:, j:j + 1], ts_row[:], ALU.mult, ALU.mult)
             neg_max = keep.tile([P, 1], F32, name="neg_max%d" % j)
             nc.vector.tensor_reduce(neg_max[:], z[:], AX.X, ALU.max, negate=True)
-            e = keep.tile([P, SLOTS], F32, name="e%d" % j)
-            t1 = keep.tile([P, 1], F32, name="t1_%d" % j)
-            nc.scalar.activation(e[:], z[:], ACT.Exp, bias=neg_max[:], accum_out=t1[:])
-            inv1 = keep.tile([P, 1], F32, name="inv1_%d" % j)
-            nc.vector.reciprocal(inv1[:], t1[:])
+            nc.scalar.activation(e[j][:], z[:], ACT.Exp, bias=neg_max[:], accum_out=stats[j][:, 0:1])
+
+        def scores_by_slots():
+            x_codes, x_scales = quantize_x(2)
+            scaled = keep.tile([P, SLOT_TILES, 2 * P], F32, name="scaled")
+            for pair in range(SLOT_TILES // 2):
+                a = prep_ps.tile([P, 2, 2 * P], F32, name="prep_bank")
+                for k in range(2):
+                    cols = slice((2 * pair + k) * P, (2 * pair + k + 1) * P)
+                    nc.tensor.matmul_mx(out=a[:, k, :], lhsT=d_codes[:, cols].bitcast(E4M3X4), lhsT_scale=d_scales[:, cols],
+                                        rhs=x_codes[:].bitcast(E4M3X4), rhs_scale=x_scales[:], start=True, stop=True)
+                for k in range(2):
+                    s = 2 * pair + k
+                    nc.scalar.activation(scaled[:, s, :], a[:, k, :], ACT.Copy, scale=ts_col[:, s:s + 1])
+            return scaled
+
+        def turn_scores(scaled, j):
+            y = score_ps.tile([P, SLOTS], F32, name="score_bank")
+            for s in range(SLOT_TILES):
+                nc.tensor.transpose(y[:, s * P:(s + 1) * P], scaled[:, s, (j - 2) * P:(j - 1) * P], ident[:])
+            neg_z = keep.tile([P, SLOTS], F32, name="z%d" % j)
+            neg_max = keep.tile([P, 1], F32, name="neg_max%d" % j)
+            nc.vector.tensor_scalar(neg_z[:], y[:], neg_us[:, j:j + 1], None, ALU.mult, ALU.min, accum_out=neg_max[:])
+            nc.scalar.activation(e[j][:], neg_z[:], ACT.Exp, bias=neg_max[:], scale=-1.0, accum_out=stats[j][:, 0:1])
+
+        def turn_last_planes():
+            dealt = keep.tile([P, PACK, P], F32, name="dealt23")
+            words = d_grouped[:].rearrange("p i t -> p (i t)").bitcast(F32).rearrange("p (s t v) -> p s t v", t=PACK, v=2)
+            nc.scalar.copy(dealt[:].rearrange("p t s -> p s t"), words[:, :, :, 1])
+            bank = turn_ps.tile([P, PACK, P], F32, name="turn_bank")
+            for t in range(PACK):
+                nc.tensor.transpose(bank[:, t, :], dealt[:, t, :], ident[:])
+            grouped = keep.tile([P, 2 * P * PACK], BF16, name="dt_grouped23", align_bytes=64)
+            nc.scalar.copy(grouped[:].rearrange("p (v c t) -> p v c t", v=2, t=PACK),
+                           bank[:].rearrange("p t c -> p (t c)").bitcast(BF16).rearrange("p (t c v) -> p v c t", t=PACK, v=2))
+            quantize_turned(grouped, 1)
+
+        def gradient(j):
+            st = stats[j]
             f = keep.tile([P, SLOTS], F32, name="f%d" % j)
-            t2 = keep.tile([P, 1], F32, name="t2_%d" % j)
-            g_grouped = keep.tile([P, P * PACK], BF16, name="g_grouped%d" % j, align_bytes=64)
-            if FORMS[j] == "A":
-                nc.vector.scalar_tensor_tensor(f[:], e[:], 1.0, lk_sb[j][:], ALU.mult, ALU.mult, accum_out=t2[:])
-                ratio = keep.tile([P, 1], F32, name="ratio%d" % j)
-                nc.vector.tensor_tensor(ratio[:], t2[:], inv1[:], ALU.mult)
-                w = keep.tile([P, SLOTS], F32, name="w%d" % j)
-                nc.vector.scalar_tensor_tensor(w[:], e[:], ratio[:], f[:], ALU.mult, ALU.subtract)
-                inv2 = keep.tile([P, 1], F32, name="inv2_%d" % j)
-                nc.vector.reciprocal(inv2[:], t2[:])
-                beta = keep.tile([P, 1], F32, name="beta%d" % j)
-                nc.vector.tensor_tensor(beta[:], inv2[:], coef[:, j:j + 1], ALU.mult)
-                g = keep.tile([P, SLOTS], BF16, name="g%d" % j, align_bytes=64)
-                nc.vector.scalar_tensor_tensor(g[:], w[:], beta[:], ts_row[:], ALU.mult, ALU.mult)
-                turned = turn_ps.tile([P, PACK, P], F32, name="turned")
-                g_words = g[:].bitcast(F32)
-                for u in range(2):
-                    nc.tensor.transpose(turned[:, u, :], g_words[:, u:SLOTS // 2:2], ident[:])
-                nc.scalar.copy(g_grouped[:].bitcast(F32).rearrange("p (r u) -> p r u", u=2), turned[:, 0:2, :].rearrange("p u r -> p r u"))
-            else:
-                nc.vector.scalar_tensor_tensor(f[:], e[:], 1.0, lk_sb[j][:], ALU.mult, ALU.mult, accum_out=t2[:])
-                inv2 = keep.tile([P, 1], F32, name="inv2_%d" % j)
-                nc.vector.reciprocal(inv2[:], t2[:])
-                turned = turn_ps.tile([P, PACK, P], F32, name="turned")
-                for k, (src, inv, cf) in enumerate(((e, inv1, coef), (f, inv2, neg_coef))):
-                    term = keep.tile([P, PACK, P], F32, name="term%d_%d" % (j, k))
-                    factor = keep.tile([P, 1], F32, name="factor%d_%d" % (j, k))
-                    nc.scalar.activation(factor[:], inv[:], ACT.Copy, scale=cf[:, j:j + 1])
-                    nc.scalar.activation(term[:].rearrange("p t s -> p s t"), src[:].rearrange("p (s t) -> p s t", t=PACK),
-                                         ACT.Copy, scale=factor[:])
-                    for t in range(PACK):
-                        nc.tensor.matmul(turned[:, t, :], lhsT=term[:, t, :], rhs=ident[:], is_transpose=True,
-                                         start=(k == 0 and t == 0), stop=(k == 1 and t == PACK - 1))
-                nc.vector.tensor_tensor(g_grouped[:].rearrange("p (r t) -> p r t", t=PACK), turned[:].rearrange("p t r -> p r t"), ts_turned[:].unsqueeze(1).to_broadcast([P, P, PACK]), ALU.mult)
-            if j == 0:
-                turn_last()
+            nc.vector.scalar_tensor_tensor(f[:], e[j][:], 1.0, lk_sb[j][:], ALU.mult, ALU.mult, accum_out=st[:, 1:2])
+            inv = keep.tile([P, 2], F32, name="inv%d" % j)
+            nc.vector.reciprocal(inv[:], st[:, 0:2])
+            factor = keep.tile([P, 2], F32, name="factor%d" % j)
+            nc.vector.tensor_tensor(factor[:], inv[:], st[:, 1:3], ALU.mult)
+            w = keep.tile([P, SLOTS], F32, name="w%d" % j)
+            nc.vector.scalar_tensor_tensor(w[:], e[j][:], factor[:, 0:1], f[:], ALU.mult, ALU.subtract)
+            g = keep.tile([P, SLOTS], BF16, name="g%d" % j, align_bytes=64)
+            nc.vector.scalar_tensor_tensor(g[:], w[:], factor[:, 1:2], ts_row[:], ALU.mult, ALU.mult)
+            turned = turn_ps.tile([P, PACK, P], F32, name="turn_bank")
+            g_words = g[:].bitcast(F32)
+            for u in range(2):
+                nc.tensor.transpose(turned[:, u, :], g_words[:, u:SLOTS // 2:2], ident[:])
+            nc.scalar.copy(g_grouped[j][:].bitcast(F32).rearrange("p (r u) -> p r u", u=2), turned[:, 0:2, :].rearrange("p u r -> p r u"))
+
+        def product(j):
             g_codes = keep.tile([P, P], U32, name="g_codes%d" % j, align_bytes=64)
             g_scales = keep.tile([P, P], U8, name="g_scales%d" % j, align_bytes=64)
-            nc.vector.quantize_mx(out=g_codes[:].bitcast(E5M2X4), scales=g_scales[:], in_=g_grouped[:])
+            nc.vector.quantize_mx(out=g_codes[:].bitcast(E5M2X4), scales=g_scales[:], in_=g_grouped[j][:])
             res = out_ps.tile([P, D], F32, name="res")
             nc.tensor.matmul_mx(out=res[:], lhsT=g_codes[:].bitcast(E5M2X4), lhsT_scale=g_scales[:],
                                 rhs=dt_codes[:].bitcast(E4M3X4), rhs_scale=dt_scales[:], start=True, stop=True)
@@ -230,3 +236,18 @@ def tile_attend_grag_q_kernel(tc, xT, dT, us, ts, lk, wt, offs, out):
                     cs = slice(half * P // 2, (half + 1) * P // 2)
                     nc.vector.tensor_copy(staged[:, cs, :], res_natural[:, cs, :])
                     nc.sync.dma_start(out[rows, half * D // 2:(half + 1) * D // 2], staged[:, cs, :].rearrange("r c t -> r (c t)"))
+
+        scores_by_rows(0)
+        scores_by_rows(1)
+        turn_last_planes()
+        scaled = scores_by_slots()
+        gradient(0)
+        turn_scores(scaled, 2)
+        gradient(1)
+        turn_scores(scaled, 3)
+        product(0)
+        gradient(2)
+        product(1)
+        gradient(3)
+        product(2)
+        product(3)

@@ -22,10 +22,28 @@ SLOTS = 512
 DOCS = 2048
 ROW_TILES = R // P
 SLOT_TILES = SLOTS // P
-KIB = 1024
+HALF = SLOTS // 2
+OFFSETS_PER_COLUMN = 16
+BANK_BLOCKS = 4
+
+X_SPANS = ((0, P), (P, 2 * P), (2 * P, R))
+PRODUCT_GROUPS = ((0, 1), (2,), (3,))
+
+TS_WINDOW_AT = 0
+D_GROUPED_AT = 0
+D_PLANE1_AT = 5
+D_WINDOW3_AT = 8
+DT_GROUPED01_AT = 16
+X_GROUPED_AT = (4.5, 5.5, 16)
+X_CODES_AT = (9, 8, 21)
+DT_GROUPED23_AT = 18.5
+Z_AT = (20, 22, 32, 34)
+F_AT = (32, 34, 36, 38)
+LK_AT = (40, 42, 44, 46)
+G_CODES_AT = (44, 40, 42)
 
 FLOPS = 2 * 2 * R * SLOTS * D
-BYTES = 4 * (D * R + D * DOCS + R * SLOTS + R * D + DOCS + 2 * R) + 2 * SLOTS * 8
+BYTES = 4 * (D * R + D * DOCS + R * SLOTS + R * D + DOCS + 2 * R) + 2 * P * SLOTS // OFFSETS_PER_COLUMN
 
 
 def tile_attend_grag_q_kernel(tc, xT, dT, us, ts, lk, wt, offs, out):
@@ -39,108 +57,107 @@ def tile_attend_grag_q_kernel(tc, xT, dT, us, ts, lk, wt, offs, out):
         out_ps = ctx.enter_context(tc.psum_pool(name="out_ps", bufs=2))
 
         def placed(shape, dtype, name, kib):
-            return reused.tile(shape, dtype, name=name, align_bytes=64, offset=int(kib * KIB))
+            return reused.tile(shape, dtype, name=name, align_bytes=64, offset=int(kib * 1024))
 
-        offsets = keep.tile([P, SLOTS // 16], U16, name="offsets")
+        offsets = keep.tile([P, SLOTS // OFFSETS_PER_COLUMN], U16, name="offsets")
         d_planes = dT.rearrange("(p t) n -> t p n", t=PACK)
-        d_win = [keep.tile([P, DOCS], F32, name="d_win%d" % t) for t in range(PACK - 1)]
-        d_win.append(placed([P, DOCS], F32, "d_win3", 8))
+        d_window = [keep.tile([P, DOCS], F32, name="d_window%d" % t) for t in range(PACK - 1)]
+        d_window.append(placed([P, DOCS], F32, "d_window3", D_WINDOW3_AT))
         ts_seed = keep.tile([P, DOCS // P], F32, name="ts_seed")
         uw_rows = keep.tile([P, P], F32, name="uw_rows")
         nc.gpsimd.memset(uw_rows[:], 0.0)
 
         nc.sync.dma_start(ts_seed[:], ts[0].rearrange("(p c) -> p c", p=P))
-        nc.sync.dma_start(d_win[0][:], d_planes[0])
+        nc.sync.dma_start(d_window[0][:], d_planes[0])
         nc.sync.dma_start(offsets[:], offs)
         nc.sync.dma_start(uw_rows[0:ROW_TILES, :], us.rearrange("(j p) o -> j (p o)", p=P))
         nc.sync.dma_start(uw_rows[ROW_TILES:2 * ROW_TILES, :], wt.rearrange("(j p) o -> j (p o)", p=P))
         for t in range(1, PACK):
-            nc.sync.dma_start(d_win[t][:], d_planes[t])
-        x_rows = xT.rearrange("(p t) r -> p t r", t=PACK)
-        x_spans = ((0, P), (P, 2 * P), (2 * P, R))
+            nc.sync.dma_start(d_window[t][:], d_planes[t])
+        x_planes = xT.rearrange("(p t) r -> p t r", t=PACK)
         x_raw = []
-        for c0, c1 in x_spans:
-            chunk = keep.tile([P, PACK, c1 - c0], F32, name="x_chunk%d" % c0)
-            nc.sync.dma_start(chunk[:], x_rows[:, :, c0:c1])
-            x_raw.append(chunk)
-        lk_sb = [keep.tile([P, SLOTS], F32, name="lk_sb%d" % j) for j in range(ROW_TILES)]
+        for first, end in X_SPANS:
+            span = keep.tile([P, PACK, end - first], F32, name="x_raw%d" % first)
+            nc.sync.dma_start(span[:], x_planes[:, :, first:end])
+            x_raw.append(span)
+        lk_rows = [placed([P, SLOTS], F32, "lk_rows%d" % j, LK_AT[j]) for j in range(ROW_TILES)]
         for j in range(ROW_TILES):
-            nc.sync.dma_start(lk_sb[j][:], lk[j * P:(j + 1) * P, :])
+            nc.sync.dma_start(lk_rows[j][:], lk[j * P:(j + 1) * P, :])
 
         ident = keep.tile([P, P], F32, name="ident")
         make_identity(nc, ident[:])
 
-        warm = keep.tile([P, 1], F32, name="warm")
-        nc.scalar.activation(warm[:], ident[:, 0:1], ACT.Exp)
+        one = keep.tile([P, 1], F32, name="one")
+        nc.scalar.activation(one[:], ident[:, 0:1], ACT.Exp, scale=0.0)
 
-        ts_win = placed([P, DOCS], F32, "ts_win", 0)
-        ts_win_v = ts_win[:].rearrange("m (p b c) -> m b p c", b=4, c=4)
-        for b in range(4):
-            bank = prep_ps.tile([P, 4, P], F32, name="prep_bank")
-            for c in range(4):
-                col = 4 * b + c
+        ts_window = placed([P, DOCS], F32, "ts_window", TS_WINDOW_AT)
+        ts_window_parts = ts_window[:].rearrange("m (p b c) -> m b p c", b=DOCS // P // BANK_BLOCKS, c=BANK_BLOCKS)
+        for b in range(DOCS // P // BANK_BLOCKS):
+            bank = prep_ps.tile([P, BANK_BLOCKS, P], F32, name="prep_bank")
+            for c in range(BANK_BLOCKS):
+                col = BANK_BLOCKS * b + c
                 nc.tensor.transpose(bank[:, c, :], ts_seed[:, col:col + 1].to_broadcast([P, P]), ident[:])
-            nc.scalar.activation(ts_win_v[:, b], bank[:].rearrange("m c p -> m p c"), ACT.Copy)
+            nc.scalar.activation(ts_window_parts[:, b], bank[:].rearrange("m c p -> m p c"), ACT.Copy)
 
         dt_codes = keep.tile([P, D], U32, name="dt_codes", align_bytes=64)
         dt_scales = keep.tile([P, D], U8, name="dt_scales", align_bytes=64)
 
-        def quantize_turned(grouped, half):
-            cols = slice(half * 2 * P, (half + 1) * 2 * P)
+        def quantize_turned_planes(grouped, first_plane):
+            cols = slice(first_plane * P, (first_plane + 2) * P)
             nc.vector.quantize_mx(out=dt_codes[:, cols].bitcast(E4M3X4), scales=dt_scales[:, cols], in_=grouped[:])
 
-        def turn_plain(plane, dst):
+        def turn_plane(plane, grouped):
             words = plane.bitcast(F32)
-            bank = prep_ps.tile([P, 4, P], F32, name="prep_bank")
+            bank = prep_ps.tile([P, BANK_BLOCKS, P], F32, name="prep_bank")
             for u in range(2):
-                nc.tensor.transpose(bank[:, u, :], words[:, u:SLOTS // 2:2], ident[:])
-            nc.scalar.copy(dst.bitcast(F32).rearrange("p (c u) -> p c u", u=2),
-                           bank[:, 0:2, :].rearrange("p u c -> p c u"))
+                nc.tensor.transpose(bank[:, u, :], words[:, u:HALF:2], ident[:])
+            nc.scalar.copy(grouped.bitcast(F32).rearrange("p (q u) -> p q u", u=2),
+                           bank[:, 0:2, :].rearrange("p u q -> p q u"))
 
-        d0 = keep.tile([P, SLOTS], BF16, name="d0", align_bytes=64)
-        nc.vector.tensor_copy(d0[:], d_win[0][:].indirect(offsets[:]))
+        d_plane0 = keep.tile([P, SLOTS], BF16, name="d_plane0", align_bytes=64)
+        nc.vector.tensor_copy(d_plane0[:], d_window[0][:].indirect(offsets[:]))
         ts_row = keep.tile([P, SLOTS], F32, name="ts_row")
-        nc.vector.tensor_copy(ts_row[:], ts_win[:].indirect(offsets[:]))
-        d_grouped = placed([P, SLOTS, PACK], BF16, "d_grouped", 0)
-        d1 = placed([P, SLOTS], BF16, "d1", 5)
-        dt_grouped01 = placed([P, 2 * P * PACK], BF16, "dt_grouped01", 16)
-        nc.vector.tensor_copy(d1[:], d_win[1][:].indirect(offsets[:]))
-        for t, plane in enumerate((d0, d1)):
-            turn_plain(plane[:], dt_grouped01[:, t * P * PACK:(t + 1) * P * PACK])
+        nc.vector.tensor_copy(ts_row[:], ts_window[:].indirect(offsets[:]))
+        d_grouped = placed([P, SLOTS, PACK], BF16, "d_grouped", D_GROUPED_AT)
+        d_plane1 = placed([P, SLOTS], BF16, "d_plane1", D_PLANE1_AT)
+        dt_grouped01 = placed([P, 2 * P * PACK], BF16, "dt_grouped01", DT_GROUPED01_AT)
+        nc.vector.tensor_copy(d_plane1[:], d_window[1][:].indirect(offsets[:]))
+        for t, plane in enumerate((d_plane0, d_plane1)):
+            turn_plane(plane[:], dt_grouped01[:, t * P * PACK:(t + 1) * P * PACK])
             nc.scalar.copy(d_grouped[:, :, t], plane[:])
-        quantize_turned(dt_grouped01, 0)
-        for t in (2, 3):
-            nc.vector.tensor_copy(d_grouped[:, :, t], d_win[t][:].indirect(offsets[:]))
+        quantize_turned_planes(dt_grouped01, 0)
+        nc.vector.tensor_copy(d_grouped[:, :, 2], d_window[2][:].indirect(offsets[:]))
+        half_columns = HALF // OFFSETS_PER_COLUMN
+        for half in range(2):
+            nc.vector.tensor_copy(d_grouped[:, half * HALF:(half + 1) * HALF, 3],
+                                  d_window[3][:].indirect(offsets[:, half * half_columns:(half + 1) * half_columns]))
 
-        bank = prep_ps.tile([P, 4, P], F32, name="prep_bank")
+        bank = prep_ps.tile([P, BANK_BLOCKS, P], F32, name="prep_bank")
         nc.tensor.transpose(bank[:, 0, :], uw_rows[:], ident[:])
         uw = keep.tile([P, 2 * ROW_TILES], F32, name="uw")
         nc.scalar.copy(uw[:], bank[:, 0, 0:2 * ROW_TILES])
         neg_us = keep.tile([P, ROW_TILES], F32, name="neg_us")
         nc.scalar.activation(neg_us[:], uw[:, 0:ROW_TILES], ACT.Copy, scale=-1.0)
-        stats = []
+        stats = [keep.tile([P, 2, 3], F32, name="stats%d" % pair) for pair in range(ROW_TILES // 2)]
         for j in range(ROW_TILES):
-            st = keep.tile([P, 3], F32, name="stats%d" % j)
-            nc.scalar.activation(st[:, 2:3], uw[:, ROW_TILES + j:ROW_TILES + j + 1], ACT.Copy, scale=uw[:, j:j + 1])
-            stats.append(st)
-        bank = prep_ps.tile([P, 4, P], F32, name="prep_bank")
+            nc.scalar.activation(stats[j // 2][:, j % 2, 2:3], uw[:, ROW_TILES + j:ROW_TILES + j + 1], ACT.Copy,
+                                 scale=uw[:, j:j + 1])
+        bank = prep_ps.tile([P, BANK_BLOCKS, P], F32, name="prep_bank")
         for s in range(SLOT_TILES):
             nc.tensor.transpose(bank[:, s, :], ts_row[:, s * P:(s + 1) * P], ident[:])
         ts_col = keep.tile([P, SLOT_TILES], F32, name="ts_col")
         nc.scalar.copy(ts_col[:], bank[:, :, 0])
 
-        x_grouped_at = [4.5, 5.5, 16]
-        x_codes_at = [9, 8, 9]
         x_grouped = []
-        for n, (c0, c1) in enumerate(x_spans):
-            grouped = placed([P, c1 - c0, PACK], BF16, "x_grouped%d" % n, x_grouped_at[n])
-            nc.scalar.copy(grouped[:].rearrange("p (c i) t -> p c t i", i=4),
-                           x_raw[n][:].rearrange("p t (c i) -> p c t i", i=4))
+        for n, (first, end) in enumerate(X_SPANS):
+            grouped = placed([P, end - first, PACK], BF16, "x_grouped%d" % n, X_GROUPED_AT[n])
+            nc.scalar.copy(grouped[:].rearrange("p (c m) t -> p c t m", m=4),
+                           x_raw[n][:].rearrange("p t (c m) -> p c t m", m=4))
             x_grouped.append(grouped)
 
         def quantize_x(n):
-            width = x_spans[n][1] - x_spans[n][0]
-            codes = placed([P, width], U32, "x_codes%d" % n, x_codes_at[n])
+            width = X_SPANS[n][1] - X_SPANS[n][0]
+            codes = placed([P, width], U32, "x_codes%d" % n, X_CODES_AT[n])
             scales = keep.tile([P, width], U8, name="x_scales%d" % n, align_bytes=64)
             nc.vector.quantize_mx(out=codes[:].bitcast(E4M3X4), scales=scales[:],
                                   in_=x_grouped[n][:].rearrange("p r t -> p (r t)"))
@@ -148,106 +165,130 @@ def tile_attend_grag_q_kernel(tc, xT, dT, us, ts, lk, wt, offs, out):
 
         d_codes = keep.tile([P, SLOTS], U32, name="d_codes", align_bytes=64)
         d_scales = keep.tile([P, SLOTS], U8, name="d_scales", align_bytes=64)
-        nc.vector.quantize_mx(out=d_codes[:].bitcast(E4M3X4), scales=d_scales[:],
-                              in_=d_grouped[:].rearrange("p i t -> p (i t)"))
+        for half in range(2):
+            cols = slice(half * HALF, (half + 1) * HALF)
+            nc.vector.quantize_mx(out=d_codes[:, cols].bitcast(E4M3X4), scales=d_scales[:, cols],
+                                  in_=d_grouped[:, cols, :].rearrange("p i t -> p (i t)"))
 
         e = [keep.tile([P, SLOTS], F32, name="e%d" % j) for j in range(ROW_TILES)]
-        g_grouped = [keep.tile([P, P * PACK], BF16, name="g_grouped%d" % j, align_bytes=64) for j in range(ROW_TILES)]
+        g_group_tiles = [keep.tile([P, len(group) * P * PACK], BF16, name="g_grouped%d" % group[0], align_bytes=64)
+                         for group in PRODUCT_GROUPS]
+        g_grouped = [tile[:, k * P * PACK:(k + 1) * P * PACK]
+                     for group, tile in zip(PRODUCT_GROUPS, g_group_tiles) for k in range(len(group))]
 
-        def scores_by_rows(j):
+        def scores_by_rows(j, pieces, pool, tag):
             x_codes, x_scales = quantize_x(j)
-            a = score_ps.tile([P, SLOTS], F32, name="score_bank")
-            nc.tensor.matmul_mx(out=a[:], lhsT=x_codes[:].bitcast(E4M3X4), lhsT_scale=x_scales[:],
-                                rhs=d_codes[:].bitcast(E4M3X4), rhs_scale=d_scales[:], start=True, stop=True)
-            z = keep.tile([P, SLOTS], F32, name="z%d" % j)
-            nc.vector.scalar_tensor_tensor(z[:], a[:], uw[:, j:j + 1], ts_row[:], ALU.mult, ALU.mult)
+            z = placed([P, SLOTS], F32, "z%d" % j, Z_AT[j])
+            width = SLOTS // pieces
+            for piece in range(pieces):
+                cols = slice(piece * width, (piece + 1) * width)
+                a = pool.tile([P, width], F32, name=tag)
+                nc.tensor.matmul_mx(out=a[:], lhsT=x_codes[:].bitcast(E4M3X4), lhsT_scale=x_scales[:],
+                                    rhs=d_codes[:, cols].bitcast(E4M3X4), rhs_scale=d_scales[:, cols],
+                                    start=True, stop=True)
+                nc.vector.scalar_tensor_tensor(z[:, cols], a[:], uw[:, j:j + 1], ts_row[:, cols], ALU.mult, ALU.mult)
             neg_max = keep.tile([P, 1], F32, name="neg_max%d" % j)
             nc.vector.tensor_reduce(neg_max[:], z[:], AX.X, ALU.max, negate=True)
-            nc.scalar.activation(e[j][:], z[:], ACT.Exp, bias=neg_max[:], accum_out=stats[j][:, 0:1])
+            nc.scalar.activation(e[j][:], z[:], ACT.Exp, bias=neg_max[:], accum_out=stats[j // 2][:, j % 2, 0:1])
 
         def scores_by_slots():
             x_codes, x_scales = quantize_x(2)
             scaled = keep.tile([P, SLOT_TILES, 2 * P], F32, name="scaled")
-            for pair in range(SLOT_TILES // 2):
+            for s0 in range(0, SLOT_TILES, 2):
                 a = prep_ps.tile([P, 2, 2 * P], F32, name="prep_bank")
                 for k in range(2):
-                    cols = slice((2 * pair + k) * P, (2 * pair + k + 1) * P)
-                    nc.tensor.matmul_mx(out=a[:, k, :], lhsT=d_codes[:, cols].bitcast(E4M3X4), lhsT_scale=d_scales[:, cols],
-                                        rhs=x_codes[:].bitcast(E4M3X4), rhs_scale=x_scales[:], start=True, stop=True)
+                    cols = slice((s0 + k) * P, (s0 + k + 1) * P)
+                    nc.tensor.matmul_mx(out=a[:, k, :], lhsT=d_codes[:, cols].bitcast(E4M3X4),
+                                        lhsT_scale=d_scales[:, cols], rhs=x_codes[:].bitcast(E4M3X4),
+                                        rhs_scale=x_scales[:], start=True, stop=True)
                 for k in range(2):
-                    s = 2 * pair + k
-                    nc.scalar.activation(scaled[:, s, :], a[:, k, :], ACT.Copy, scale=ts_col[:, s:s + 1])
+                    nc.scalar.activation(scaled[:, s0 + k, :], a[:, k, :], ACT.Copy, scale=ts_col[:, s0 + k:s0 + k + 1])
             return scaled
 
         def turn_scores(scaled, j):
-            y = score_ps.tile([P, SLOTS], F32, name="score_bank")
+            ts_a = score_ps.tile([P, SLOTS], F32, name="score_bank")
+            rows = slice(j * P - X_SPANS[2][0], (j + 1) * P - X_SPANS[2][0])
             for s in range(SLOT_TILES):
-                nc.tensor.transpose(y[:, s * P:(s + 1) * P], scaled[:, s, (j - 2) * P:(j - 1) * P], ident[:])
-            neg_z = keep.tile([P, SLOTS], F32, name="z%d" % j)
+                nc.tensor.transpose(ts_a[:, s * P:(s + 1) * P], scaled[:, s, rows], ident[:])
+            neg_z = placed([P, SLOTS], F32, "neg_z%d" % j, Z_AT[j])
             neg_max = keep.tile([P, 1], F32, name="neg_max%d" % j)
-            nc.vector.tensor_scalar(neg_z[:], y[:], neg_us[:, j:j + 1], None, ALU.mult, ALU.min, accum_out=neg_max[:])
-            nc.scalar.activation(e[j][:], neg_z[:], ACT.Exp, bias=neg_max[:], scale=-1.0, accum_out=stats[j][:, 0:1])
+            nc.vector.tensor_scalar(neg_z[:], ts_a[:], neg_us[:, j:j + 1], None, ALU.mult, ALU.min, accum_out=neg_max[:])
+            nc.scalar.activation(e[j][:], neg_z[:], ACT.Exp, bias=neg_max[:], scale=-1.0,
+                                 accum_out=stats[j // 2][:, j % 2, 0:1])
 
-        def turn_last_planes():
-            dealt = keep.tile([P, PACK, P], F32, name="dealt23")
+        def turn_planes_2_and_3():
+            sorted_words = keep.tile([P, PACK, P], F32, name="sorted_words")
             words = d_grouped[:].rearrange("p i t -> p (i t)").bitcast(F32).rearrange("p (s t v) -> p s t v", t=PACK, v=2)
-            nc.scalar.copy(dealt[:].rearrange("p t s -> p s t"), words[:, :, :, 1])
+            nc.scalar.copy(sorted_words[:].rearrange("p t s -> p s t"), words[:, :, :, 1])
             bank = turn_ps.tile([P, PACK, P], F32, name="turn_bank")
             for t in range(PACK):
-                nc.tensor.transpose(bank[:, t, :], dealt[:, t, :], ident[:])
-            grouped = keep.tile([P, 2 * P * PACK], BF16, name="dt_grouped23", align_bytes=64)
-            nc.scalar.copy(grouped[:].rearrange("p (v c t) -> p v c t", v=2, t=PACK),
-                           bank[:].rearrange("p t c -> p (t c)").bitcast(BF16).rearrange("p (t c v) -> p v c t", t=PACK, v=2))
-            quantize_turned(grouped, 1)
+                nc.tensor.transpose(bank[:, t, :], sorted_words[:, t, :], ident[:])
+            grouped = placed([P, 2 * P * PACK], BF16, "dt_grouped23", DT_GROUPED23_AT)
+            halves = bank[:].rearrange("s t q -> s (t q)").bitcast(BF16)
+            nc.scalar.copy(grouped[:].rearrange("s (v q t) -> s v q t", v=2, t=PACK),
+                           halves.rearrange("s (t q v) -> s v q t", t=PACK, v=2))
+            quantize_turned_planes(grouped, 2)
 
-        def gradient(j):
-            st = stats[j]
-            f = keep.tile([P, SLOTS], F32, name="f%d" % j)
-            nc.vector.scalar_tensor_tensor(f[:], e[j][:], 1.0, lk_sb[j][:], ALU.mult, ALU.mult, accum_out=st[:, 1:2])
-            inv = keep.tile([P, 2], F32, name="inv%d" % j)
-            nc.vector.reciprocal(inv[:], st[:, 0:2])
-            factor = keep.tile([P, 2], F32, name="factor%d" % j)
-            nc.vector.tensor_tensor(factor[:], inv[:], st[:, 1:3], ALU.mult)
-            w = keep.tile([P, SLOTS], F32, name="w%d" % j)
-            nc.vector.scalar_tensor_tensor(w[:], e[j][:], factor[:, 0:1], f[:], ALU.mult, ALU.subtract)
-            g = keep.tile([P, SLOTS], BF16, name="g%d" % j, align_bytes=64)
-            nc.vector.scalar_tensor_tensor(g[:], w[:], factor[:, 1:2], ts_row[:], ALU.mult, ALU.mult)
-            turned = turn_ps.tile([P, PACK, P], F32, name="turn_bank")
-            g_words = g[:].bitcast(F32)
-            for u in range(2):
-                nc.tensor.transpose(turned[:, u, :], g_words[:, u:SLOTS // 2:2], ident[:])
-            nc.scalar.copy(g_grouped[j][:].bitcast(F32).rearrange("p (r u) -> p r u", u=2), turned[:, 0:2, :].rearrange("p u r -> p r u"))
+        def gradient(pair):
+            pair_stats = stats[pair]
+            tiles = (2 * pair, 2 * pair + 1)
+            f = {}
+            for j in tiles:
+                f[j] = placed([P, SLOTS], F32, "f%d" % j, F_AT[j])
+                nc.vector.scalar_tensor_tensor(f[j][:], e[j][:], one[:], lk_rows[j][:], ALU.mult, ALU.mult,
+                                               accum_out=pair_stats[:, j % 2, 1:2])
+            inverse = keep.tile([P, 2, 2], F32, name="inverse%d" % pair)
+            nc.vector.reciprocal(inverse[:], pair_stats[:, :, 0:2])
+            factor = keep.tile([P, 2, 2], F32, name="factor%d" % pair)
+            nc.vector.tensor_tensor(factor[:], inverse[:], pair_stats[:, :, 1:3], ALU.mult)
+            difference = {}
+            for j in tiles:
+                difference[j] = keep.tile([P, SLOTS], F32, name="difference%d" % j)
+                nc.vector.scalar_tensor_tensor(difference[j][:], e[j][:], factor[:, j % 2, 0:1], f[j][:],
+                                               ALU.mult, ALU.subtract)
+            ts_by_four = ts_row[:].rearrange("r (p t) -> r p t", t=PACK)
+            for j in tiles:
+                by_four = difference[j][:].rearrange("r (p t) -> r p t", t=PACK)
+                bank = turn_ps.tile([P, PACK, P], F32, name="turn_bank")
+                for u in range(2):
+                    g_part = keep.tile([P, HALF], BF16, name="g%d_%d" % (j, u), align_bytes=64)
+                    nc.vector.scalar_tensor_tensor(g_part[:].rearrange("r (p v) -> r p v", v=2),
+                                                   by_four[:, :, 2 * u:2 * u + 2], factor[:, j % 2, 1:2],
+                                                   ts_by_four[:, :, 2 * u:2 * u + 2], ALU.mult, ALU.mult)
+                    nc.tensor.transpose(bank[:, u, :], g_part[:].bitcast(F32), ident[:])
+                nc.scalar.copy(g_grouped[j].bitcast(F32).rearrange("p (r u) -> p r u", u=2),
+                               bank[:, 0:2, :].rearrange("p u r -> p r u"))
 
-        def product(j):
-            g_codes = keep.tile([P, P], U32, name="g_codes%d" % j, align_bytes=64)
-            g_scales = keep.tile([P, P], U8, name="g_scales%d" % j, align_bytes=64)
-            nc.vector.quantize_mx(out=g_codes[:].bitcast(E5M2X4), scales=g_scales[:], in_=g_grouped[j][:])
-            res = out_ps.tile([P, D], F32, name="res")
-            nc.tensor.matmul_mx(out=res[:], lhsT=g_codes[:].bitcast(E5M2X4), lhsT_scale=g_scales[:],
-                                rhs=dt_codes[:].bitcast(E4M3X4), rhs_scale=dt_scales[:], start=True, stop=True)
-            staged = keep.tile([P, P, PACK], F32, name="staged%d" % j)
-            res_natural = res[:].rearrange("r (t c) -> r c t", t=PACK)
-            rows = slice(j * P, (j + 1) * P)
-            if j < ROW_TILES - 1:
-                nc.scalar.copy(staged[:], res_natural)
-                nc.sync.dma_start(out[rows, :], staged[:].rearrange("r c t -> r (c t)"))
-            else:
-                for half in range(2):
-                    cs = slice(half * P // 2, (half + 1) * P // 2)
-                    nc.vector.tensor_copy(staged[:, cs, :], res_natural[:, cs, :])
-                    nc.sync.dma_start(out[rows, half * D // 2:(half + 1) * D // 2], staged[:, cs, :].rearrange("r c t -> r (c t)"))
+        def product(n):
+            group = PRODUCT_GROUPS[n]
+            g_codes = placed([P, len(group) * P], U32, "g_codes%d" % n, G_CODES_AT[n])
+            g_scales = keep.tile([P, len(group) * P], U8, name="g_scales%d" % n, align_bytes=64)
+            nc.vector.quantize_mx(out=g_codes[:].bitcast(E5M2X4), scales=g_scales[:], in_=g_group_tiles[n][:])
+            for k, j in enumerate(group):
+                cols = slice(k * P, (k + 1) * P)
+                sums = out_ps.tile([P, D], F32, name="sums")
+                nc.tensor.matmul_mx(out=sums[:], lhsT=g_codes[:, cols].bitcast(E5M2X4), lhsT_scale=g_scales[:, cols],
+                                    rhs=dt_codes[:].bitcast(E4M3X4), rhs_scale=dt_scales[:], start=True, stop=True)
+                staged = keep.tile([P, P, PACK], F32, name="staged%d" % j)
+                in_order = sums[:].rearrange("r (t q) -> r q t", t=PACK)
+                rows = slice(j * P, (j + 1) * P)
+                if j < ROW_TILES - 1:
+                    nc.scalar.copy(staged[:], in_order)
+                    nc.sync.dma_start(out[rows, :], staged[:].rearrange("r q t -> r (q t)"))
+                else:
+                    for half in range(2):
+                        qs = slice(half * P // 2, (half + 1) * P // 2)
+                        nc.vector.tensor_copy(staged[:, qs, :], in_order[:, qs, :])
+                        nc.sync.dma_start(out[rows, half * D // 2:(half + 1) * D // 2],
+                                          staged[:, qs, :].rearrange("r q t -> r (q t)"))
 
-        scores_by_rows(0)
-        scores_by_rows(1)
-        turn_last_planes()
+        scores_by_rows(0, 2, score_ps, "score_bank")
+        scores_by_rows(1, 1, prep_ps, "prep_bank")
+        turn_planes_2_and_3()
         scaled = scores_by_slots()
         gradient(0)
         turn_scores(scaled, 2)
-        gradient(1)
         turn_scores(scaled, 3)
-        product(0)
-        gradient(2)
-        product(1)
-        gradient(3)
-        product(2)
-        product(3)
+        gradient(1)
+        for n in range(len(PRODUCT_GROUPS)):
+            product(n)

@@ -27,20 +27,16 @@ OFFSETS_PER_COLUMN = 16
 BANK_BLOCKS = 4
 
 X_SPANS = ((0, P), (P, 2 * P), (2 * P, R))
-PRODUCT_GROUPS = ((0, 1), (2,), (3,))
 
-TS_WINDOW_AT = 0
-D_GROUPED_AT = 0
-D_PLANE1_AT = 5
-D_WINDOW3_AT = 8
-DT_GROUPED01_AT = 16
-X_GROUPED_AT = (4.5, 5.5, 16)
-X_CODES_AT = (9, 8, 21)
-DT_GROUPED23_AT = 18.5
-Z_AT = (20, 22, 32, 34)
-F_AT = (32, 34, 36, 38)
-LK_AT = (40, 42, 44, 46)
-G_CODES_AT = (44, 40, 42)
+D_WINDOW_AT = (0, 8, 16, 32)
+X_RAW_AT = (8, 10, 12)
+LK_AT = (16, 18, 20, 22)
+TS_WINDOW_AT = 24
+D_GROUPED_AT = 24
+Z_AT = (40, 42, 44, 46)
+D_CODES_AT = 8
+DT_CODES_AT = 10
+D_PLANE_AT = {2: 12, 3: 42}
 
 FLOPS = 2 * 2 * R * SLOTS * D
 BYTES = 4 * (D * R + D * DOCS + R * SLOTS + R * D + DOCS + 2 * R) + 2 * P * SLOTS // OFFSETS_PER_COLUMN
@@ -61,8 +57,7 @@ def tile_attend_grag_q_kernel(tc, xT, dT, us, ts, lk, wt, offs, out):
 
         offsets = keep.tile([P, SLOTS // OFFSETS_PER_COLUMN], U16, name="offsets")
         d_planes = dT.rearrange("(p t) n -> t p n", t=PACK)
-        d_window = [keep.tile([P, DOCS], F32, name="d_window%d" % t) for t in range(PACK - 1)]
-        d_window.append(placed([P, DOCS], F32, "d_window3", D_WINDOW3_AT))
+        d_window = [placed([P, DOCS], F32, "d_window%d" % t, D_WINDOW_AT[t]) for t in range(PACK)]
         ts_seed = keep.tile([P, DOCS // P], F32, name="ts_seed")
         uw_rows = keep.tile([P, P], F32, name="uw_rows")
         nc.gpsimd.memset(uw_rows[:], 0.0)
@@ -74,15 +69,6 @@ def tile_attend_grag_q_kernel(tc, xT, dT, us, ts, lk, wt, offs, out):
         nc.sync.dma_start(uw_rows[ROW_TILES:2 * ROW_TILES, :], wt.rearrange("(j p) o -> j (p o)", p=P))
         for t in range(1, PACK):
             nc.sync.dma_start(d_window[t][:], d_planes[t])
-        x_planes = xT.rearrange("(p t) r -> p t r", t=PACK)
-        x_raw = []
-        for first, end in X_SPANS:
-            span = keep.tile([P, PACK, end - first], F32, name="x_raw%d" % first)
-            nc.sync.dma_start(span[:], x_planes[:, :, first:end])
-            x_raw.append(span)
-        lk_rows = [placed([P, SLOTS], F32, "lk_rows%d" % j, LK_AT[j]) for j in range(ROW_TILES)]
-        for j in range(ROW_TILES):
-            nc.sync.dma_start(lk_rows[j][:], lk[j * P:(j + 1) * P, :])
 
         ident = keep.tile([P, P], F32, name="ident")
         make_identity(nc, ident[:])
@@ -99,38 +85,38 @@ def tile_attend_grag_q_kernel(tc, xT, dT, us, ts, lk, wt, offs, out):
                 nc.tensor.transpose(bank[:, c, :], ts_seed[:, col:col + 1].to_broadcast([P, P]), ident[:])
             nc.scalar.activation(ts_window_parts[:, b], bank[:].rearrange("m c p -> m p c"), ACT.Copy)
 
-        dt_codes = keep.tile([P, D], U32, name="dt_codes", align_bytes=64)
+        dt_codes = placed([P, D], U32, "dt_codes", DT_CODES_AT)
         dt_scales = keep.tile([P, D], U8, name="dt_scales", align_bytes=64)
+        dt_grouped = [keep.tile([P, 2 * P * PACK], BF16, name="dt_grouped%d" % n, align_bytes=64) for n in range(2)]
 
-        def quantize_turned_planes(grouped, first_plane):
-            cols = slice(first_plane * P, (first_plane + 2) * P)
-            nc.vector.quantize_mx(out=dt_codes[:, cols].bitcast(E4M3X4), scales=dt_scales[:, cols], in_=grouped[:])
+        def quantize_turned_planes(n):
+            cols = slice(2 * n * P, (2 * n + 2) * P)
+            nc.vector.quantize_mx(out=dt_codes[:, cols].bitcast(E4M3X4), scales=dt_scales[:, cols], in_=dt_grouped[n][:])
 
-        def turn_plane(plane, grouped):
+        def turn_plane(plane, t):
             words = plane.bitcast(F32)
+            grouped = dt_grouped[t // 2][:, t % 2 * P * PACK:(t % 2 + 1) * P * PACK]
             bank = prep_ps.tile([P, BANK_BLOCKS, P], F32, name="prep_bank")
             for u in range(2):
                 nc.tensor.transpose(bank[:, u, :], words[:, u:HALF:2], ident[:])
             nc.scalar.copy(grouped.bitcast(F32).rearrange("p (q u) -> p q u", u=2),
                            bank[:, 0:2, :].rearrange("p u q -> p q u"))
 
-        d_plane0 = keep.tile([P, SLOTS], BF16, name="d_plane0", align_bytes=64)
-        nc.vector.tensor_copy(d_plane0[:], d_window[0][:].indirect(offsets[:]))
+        d_planes01 = keep.tile([P, 2, SLOTS], BF16, name="d_planes01", align_bytes=64)
+        nc.vector.tensor_copy(d_planes01[:, 0, :], d_window[0][:].indirect(offsets[:]))
         ts_row = keep.tile([P, SLOTS], F32, name="ts_row")
         nc.vector.tensor_copy(ts_row[:], ts_window[:].indirect(offsets[:]))
         d_grouped = placed([P, SLOTS, PACK], BF16, "d_grouped", D_GROUPED_AT)
-        d_plane1 = placed([P, SLOTS], BF16, "d_plane1", D_PLANE1_AT)
-        dt_grouped01 = placed([P, 2 * P * PACK], BF16, "dt_grouped01", DT_GROUPED01_AT)
-        nc.vector.tensor_copy(d_plane1[:], d_window[1][:].indirect(offsets[:]))
-        for t, plane in enumerate((d_plane0, d_plane1)):
-            turn_plane(plane[:], dt_grouped01[:, t * P * PACK:(t + 1) * P * PACK])
-            nc.scalar.copy(d_grouped[:, :, t], plane[:])
-        quantize_turned_planes(dt_grouped01, 0)
-        nc.vector.tensor_copy(d_grouped[:, :, 2], d_window[2][:].indirect(offsets[:]))
-        half_columns = HALF // OFFSETS_PER_COLUMN
-        for half in range(2):
-            nc.vector.tensor_copy(d_grouped[:, half * HALF:(half + 1) * HALF, 3],
-                                  d_window[3][:].indirect(offsets[:, half * half_columns:(half + 1) * half_columns]))
+        turn_plane(d_planes01[:, 0, :], 0)
+        nc.vector.tensor_copy(d_planes01[:, 1, :], d_window[1][:].indirect(offsets[:]))
+        x_planes = xT.rearrange("(p t) r -> p t r", t=PACK)
+        x_raw = []
+        for n, (first, end) in enumerate(X_SPANS):
+            span = placed([P, PACK, end - first], F32, "x_raw%d" % n, X_RAW_AT[n])
+            nc.sync.dma_start(span[:], x_planes[:, :, first:end])
+            x_raw.extend(span[:, :, k:k + P] for k in range(0, end - first, P))
+        turn_plane(d_planes01[:, 1, :], 1)
+        nc.scalar.copy(d_grouped[:, :, 0:2], d_planes01[:].rearrange("p t i -> p i t"))
 
         bank = prep_ps.tile([P, BANK_BLOCKS, P], F32, name="prep_bank")
         nc.tensor.transpose(bank[:, 0, :], uw_rows[:], ident[:])
@@ -138,9 +124,9 @@ def tile_attend_grag_q_kernel(tc, xT, dT, us, ts, lk, wt, offs, out):
         nc.scalar.copy(uw[:], bank[:, 0, 0:2 * ROW_TILES])
         neg_us = keep.tile([P, ROW_TILES], F32, name="neg_us")
         nc.scalar.activation(neg_us[:], uw[:, 0:ROW_TILES], ACT.Copy, scale=-1.0)
-        stats = [keep.tile([P, 2, 3], F32, name="stats%d" % pair) for pair in range(ROW_TILES // 2)]
+        stats = [keep.tile([P, 3], F32, name="stats%d" % j) for j in range(ROW_TILES)]
         for j in range(ROW_TILES):
-            nc.scalar.activation(stats[j // 2][:, j % 2, 2:3], uw[:, ROW_TILES + j:ROW_TILES + j + 1], ACT.Copy,
+            nc.scalar.activation(stats[j][:, 2:3], uw[:, ROW_TILES + j:ROW_TILES + j + 1], ACT.Copy,
                                  scale=uw[:, j:j + 1])
         bank = prep_ps.tile([P, BANK_BLOCKS, P], F32, name="prep_bank")
         for s in range(SLOT_TILES):
@@ -148,147 +134,200 @@ def tile_attend_grag_q_kernel(tc, xT, dT, us, ts, lk, wt, offs, out):
         ts_col = keep.tile([P, SLOT_TILES], F32, name="ts_col")
         nc.scalar.copy(ts_col[:], bank[:, :, 0])
 
-        x_grouped = []
-        for n, (first, end) in enumerate(X_SPANS):
-            grouped = placed([P, end - first, PACK], BF16, "x_grouped%d" % n, X_GROUPED_AT[n])
-            nc.scalar.copy(grouped[:].rearrange("p (c m) t -> p c t m", m=4),
-                           x_raw[n][:].rearrange("p t (c m) -> p c t m", m=4))
-            x_grouped.append(grouped)
+        def turn_woven_plane(t):
+            plane = placed([P, SLOTS], BF16, "d_plane%d" % t, D_PLANE_AT[t])
+            nc.scalar.copy(plane[:], d_grouped[:, :, t])
+            turn_plane(plane[:], t)
 
-        def quantize_x(n):
-            width = X_SPANS[n][1] - X_SPANS[n][0]
-            codes = placed([P, width], U32, "x_codes%d" % n, X_CODES_AT[n])
-            scales = keep.tile([P, width], U8, name="x_scales%d" % n, align_bytes=64)
-            nc.vector.quantize_mx(out=codes[:].bitcast(E4M3X4), scales=scales[:],
-                                  in_=x_grouped[n][:].rearrange("p r t -> p (r t)"))
-            return codes, scales
-
-        d_codes = keep.tile([P, SLOTS], U32, name="d_codes", align_bytes=64)
-        d_scales = keep.tile([P, SLOTS], U8, name="d_scales", align_bytes=64)
+        nc.vector.tensor_copy(d_grouped[:, :, 2], d_window[2][:].indirect(offsets[:]))
+        lk_rows = [placed([P, SLOTS], F32, "lk_rows%d" % j, LK_AT[j]) for j in range(ROW_TILES)]
+        for j in range(ROW_TILES):
+            nc.sync.dma_start(lk_rows[j][:], lk[j * P:(j + 1) * P, :])
+        half_columns = HALF // OFFSETS_PER_COLUMN
         for half in range(2):
+            nc.vector.tensor_copy(d_grouped[:, half * HALF:(half + 1) * HALF, 3],
+                                  d_window[3][:].indirect(offsets[:, half * half_columns:(half + 1) * half_columns]))
+
+        d_codes = placed([P, SLOTS], U32, "d_codes", D_CODES_AT)
+        d_scales = keep.tile([P, SLOTS], U8, name="d_scales", align_bytes=64)
+
+        def quantize_d(half):
             cols = slice(half * HALF, (half + 1) * HALF)
             nc.vector.quantize_mx(out=d_codes[:, cols].bitcast(E4M3X4), scales=d_scales[:, cols],
                                   in_=d_grouped[:, cols, :].rearrange("p i t -> p (i t)"))
 
-        e = [keep.tile([P, SLOTS], F32, name="e%d" % j) for j in range(ROW_TILES)]
-        g_group_tiles = [keep.tile([P, len(group) * P * PACK], BF16, name="g_grouped%d" % group[0], align_bytes=64)
-                         for group in PRODUCT_GROUPS]
-        g_grouped = [tile[:, k * P * PACK:(k + 1) * P * PACK]
-                     for group, tile in zip(PRODUCT_GROUPS, g_group_tiles) for k in range(len(group))]
+        def tiles(name, shape, dtype):
+            return [keep.tile(shape, dtype, name="%s%d" % (name, j), align_bytes=64) for j in range(ROW_TILES)]
 
-        def scores_by_rows(j, pieces, pool, tag):
-            x_codes, x_scales = quantize_x(j)
-            z = placed([P, SLOTS], F32, "z%d" % j, Z_AT[j])
-            width = SLOTS // pieces
-            for piece in range(pieces):
-                cols = slice(piece * width, (piece + 1) * width)
-                a = pool.tile([P, width], F32, name=tag)
-                nc.tensor.matmul_mx(out=a[:], lhsT=x_codes[:].bitcast(E4M3X4), lhsT_scale=x_scales[:],
-                                    rhs=d_codes[:, cols].bitcast(E4M3X4), rhs_scale=d_scales[:, cols],
-                                    start=True, stop=True)
-                nc.vector.scalar_tensor_tensor(z[:, cols], a[:], uw[:, j:j + 1], ts_row[:, cols], ALU.mult, ALU.mult)
-            neg_max = keep.tile([P, 1], F32, name="neg_max%d" % j)
-            nc.vector.tensor_reduce(neg_max[:], z[:], AX.X, ALU.max, negate=True)
-            nc.scalar.activation(e[j][:], z[:], ACT.Exp, bias=neg_max[:], accum_out=stats[j // 2][:, j % 2, 0:1])
+        x_grouped = tiles("x_grouped", [P, P, PACK], BF16)
+        x_codes = tiles("x_codes", [P, P], U32)
+        x_scales = tiles("x_scales", [P, P], U8)
+        scaled = tiles("scaled", [P, SLOT_TILES, P], F32)
+        z = [placed([P, SLOTS], F32, "z%d" % j, Z_AT[j]) for j in range(ROW_TILES)]
+        neg_max = tiles("neg_max", [P, 1], F32)
+        e = tiles("e", [P, SLOTS], F32)
+        f = tiles("f", [P, SLOTS], F32)
+        inverse = tiles("inverse", [P, 2], F32)
+        factor = tiles("factor", [P, 2], F32)
+        difference = tiles("difference", [P, SLOTS], F32)
+        g_words = [tiles("g_words%d_" % u, [P, HALF], BF16) for u in range(2)]
+        g_grouped = tiles("g_grouped", [P, P * PACK], BF16)
+        g_codes = tiles("g_codes", [P, P], U32)
+        g_scales = tiles("g_scales", [P, P], U8)
+        staged = tiles("staged", [P, P, PACK], F32)
+        turned_g = {}
+        sums = {}
 
-        def scores_by_slots():
-            x_codes, x_scales = quantize_x(2)
-            scaled = keep.tile([P, SLOT_TILES, 2 * P], F32, name="scaled")
-            for s0 in range(0, SLOT_TILES, 2):
-                a = prep_ps.tile([P, 2, 2 * P], F32, name="prep_bank")
-                for k in range(2):
-                    cols = slice((s0 + k) * P, (s0 + k + 1) * P)
-                    nc.tensor.matmul_mx(out=a[:, k, :], lhsT=d_codes[:, cols].bitcast(E4M3X4),
-                                        lhsT_scale=d_scales[:, cols], rhs=x_codes[:].bitcast(E4M3X4),
-                                        rhs_scale=x_scales[:], start=True, stop=True)
-                for k in range(2):
-                    nc.scalar.activation(scaled[:, s0 + k, :], a[:, k, :], ACT.Copy, scale=ts_col[:, s0 + k:s0 + k + 1])
-            return scaled
+        def group_x(j):
+            nc.scalar.copy(x_grouped[j][:].rearrange("p (c m) t -> p c t m", m=4),
+                           x_raw[j].rearrange("p t (c m) -> p c t m", m=4))
 
-        def turn_scores(scaled, j):
-            ts_a = score_ps.tile([P, SLOTS], F32, name="score_bank")
-            rows = slice(j * P - X_SPANS[2][0], (j + 1) * P - X_SPANS[2][0])
+        def quantize_x(j):
+            nc.vector.quantize_mx(out=x_codes[j][:].bitcast(E4M3X4), scales=x_scales[j][:],
+                                  in_=x_grouped[j][:].rearrange("p r t -> p (r t)"))
+
+        def score_half_by_rows(j, half):
+            cols = slice(half * HALF, (half + 1) * HALF)
+            a = score_ps.tile([P, HALF], F32, name="score_bank")
+            nc.tensor.matmul_mx(out=a[:], lhsT=x_codes[j][:].bitcast(E4M3X4), lhsT_scale=x_scales[j][:],
+                                rhs=d_codes[:, cols].bitcast(E4M3X4), rhs_scale=d_scales[:, cols],
+                                start=True, stop=True)
+            nc.vector.scalar_tensor_tensor(z[j][:, cols], a[:], neg_us[:, j:j + 1], ts_row[:, cols], ALU.mult, ALU.mult)
+
+        def score_by_rows(j):
+            a = prep_ps.tile([P, SLOTS], F32, name="prep_bank")
+            nc.tensor.matmul_mx(out=a[:], lhsT=x_codes[j][:].bitcast(E4M3X4), lhsT_scale=x_scales[j][:],
+                                rhs=d_codes[:].bitcast(E4M3X4), rhs_scale=d_scales[:], start=True, stop=True)
+            nc.vector.scalar_tensor_tensor(z[j][:], a[:], neg_us[:, j:j + 1], ts_row[:], ALU.mult, ALU.mult)
+
+        def row_minimum(j):
+            nc.vector.tensor_reduce(neg_max[j][:], z[j][:], AX.X, ALU.min)
+
+        def score_by_slots(j):
+            a = prep_ps.tile([P, SLOT_TILES, P], F32, name="prep_bank")
             for s in range(SLOT_TILES):
-                nc.tensor.transpose(ts_a[:, s * P:(s + 1) * P], scaled[:, s, rows], ident[:])
-            neg_z = placed([P, SLOTS], F32, "neg_z%d" % j, Z_AT[j])
-            neg_max = keep.tile([P, 1], F32, name="neg_max%d" % j)
-            nc.vector.tensor_scalar(neg_z[:], ts_a[:], neg_us[:, j:j + 1], None, ALU.mult, ALU.min, accum_out=neg_max[:])
-            nc.scalar.activation(e[j][:], neg_z[:], ACT.Exp, bias=neg_max[:], scale=-1.0,
-                                 accum_out=stats[j // 2][:, j % 2, 0:1])
+                cols = slice(s * P, (s + 1) * P)
+                nc.tensor.matmul_mx(out=a[:, s, :], lhsT=d_codes[:, cols].bitcast(E4M3X4),
+                                    lhsT_scale=d_scales[:, cols], rhs=x_codes[j][:].bitcast(E4M3X4),
+                                    rhs_scale=x_scales[j][:], start=True, stop=True)
+            for s in range(SLOT_TILES):
+                nc.scalar.activation(scaled[j][:, s, :], a[:, s, :], ACT.Copy, scale=ts_col[:, s:s + 1])
 
-        def turn_planes_2_and_3():
-            sorted_words = keep.tile([P, PACK, P], F32, name="sorted_words")
-            words = d_grouped[:].rearrange("p i t -> p (i t)").bitcast(F32).rearrange("p (s t v) -> p s t v", t=PACK, v=2)
-            nc.scalar.copy(sorted_words[:].rearrange("p t s -> p s t"), words[:, :, :, 1])
-            bank = turn_ps.tile([P, PACK, P], F32, name="turn_bank")
-            for t in range(PACK):
-                nc.tensor.transpose(bank[:, t, :], sorted_words[:, t, :], ident[:])
-            grouped = placed([P, 2 * P * PACK], BF16, "dt_grouped23", DT_GROUPED23_AT)
-            halves = bank[:].rearrange("s t q -> s (t q)").bitcast(BF16)
-            nc.scalar.copy(grouped[:].rearrange("s (v q t) -> s v q t", v=2, t=PACK),
-                           halves.rearrange("s (t q v) -> s v q t", t=PACK, v=2))
-            quantize_turned_planes(grouped, 2)
+        def turn_scores(j):
+            ts_a = score_ps.tile([P, SLOTS], F32, name="score_bank")
+            for s in range(SLOT_TILES):
+                nc.tensor.transpose(ts_a[:, s * P:(s + 1) * P], scaled[j][:, s, :], ident[:])
+            nc.vector.tensor_scalar(z[j][:], ts_a[:], neg_us[:, j:j + 1], None, ALU.mult, ALU.min, accum_out=neg_max[j][:])
 
-        def gradient(pair):
-            pair_stats = stats[pair]
-            tiles = (2 * pair, 2 * pair + 1)
-            f = {}
-            for j in tiles:
-                f[j] = placed([P, SLOTS], F32, "f%d" % j, F_AT[j])
-                nc.vector.scalar_tensor_tensor(f[j][:], e[j][:], one[:], lk_rows[j][:], ALU.mult, ALU.mult,
-                                               accum_out=pair_stats[:, j % 2, 1:2])
-            inverse = keep.tile([P, 2, 2], F32, name="inverse%d" % pair)
-            nc.vector.reciprocal(inverse[:], pair_stats[:, :, 0:2])
-            factor = keep.tile([P, 2, 2], F32, name="factor%d" % pair)
-            nc.vector.tensor_tensor(factor[:], inverse[:], pair_stats[:, :, 1:3], ALU.mult)
-            difference = {}
-            for j in tiles:
-                difference[j] = keep.tile([P, SLOTS], F32, name="difference%d" % j)
-                nc.vector.scalar_tensor_tensor(difference[j][:], e[j][:], factor[:, j % 2, 0:1], f[j][:],
-                                               ALU.mult, ALU.subtract)
+        def exponentials(j):
+            nc.scalar.activation(e[j][:], z[j][:], ACT.Exp, bias=neg_max[j][:], scale=-1.0, accum_out=stats[j][:, 0:1])
+
+        def weigh(j):
+            nc.vector.scalar_tensor_tensor(f[j][:], e[j][:], one[:], lk_rows[j][:], ALU.mult, ALU.mult,
+                                           accum_out=stats[j][:, 1:2])
+
+        def invert(j):
+            nc.vector.reciprocal(inverse[j][:], stats[j][:, 0:2])
+
+        def make_factors(j):
+            nc.vector.tensor_tensor(factor[j][:], inverse[j][:], stats[j][:, 1:3], ALU.mult)
+
+        def subtract(j):
+            nc.vector.scalar_tensor_tensor(difference[j][:], e[j][:], factor[j][:, 0:1], f[j][:], ALU.mult, ALU.subtract)
+
+        def round_g(j, u):
+            by_four = difference[j][:].rearrange("r (p t) -> r p t", t=PACK)
             ts_by_four = ts_row[:].rearrange("r (p t) -> r p t", t=PACK)
-            for j in tiles:
-                by_four = difference[j][:].rearrange("r (p t) -> r p t", t=PACK)
-                bank = turn_ps.tile([P, PACK, P], F32, name="turn_bank")
-                for u in range(2):
-                    g_part = keep.tile([P, HALF], BF16, name="g%d_%d" % (j, u), align_bytes=64)
-                    nc.vector.scalar_tensor_tensor(g_part[:].rearrange("r (p v) -> r p v", v=2),
-                                                   by_four[:, :, 2 * u:2 * u + 2], factor[:, j % 2, 1:2],
-                                                   ts_by_four[:, :, 2 * u:2 * u + 2], ALU.mult, ALU.mult)
-                    nc.tensor.transpose(bank[:, u, :], g_part[:].bitcast(F32), ident[:])
-                nc.scalar.copy(g_grouped[j].bitcast(F32).rearrange("p (r u) -> p r u", u=2),
-                               bank[:, 0:2, :].rearrange("p u r -> p r u"))
+            if u == 0:
+                turned_g[j] = turn_ps.tile([P, PACK, P], F32, name="turn_bank")
+            nc.vector.scalar_tensor_tensor(g_words[u][j][:].rearrange("r (p v) -> r p v", v=2),
+                                           by_four[:, :, 2 * u:2 * u + 2], factor[j][:, 1:2],
+                                           ts_by_four[:, :, 2 * u:2 * u + 2], ALU.mult, ALU.mult)
+            nc.tensor.transpose(turned_g[j][:, u, :], g_words[u][j][:].bitcast(F32), ident[:])
 
-        def product(n):
-            group = PRODUCT_GROUPS[n]
-            g_codes = placed([P, len(group) * P], U32, "g_codes%d" % n, G_CODES_AT[n])
-            g_scales = keep.tile([P, len(group) * P], U8, name="g_scales%d" % n, align_bytes=64)
-            nc.vector.quantize_mx(out=g_codes[:].bitcast(E5M2X4), scales=g_scales[:], in_=g_group_tiles[n][:])
-            for k, j in enumerate(group):
-                cols = slice(k * P, (k + 1) * P)
-                sums = out_ps.tile([P, D], F32, name="sums")
-                nc.tensor.matmul_mx(out=sums[:], lhsT=g_codes[:, cols].bitcast(E5M2X4), lhsT_scale=g_scales[:, cols],
-                                    rhs=dt_codes[:].bitcast(E4M3X4), rhs_scale=dt_scales[:], start=True, stop=True)
-                staged = keep.tile([P, P, PACK], F32, name="staged%d" % j)
-                in_order = sums[:].rearrange("r (t q) -> r q t", t=PACK)
-                rows = slice(j * P, (j + 1) * P)
-                if j < ROW_TILES - 1:
-                    nc.scalar.copy(staged[:], in_order)
-                    nc.sync.dma_start(out[rows, :], staged[:].rearrange("r q t -> r (q t)"))
-                else:
-                    for half in range(2):
-                        qs = slice(half * P // 2, (half + 1) * P // 2)
-                        nc.vector.tensor_copy(staged[:, qs, :], in_order[:, qs, :])
-                        nc.sync.dma_start(out[rows, half * D // 2:(half + 1) * D // 2],
-                                          staged[:, qs, :].rearrange("r q t -> r (q t)"))
+        def group_g(j):
+            nc.scalar.copy(g_grouped[j][:].bitcast(F32).rearrange("p (r u) -> p r u", u=2),
+                           turned_g[j][:, 0:2, :].rearrange("p u r -> p r u"))
 
-        scores_by_rows(0, 2, score_ps, "score_bank")
-        scores_by_rows(1, 1, prep_ps, "prep_bank")
-        turn_planes_2_and_3()
-        scaled = scores_by_slots()
-        gradient(0)
-        turn_scores(scaled, 2)
-        turn_scores(scaled, 3)
-        gradient(1)
-        for n in range(len(PRODUCT_GROUPS)):
-            product(n)
+        def product(j):
+            nc.vector.quantize_mx(out=g_codes[j][:].bitcast(E5M2X4), scales=g_scales[j][:], in_=g_grouped[j][:])
+            sums[j] = out_ps.tile([P, D], F32, name="sums")
+            nc.tensor.matmul_mx(out=sums[j][:], lhsT=g_codes[j][:].bitcast(E5M2X4), lhsT_scale=g_scales[j][:],
+                                rhs=dt_codes[:].bitcast(E4M3X4), rhs_scale=dt_scales[:], start=True, stop=True)
+
+        def store(j):
+            in_order = sums[j][:].rearrange("r (t q) -> r q t", t=PACK)
+            rows = slice(j * P, (j + 1) * P)
+            if j < ROW_TILES - 1:
+                nc.scalar.copy(staged[j][:], in_order)
+                nc.sync.dma_start(out[rows, :], staged[j][:].rearrange("r q t -> r (q t)"))
+            else:
+                for half in range(2):
+                    qs = slice(half * P // 2, (half + 1) * P // 2)
+                    nc.vector.tensor_copy(staged[j][:, qs, :], in_order[:, qs, :])
+                    nc.sync.dma_start(out[rows, half * D // 2:(half + 1) * D // 2],
+                                      staged[j][:, qs, :].rearrange("r q t -> r (q t)"))
+
+        group_x(0)
+        group_x(1)
+        group_x(2)
+        group_x(3)
+        quantize_d(0)
+        quantize_x(0)
+        quantize_d(1)
+        quantize_x(1)
+        quantize_turned_planes(0)
+        score_half_by_rows(0, 0)
+        score_half_by_rows(0, 1)
+        row_minimum(0)
+        exponentials(0)
+        score_by_rows(1)
+        quantize_x(2)
+        row_minimum(1)
+        exponentials(1)
+        quantize_x(3)
+        score_by_slots(2)
+        turn_scores(2)
+        exponentials(2)
+        score_by_slots(3)
+        turn_scores(3)
+        exponentials(3)
+        weigh(0)
+        invert(0)
+        make_factors(0)
+        weigh(1)
+        invert(1)
+        make_factors(1)
+        subtract(0)
+        subtract(1)
+        turn_woven_plane(2)
+        turn_woven_plane(3)
+        round_g(0, 0)
+        round_g(0, 1)
+        group_g(0)
+        round_g(1, 0)
+        round_g(1, 1)
+        group_g(1)
+        quantize_turned_planes(1)
+        weigh(2)
+        invert(2)
+        make_factors(2)
+        weigh(3)
+        invert(3)
+        make_factors(3)
+        subtract(2)
+        product(0)
+        subtract(3)
+        product(1)
+        round_g(2, 0)
+        round_g(2, 1)
+        group_g(2)
+        round_g(3, 0)
+        round_g(3, 1)
+        group_g(3)
+        store(0)
+        product(2)
+        product(3)
+        store(1)
+        store(2)
+        store(3)

@@ -26,17 +26,28 @@ HALF = SLOTS // 2
 OFFSETS_PER_COLUMN = 16
 BANK_BLOCKS = 4
 
-X_SPANS = ((0, P), (P, 2 * P), (2 * P, R))
+X_SPANS = tuple((j * P, (j + 1) * P) for j in range(ROW_TILES))
 
 D_WINDOW_AT = (0, 8, 16, 32)
-X_RAW_AT = (8, 10, 12)
+X_RAW_AT = (8, 10, 12, 14)
 LK_AT = (16, 18, 20, 22)
 TS_WINDOW_AT = 24
 D_GROUPED_AT = 24
-Z_AT = (40, 42, 44, 46)
+Z_AT = (40, 42, 40, 42)
+SCALED_AT = (None, 56, 44, 46)
 D_CODES_AT = 8
-DT_CODES_AT = 10
-D_PLANE_AT = {2: 12, 3: 42}
+TS_ROW_AT = 0
+X_GROUPED_AT = (48, 49, 50, 51)
+DT_CODES_AT = 51
+D_PLANE_AT = {2: 28, 3: 46}
+DT_GROUPED_AT = (53, 12, 42)
+DT_GROUPS = ((0, 1), (2,), (3,))
+
+PLANE_BANK = (0, 1, 7, 4)
+SCORE_BANK = (None, 2, 3, 5)
+TURNED_SCORE_BANK = (None, 5, 0, 1)
+TURNED_G_BANK = (5, 6, 2, 0)
+PRODUCT_BANK = (3, 4, 7, 1)
 
 FLOPS = 2 * 2 * R * SLOTS * D
 BYTES = 4 * (D * R + D * DOCS + R * SLOTS + R * D + DOCS + 2 * R) + 2 * P * SLOTS // OFFSETS_PER_COLUMN
@@ -47,10 +58,10 @@ def tile_attend_grag_q_kernel(tc, xT, dT, us, ts, lk, wt, offs, out):
     with ExitStack() as ctx:
         keep = ctx.enter_context(tc.tile_pool(name="keep", bufs=1))
         reused = ctx.enter_context(tc.tile_pool(name="reused", bufs=1))
-        prep_ps = ctx.enter_context(tc.psum_pool(name="prep_ps", bufs=2))
-        score_ps = ctx.enter_context(tc.psum_pool(name="score_ps", bufs=2))
-        turn_ps = ctx.enter_context(tc.psum_pool(name="turn_ps", bufs=2))
-        out_ps = ctx.enter_context(tc.psum_pool(name="out_ps", bufs=2))
+        psum = ctx.enter_context(tc.psum_pool(name="psum", bufs=1))
+
+        def psum_bank(n, shape):
+            return psum.tile(shape, F32, name="bank%d" % n)
 
         def placed(shape, dtype, name, kib):
             return reused.tile(shape, dtype, name=name, align_bytes=64, offset=int(kib * 1024))
@@ -79,7 +90,7 @@ def tile_attend_grag_q_kernel(tc, xT, dT, us, ts, lk, wt, offs, out):
         ts_window = placed([P, DOCS], F32, "ts_window", TS_WINDOW_AT)
         ts_window_parts = ts_window[:].rearrange("m (p b c) -> m b p c", b=DOCS // P // BANK_BLOCKS, c=BANK_BLOCKS)
         for b in range(DOCS // P // BANK_BLOCKS):
-            bank = prep_ps.tile([P, BANK_BLOCKS, P], F32, name="prep_bank")
+            bank = psum_bank(b, [P, BANK_BLOCKS, P])
             for c in range(BANK_BLOCKS):
                 col = BANK_BLOCKS * b + c
                 nc.tensor.transpose(bank[:, c, :], ts_seed[:, col:col + 1].to_broadcast([P, P]), ident[:])
@@ -87,27 +98,31 @@ def tile_attend_grag_q_kernel(tc, xT, dT, us, ts, lk, wt, offs, out):
 
         dt_codes = placed([P, D], U32, "dt_codes", DT_CODES_AT)
         dt_scales = keep.tile([P, D], U8, name="dt_scales", align_bytes=64)
-        dt_grouped = [keep.tile([P, 2 * P * PACK], BF16, name="dt_grouped%d" % n, align_bytes=64) for n in range(2)]
+        dt_grouped = [placed([P, len(group) * P * PACK], BF16, "dt_grouped%d" % n, DT_GROUPED_AT[n])
+                      for n, group in enumerate(DT_GROUPS)]
 
         def quantize_turned_planes(n):
-            cols = slice(2 * n * P, (2 * n + 2) * P)
+            cols = slice(DT_GROUPS[n][0] * P, (DT_GROUPS[n][-1] + 1) * P)
             nc.vector.quantize_mx(out=dt_codes[:, cols].bitcast(E4M3X4), scales=dt_scales[:, cols], in_=dt_grouped[n][:])
 
-        def turn_plane(plane, t):
+        def turn_plane(plane, bank):
             words = plane.bitcast(F32)
-            grouped = dt_grouped[t // 2][:, t % 2 * P * PACK:(t % 2 + 1) * P * PACK]
-            bank = prep_ps.tile([P, BANK_BLOCKS, P], F32, name="prep_bank")
             for u in range(2):
                 nc.tensor.transpose(bank[:, u, :], words[:, u:HALF:2], ident[:])
+
+        def group_turned_plane(bank, t):
+            grouped = dt_grouped[max(t - 1, 0)][:, P * PACK:] if t == 1 else dt_grouped[max(t - 1, 0)][:, :P * PACK]
             nc.scalar.copy(grouped.bitcast(F32).rearrange("p (q u) -> p q u", u=2),
                            bank[:, 0:2, :].rearrange("p u q -> p q u"))
 
         d_planes01 = keep.tile([P, 2, SLOTS], BF16, name="d_planes01", align_bytes=64)
         nc.vector.tensor_copy(d_planes01[:, 0, :], d_window[0][:].indirect(offsets[:]))
-        ts_row = keep.tile([P, SLOTS], F32, name="ts_row")
+        ts_row = placed([P, SLOTS], F32, "ts_row", TS_ROW_AT)
         nc.vector.tensor_copy(ts_row[:], ts_window[:].indirect(offsets[:]))
         d_grouped = placed([P, SLOTS, PACK], BF16, "d_grouped", D_GROUPED_AT)
-        turn_plane(d_planes01[:, 0, :], 0)
+        bank = psum_bank(PLANE_BANK[0], [P, BANK_BLOCKS, P])
+        turn_plane(d_planes01[:, 0, :], bank)
+        group_turned_plane(bank, 0)
         nc.vector.tensor_copy(d_planes01[:, 1, :], d_window[1][:].indirect(offsets[:]))
         x_planes = xT.rearrange("(p t) r -> p t r", t=PACK)
         x_raw = []
@@ -115,20 +130,30 @@ def tile_attend_grag_q_kernel(tc, xT, dT, us, ts, lk, wt, offs, out):
             span = placed([P, PACK, end - first], F32, "x_raw%d" % n, X_RAW_AT[n])
             nc.sync.dma_start(span[:], x_planes[:, :, first:end])
             x_raw.extend(span[:, :, k:k + P] for k in range(0, end - first, P))
-        turn_plane(d_planes01[:, 1, :], 1)
+        bank = psum_bank(PLANE_BANK[1], [P, BANK_BLOCKS, P])
+        turn_plane(d_planes01[:, 1, :], bank)
+        group_turned_plane(bank, 1)
         nc.scalar.copy(d_grouped[:, :, 0:2], d_planes01[:].rearrange("p t i -> p i t"))
 
-        bank = prep_ps.tile([P, BANK_BLOCKS, P], F32, name="prep_bank")
+        bank = psum_bank(4, [P, BANK_BLOCKS, P])
         nc.tensor.transpose(bank[:, 0, :], uw_rows[:], ident[:])
         uw = keep.tile([P, 2 * ROW_TILES], F32, name="uw")
         nc.scalar.copy(uw[:], bank[:, 0, 0:2 * ROW_TILES])
         neg_us = keep.tile([P, ROW_TILES], F32, name="neg_us")
         nc.scalar.activation(neg_us[:], uw[:, 0:ROW_TILES], ACT.Copy, scale=-1.0)
         stats = [keep.tile([P, 3], F32, name="stats%d" % j) for j in range(ROW_TILES)]
-        for j in range(ROW_TILES):
+        for j in (2, 3):
             nc.scalar.activation(stats[j][:, 2:3], uw[:, ROW_TILES + j:ROW_TILES + j + 1], ACT.Copy,
                                  scale=uw[:, j:j + 1])
-        bank = prep_ps.tile([P, BANK_BLOCKS, P], F32, name="prep_bank")
+        signed_wu = keep.tile([P, 2, 2], F32, name="signed_wu")
+        nc.vector.tensor_tensor(signed_wu[:, :, 0], uw[:, 0:2], uw[:, ROW_TILES:ROW_TILES + 2], ALU.mult)
+        nc.vector.tensor_tensor(signed_wu[:, :, 1], neg_us[:, 0:2], uw[:, ROW_TILES:ROW_TILES + 2], ALU.mult)
+        bank = psum_bank(6, [P, BANK_BLOCKS, P])
+        for t in range(PACK):
+            nc.tensor.transpose(bank[:, t, :], ts_row[:, t:SLOTS:PACK], ident[:])
+        ts_places = keep.tile([P, PACK], F32, name="ts_places")
+        nc.scalar.copy(ts_places[:], bank[:, :, 0])
+        bank = psum_bank(5, [P, BANK_BLOCKS, P])
         for s in range(SLOT_TILES):
             nc.tensor.transpose(bank[:, s, :], ts_row[:, s * P:(s + 1) * P], ident[:])
         ts_col = keep.tile([P, SLOT_TILES], F32, name="ts_col")
@@ -137,12 +162,15 @@ def tile_attend_grag_q_kernel(tc, xT, dT, us, ts, lk, wt, offs, out):
         def turn_woven_plane(t):
             plane = placed([P, SLOTS], BF16, "d_plane%d" % t, D_PLANE_AT[t])
             nc.scalar.copy(plane[:], d_grouped[:, :, t])
-            turn_plane(plane[:], t)
+            bank = psum_bank(PLANE_BANK[t], [P, BANK_BLOCKS, P])
+            turn_plane(plane[:], bank)
+            return bank
 
         nc.vector.tensor_copy(d_grouped[:, :, 2], d_window[2][:].indirect(offsets[:]))
         lk_rows = [placed([P, SLOTS], F32, "lk_rows%d" % j, LK_AT[j]) for j in range(ROW_TILES)]
         for j in range(ROW_TILES):
             nc.sync.dma_start(lk_rows[j][:], lk[j * P:(j + 1) * P, :])
+        turned_plane2 = turn_woven_plane(2)
         half_columns = HALF // OFFSETS_PER_COLUMN
         for half in range(2):
             nc.vector.tensor_copy(d_grouped[:, half * HALF:(half + 1) * HALF, 3],
@@ -159,10 +187,10 @@ def tile_attend_grag_q_kernel(tc, xT, dT, us, ts, lk, wt, offs, out):
         def tiles(name, shape, dtype):
             return [keep.tile(shape, dtype, name="%s%d" % (name, j), align_bytes=64) for j in range(ROW_TILES)]
 
-        x_grouped = tiles("x_grouped", [P, P, PACK], BF16)
+        x_grouped = [placed([P, P, PACK], BF16, "x_grouped%d" % j, X_GROUPED_AT[j]) for j in range(ROW_TILES)]
         x_codes = tiles("x_codes", [P, P], U32)
         x_scales = tiles("x_scales", [P, P], U8)
-        scaled = tiles("scaled", [P, SLOT_TILES, P], F32)
+        scaled = {j: placed([P, SLOT_TILES, P], F32, "scaled%d" % j, SCALED_AT[j]) for j in (2, 3)}
         z = [placed([P, SLOTS], F32, "z%d" % j, Z_AT[j]) for j in range(ROW_TILES)]
         neg_max = tiles("neg_max", [P, 1], F32)
         e = tiles("e", [P, SLOTS], F32)
@@ -188,14 +216,14 @@ def tile_attend_grag_q_kernel(tc, xT, dT, us, ts, lk, wt, offs, out):
 
         def score_half_by_rows(j, half):
             cols = slice(half * HALF, (half + 1) * HALF)
-            a = score_ps.tile([P, HALF], F32, name="score_bank")
+            a = psum_bank(half, [P, HALF])
             nc.tensor.matmul_mx(out=a[:], lhsT=x_codes[j][:].bitcast(E4M3X4), lhsT_scale=x_scales[j][:],
                                 rhs=d_codes[:, cols].bitcast(E4M3X4), rhs_scale=d_scales[:, cols],
                                 start=True, stop=True)
             nc.vector.scalar_tensor_tensor(z[j][:, cols], a[:], neg_us[:, j:j + 1], ts_row[:, cols], ALU.mult, ALU.mult)
 
         def score_by_rows(j):
-            a = prep_ps.tile([P, SLOTS], F32, name="prep_bank")
+            a = psum_bank(SCORE_BANK[j], [P, SLOTS])
             nc.tensor.matmul_mx(out=a[:], lhsT=x_codes[j][:].bitcast(E4M3X4), lhsT_scale=x_scales[j][:],
                                 rhs=d_codes[:].bitcast(E4M3X4), rhs_scale=d_scales[:], start=True, stop=True)
             nc.vector.scalar_tensor_tensor(z[j][:], a[:], neg_us[:, j:j + 1], ts_row[:], ALU.mult, ALU.mult)
@@ -204,7 +232,7 @@ def tile_attend_grag_q_kernel(tc, xT, dT, us, ts, lk, wt, offs, out):
             nc.vector.tensor_reduce(neg_max[j][:], z[j][:], AX.X, ALU.min)
 
         def score_by_slots(j):
-            a = prep_ps.tile([P, SLOT_TILES, P], F32, name="prep_bank")
+            a = psum_bank(SCORE_BANK[j], [P, SLOT_TILES, P])
             for s in range(SLOT_TILES):
                 cols = slice(s * P, (s + 1) * P)
                 nc.tensor.matmul_mx(out=a[:, s, :], lhsT=d_codes[:, cols].bitcast(E4M3X4),
@@ -214,7 +242,7 @@ def tile_attend_grag_q_kernel(tc, xT, dT, us, ts, lk, wt, offs, out):
                 nc.scalar.activation(scaled[j][:, s, :], a[:, s, :], ACT.Copy, scale=ts_col[:, s:s + 1])
 
         def turn_scores(j):
-            ts_a = score_ps.tile([P, SLOTS], F32, name="score_bank")
+            ts_a = psum_bank(TURNED_SCORE_BANK[j], [P, SLOTS])
             for s in range(SLOT_TILES):
                 nc.tensor.transpose(ts_a[:, s * P:(s + 1) * P], scaled[j][:, s, :], ident[:])
             nc.vector.tensor_scalar(z[j][:], ts_a[:], neg_us[:, j:j + 1], None, ALU.mult, ALU.min, accum_out=neg_max[j][:])
@@ -239,11 +267,34 @@ def tile_attend_grag_q_kernel(tc, xT, dT, us, ts, lk, wt, offs, out):
             by_four = difference[j][:].rearrange("r (p t) -> r p t", t=PACK)
             ts_by_four = ts_row[:].rearrange("r (p t) -> r p t", t=PACK)
             if u == 0:
-                turned_g[j] = turn_ps.tile([P, PACK, P], F32, name="turn_bank")
+                turned_g[j] = psum_bank(TURNED_G_BANK[j], [P, PACK, P])
             nc.vector.scalar_tensor_tensor(g_words[u][j][:].rearrange("r (p v) -> r p v", v=2),
                                            by_four[:, :, 2 * u:2 * u + 2], factor[j][:, 1:2],
                                            ts_by_four[:, :, 2 * u:2 * u + 2], ALU.mult, ALU.mult)
             nc.tensor.transpose(turned_g[j][:, u, :], g_words[u][j][:].bitcast(F32), ident[:])
+
+        terms = [tiles("term%d_" % k, [P, PACK, P], F32) for k in range(2)]
+
+        def make_term_factors(j):
+            nc.vector.tensor_tensor(factor[j][:], inverse[j][:], signed_wu[:, j, :], ALU.mult)
+
+        def turn_term(j, k, engine):
+            dealt = terms[k][j][:].rearrange("r t (c m) -> r c t m", m=4)
+            source = (e, f)[k][j][:].rearrange("r (c m t) -> r c t m", m=4, t=PACK)
+            if engine == "scalar":
+                nc.scalar.activation(dealt, source, ACT.Copy, scale=factor[j][:, k:k + 1])
+            else:
+                nc.vector.tensor_scalar(dealt, source, factor[j][:, k:k + 1], None, ALU.mult)
+            if k == 0:
+                turned_g[j] = psum_bank(TURNED_G_BANK[j], [P, PACK, P])
+            for t in range(PACK):
+                nc.tensor.matmul(turned_g[j][:, t, :], terms[k][j][:, t, :], ident[:], is_transpose=True,
+                                 start=(k == 0 and t == 0), stop=(k == 1 and t == PACK - 1))
+
+        def round_turned_g(j):
+            nc.vector.tensor_tensor(g_grouped[j][:].rearrange("p (r t) -> p r t", t=PACK),
+                                    turned_g[j][:].rearrange("p t r -> p r t"),
+                                    ts_places[:].unsqueeze(1).to_broadcast([P, P, PACK]), ALU.mult)
 
         def group_g(j):
             nc.scalar.copy(g_grouped[j][:].bitcast(F32).rearrange("p (r u) -> p r u", u=2),
@@ -251,7 +302,7 @@ def tile_attend_grag_q_kernel(tc, xT, dT, us, ts, lk, wt, offs, out):
 
         def product(j):
             nc.vector.quantize_mx(out=g_codes[j][:].bitcast(E5M2X4), scales=g_scales[j][:], in_=g_grouped[j][:])
-            sums[j] = out_ps.tile([P, D], F32, name="sums")
+            sums[j] = psum_bank(PRODUCT_BANK[j], [P, D])
             nc.tensor.matmul_mx(out=sums[j][:], lhsT=g_codes[j][:].bitcast(E5M2X4), lhsT_scale=g_scales[j][:],
                                 rhs=dt_codes[:].bitcast(E4M3X4), rhs_scale=dt_scales[:], start=True, stop=True)
 
@@ -272,62 +323,62 @@ def tile_attend_grag_q_kernel(tc, xT, dT, us, ts, lk, wt, offs, out):
         group_x(1)
         group_x(2)
         group_x(3)
+        group_turned_plane(turned_plane2, 2)
         quantize_d(0)
         quantize_x(0)
         quantize_d(1)
         quantize_x(1)
-        quantize_turned_planes(0)
         score_half_by_rows(0, 0)
         score_half_by_rows(0, 1)
-        row_minimum(0)
-        exponentials(0)
-        score_by_rows(1)
         quantize_x(2)
-        row_minimum(1)
-        exponentials(1)
+        score_by_rows(1)
         quantize_x(3)
+        row_minimum(0)
+        row_minimum(1)
+        quantize_turned_planes(0)
         score_by_slots(2)
-        turn_scores(2)
-        exponentials(2)
+        exponentials(0)
         score_by_slots(3)
-        turn_scores(3)
-        exponentials(3)
+        exponentials(1)
         weigh(0)
+        turn_scores(2)
+        turn_scores(3)
+        exponentials(2)
+        exponentials(3)
+        turned_plane3 = turn_woven_plane(3)
+        group_turned_plane(turned_plane3, 3)
         invert(0)
-        make_factors(0)
         weigh(1)
+        make_term_factors(0)
         invert(1)
-        make_factors(1)
-        subtract(0)
-        subtract(1)
-        turn_woven_plane(2)
-        turn_woven_plane(3)
-        round_g(0, 0)
-        round_g(0, 1)
-        group_g(0)
-        round_g(1, 0)
-        round_g(1, 1)
-        group_g(1)
-        quantize_turned_planes(1)
         weigh(2)
-        invert(2)
-        make_factors(2)
+        make_term_factors(1)
         weigh(3)
+        turn_term(0, 0, "scalar")
+        turn_term(0, 1, "scalar")
+        turn_term(1, 0, "scalar")
+        turn_term(1, 1, "scalar")
+        invert(2)
+        quantize_turned_planes(1)
         invert(3)
+        make_factors(2)
         make_factors(3)
+        quantize_turned_planes(2)
         subtract(2)
-        product(0)
-        subtract(3)
-        product(1)
+        round_turned_g(0)
         round_g(2, 0)
         round_g(2, 1)
         group_g(2)
+        product(0)
+        subtract(3)
+        round_turned_g(1)
         round_g(3, 0)
         round_g(3, 1)
         group_g(3)
-        store(0)
         product(2)
+        product(1)
         product(3)
-        store(1)
+        store(0)
         store(2)
+        store(1)
         store(3)

@@ -28,27 +28,37 @@ BANK_BLOCKS = 4
 
 X_SPANS = tuple((j * P, (j + 1) * P) for j in range(ROW_TILES))
 
-D_WINDOW_AT = (0, 8, 16, 32)
-X_RAW_AT = (8, 10, 12, 14)
-LK_AT = (16, 18, 20, 22)
-TS_WINDOW_AT = 24
-D_GROUPED_AT = 24
-Z_AT = (40, 42, 40, 42)
-SCALED_AT = (None, 56, 44, 46)
-D_CODES_AT = 8
+D_WINDOW_AT = (0, 8, 18, 34)
+X_RAW_AT = (8.5, 10.5, 12.5, 14.5)
+LK_AT = (18, 20, 22, 24)
+TS_WINDOW_AT = 26
+D_GROUPED_AT = 26
+Z_AT = (42, 14, 42, 14)
+SCALED_AT = (None, None, 58, 44)
+D_PLANES01_AT = 60
+TS_COL_AT = 60
+TS_PLACES_AT = 52
+TERM_AT = ((62, 64, 70, 84), (68, 66, 72, 86))
+STAGED_AT = (74, 76, 78, 80)
+G_WORDS_AT = ((88, 89, 82, 83), (88.5, 89.5, 82.5, 83.5))
+D_CODES_AT = 8.5
 TS_ROW_AT = 0
-X_GROUPED_AT = (48, 49, 50, 51)
-DT_CODES_AT = 51
-D_PLANE_AT = {2: 28, 3: 46}
-DT_GROUPED_AT = (53, 12, 42)
+X_GROUPED_AT = (50, 51, 52, 53)
+DT_CODES_AT = 10.5
+D_PLANE_AT = {2: 30, 3: 16}
+DT_GROUPED_AT = (55, 12.5, 14)
 DT_GROUPS = ((0, 1), (2,), (3,))
 
-PLANE_BANK = (0, 1, 7, 4)
+BANK_BYTES = 2048
+PLANE_BANK = (0, 1, 7, 5)
 SCORE_BANK = (None, 2, 3, 5)
-TURNED_SCORE_BANK = (None, 5, 0, 1)
-TURNED_G_BANK = (5, 6, 2, 0)
+TURNED_SCORE_BANK = (None, None, 2, 1)
+TURNED_G_BANK = (4, 6, 0, 2)
 PRODUCT_BANK = (3, 4, 7, 1)
 
+ADDED = (0, 2,)
+PAIRED = (1, 3,)
+LAST = 3
 FLOPS = 2 * 2 * R * SLOTS * D
 BYTES = 4 * (D * R + D * DOCS + R * SLOTS + R * D + DOCS + 2 * R) + 2 * P * SLOTS // OFFSETS_PER_COLUMN
 
@@ -60,8 +70,11 @@ def tile_attend_grag_q_kernel(tc, xT, dT, us, ts, lk, wt, offs, out):
         reused = ctx.enter_context(tc.tile_pool(name="reused", bufs=1))
         psum = ctx.enter_context(tc.psum_pool(name="psum", bufs=1))
 
+        banks = []
+
         def psum_bank(n, shape):
-            return psum.tile(shape, F32, name="bank%d" % n)
+            banks.append(psum.tile(shape, F32, name="bank%d_%d" % (n, len(banks)), offset=n * BANK_BYTES))
+            return banks[-1]
 
         def placed(shape, dtype, name, kib):
             return reused.tile(shape, dtype, name=name, align_bytes=64, offset=int(kib * 1024))
@@ -115,7 +128,7 @@ def tile_attend_grag_q_kernel(tc, xT, dT, us, ts, lk, wt, offs, out):
             nc.scalar.copy(grouped.bitcast(F32).rearrange("p (q u) -> p q u", u=2),
                            bank[:, 0:2, :].rearrange("p u q -> p q u"))
 
-        d_planes01 = keep.tile([P, 2, SLOTS], BF16, name="d_planes01", align_bytes=64)
+        d_planes01 = placed([P, 2, SLOTS], BF16, "d_planes01", D_PLANES01_AT)
         nc.vector.tensor_copy(d_planes01[:, 0, :], d_window[0][:].indirect(offsets[:]))
         ts_row = placed([P, SLOTS], F32, "ts_row", TS_ROW_AT)
         nc.vector.tensor_copy(ts_row[:], ts_window[:].indirect(offsets[:]))
@@ -142,35 +155,41 @@ def tile_attend_grag_q_kernel(tc, xT, dT, us, ts, lk, wt, offs, out):
         neg_us = keep.tile([P, ROW_TILES], F32, name="neg_us")
         nc.scalar.activation(neg_us[:], uw[:, 0:ROW_TILES], ACT.Copy, scale=-1.0)
         stats = [keep.tile([P, 3], F32, name="stats%d" % j) for j in range(ROW_TILES)]
-        for j in (2, 3):
+        for j in PAIRED:
             nc.scalar.activation(stats[j][:, 2:3], uw[:, ROW_TILES + j:ROW_TILES + j + 1], ACT.Copy,
                                  scale=uw[:, j:j + 1])
-        signed_wu = keep.tile([P, 2, 2], F32, name="signed_wu")
-        nc.vector.tensor_tensor(signed_wu[:, :, 0], uw[:, 0:2], uw[:, ROW_TILES:ROW_TILES + 2], ALU.mult)
-        nc.vector.tensor_tensor(signed_wu[:, :, 1], neg_us[:, 0:2], uw[:, ROW_TILES:ROW_TILES + 2], ALU.mult)
-        bank = psum_bank(6, [P, BANK_BLOCKS, P])
-        for t in range(PACK):
-            nc.tensor.transpose(bank[:, t, :], ts_row[:, t:SLOTS:PACK], ident[:])
-        ts_places = keep.tile([P, PACK], F32, name="ts_places")
-        nc.scalar.copy(ts_places[:], bank[:, :, 0])
+        signed_wu = keep.tile([P, 4, 2], F32, name="signed_wu")
+        for j in ADDED:
+            for k, signed_us in enumerate((uw, neg_us)):
+                nc.scalar.activation(signed_wu[:, j, k:k + 1], uw[:, ROW_TILES + j:ROW_TILES + j + 1], ACT.Copy,
+                                     scale=signed_us[:, j:j + 1])
         bank = psum_bank(5, [P, BANK_BLOCKS, P])
         for s in range(SLOT_TILES):
             nc.tensor.transpose(bank[:, s, :], ts_row[:, s * P:(s + 1) * P], ident[:])
-        ts_col = keep.tile([P, SLOT_TILES], F32, name="ts_col")
+        ts_col = placed([P, SLOT_TILES], F32, "ts_col", TS_COL_AT)
         nc.scalar.copy(ts_col[:], bank[:, :, 0])
 
-        def turn_woven_plane(t):
-            plane = placed([P, SLOTS], BF16, "d_plane%d" % t, D_PLANE_AT[t])
-            nc.scalar.copy(plane[:], d_grouped[:, :, t])
-            bank = psum_bank(PLANE_BANK[t], [P, BANK_BLOCKS, P])
-            turn_plane(plane[:], bank)
-            return bank
+        woven_plane = {}
+        turned_plane = {}
+
+        def pick_plane(t):
+            woven_plane[t] = placed([P, SLOTS], BF16, "d_plane%d" % t, D_PLANE_AT[t])
+            nc.scalar.copy(woven_plane[t][:], d_grouped[:, :, t])
+
+        def turn_picked_plane(t):
+            turned_plane[t] = psum_bank(PLANE_BANK[t], [P, BANK_BLOCKS, P])
+            turn_plane(woven_plane[t][:], turned_plane[t])
 
         nc.vector.tensor_copy(d_grouped[:, :, 2], d_window[2][:].indirect(offsets[:]))
         lk_rows = [placed([P, SLOTS], F32, "lk_rows%d" % j, LK_AT[j]) for j in range(ROW_TILES)]
         for j in range(ROW_TILES):
             nc.sync.dma_start(lk_rows[j][:], lk[j * P:(j + 1) * P, :])
-        turned_plane2 = turn_woven_plane(2)
+        pick_plane(2)
+        turn_picked_plane(2)
+        ts_places_bank = psum_bank(6, [P, BANK_BLOCKS, P])
+        for t in range(PACK):
+            nc.tensor.transpose(ts_places_bank[:, t, :], ts_row[:, t:SLOTS:PACK], ident[:])
+        ts_places = placed([P, PACK], F32, "ts_places", TS_PLACES_AT)
         half_columns = HALF // OFFSETS_PER_COLUMN
         for half in range(2):
             nc.vector.tensor_copy(d_grouped[:, half * HALF:(half + 1) * HALF, 3],
@@ -198,11 +217,11 @@ def tile_attend_grag_q_kernel(tc, xT, dT, us, ts, lk, wt, offs, out):
         inverse = tiles("inverse", [P, 2], F32)
         factor = tiles("factor", [P, 2], F32)
         difference = tiles("difference", [P, SLOTS], F32)
-        g_words = [tiles("g_words%d_" % u, [P, HALF], BF16) for u in range(2)]
+        g_words = [{j: placed([P, HALF], BF16, "g_words%d_%d" % (u, j), G_WORDS_AT[u][j]) for j in range(4)} for u in range(2)]
         g_grouped = tiles("g_grouped", [P, P * PACK], BF16)
         g_codes = tiles("g_codes", [P, P], U32)
         g_scales = tiles("g_scales", [P, P], U8)
-        staged = tiles("staged", [P, P, PACK], F32)
+        staged = [placed([P, P, PACK], F32, "staged%d" % j, STAGED_AT[j]) for j in range(ROW_TILES)]
         turned_g = {}
         sums = {}
 
@@ -222,30 +241,40 @@ def tile_attend_grag_q_kernel(tc, xT, dT, us, ts, lk, wt, offs, out):
                                 start=True, stop=True)
             nc.vector.scalar_tensor_tensor(z[j][:, cols], a[:], neg_us[:, j:j + 1], ts_row[:, cols], ALU.mult, ALU.mult)
 
-        def score_by_rows(j):
-            a = psum_bank(SCORE_BANK[j], [P, SLOTS])
-            nc.tensor.matmul_mx(out=a[:], lhsT=x_codes[j][:].bitcast(E4M3X4), lhsT_scale=x_scales[j][:],
-                                rhs=d_codes[:].bitcast(E4M3X4), rhs_scale=d_scales[:], start=True, stop=True)
-            nc.vector.scalar_tensor_tensor(z[j][:], a[:], neg_us[:, j:j + 1], ts_row[:], ALU.mult, ALU.mult)
-
         def row_minimum(j):
             nc.vector.tensor_reduce(neg_max[j][:], z[j][:], AX.X, ALU.min)
 
+        scores = {}
+        turned_scores = {}
+
+        def score_by_rows(j):
+            scores[j] = psum_bank(SCORE_BANK[j], [P, SLOTS])
+            nc.tensor.matmul_mx(out=scores[j][:], lhsT=x_codes[j][:].bitcast(E4M3X4), lhsT_scale=x_scales[j][:],
+                                rhs=d_codes[:].bitcast(E4M3X4), rhs_scale=d_scales[:], start=True, stop=True)
+
+        def scale_by_rows(j):
+            nc.vector.scalar_tensor_tensor(z[j][:], scores[j][:], neg_us[:, j:j + 1], ts_row[:], ALU.mult, ALU.mult)
+
         def score_by_slots(j):
-            a = psum_bank(SCORE_BANK[j], [P, SLOT_TILES, P])
+            scores[j] = psum_bank(SCORE_BANK[j], [P, SLOT_TILES, P])
             for s in range(SLOT_TILES):
                 cols = slice(s * P, (s + 1) * P)
-                nc.tensor.matmul_mx(out=a[:, s, :], lhsT=d_codes[:, cols].bitcast(E4M3X4),
+                nc.tensor.matmul_mx(out=scores[j][:, s, :], lhsT=d_codes[:, cols].bitcast(E4M3X4),
                                     lhsT_scale=d_scales[:, cols], rhs=x_codes[j][:].bitcast(E4M3X4),
                                     rhs_scale=x_scales[j][:], start=True, stop=True)
+
+        def scale_by_slots(j):
             for s in range(SLOT_TILES):
-                nc.scalar.activation(scaled[j][:, s, :], a[:, s, :], ACT.Copy, scale=ts_col[:, s:s + 1])
+                nc.scalar.activation(scaled[j][:, s, :], scores[j][:, s, :], ACT.Copy, scale=ts_col[:, s:s + 1])
 
         def turn_scores(j):
-            ts_a = psum_bank(TURNED_SCORE_BANK[j], [P, SLOTS])
+            turned_scores[j] = psum_bank(TURNED_SCORE_BANK[j], [P, SLOTS])
             for s in range(SLOT_TILES):
-                nc.tensor.transpose(ts_a[:, s * P:(s + 1) * P], scaled[j][:, s, :], ident[:])
-            nc.vector.tensor_scalar(z[j][:], ts_a[:], neg_us[:, j:j + 1], None, ALU.mult, ALU.min, accum_out=neg_max[j][:])
+                nc.tensor.transpose(turned_scores[j][:, s * P:(s + 1) * P], scaled[j][:, s, :], ident[:])
+
+        def scale_turned_scores(j):
+            nc.vector.tensor_scalar(z[j][:], turned_scores[j][:], neg_us[:, j:j + 1], None, ALU.mult, ALU.min,
+                                    accum_out=neg_max[j][:])
 
         def exponentials(j):
             nc.scalar.activation(e[j][:], z[j][:], ACT.Exp, bias=neg_max[j][:], scale=-1.0, accum_out=stats[j][:, 0:1])
@@ -266,25 +295,35 @@ def tile_attend_grag_q_kernel(tc, xT, dT, us, ts, lk, wt, offs, out):
         def round_g(j, u):
             by_four = difference[j][:].rearrange("r (p t) -> r p t", t=PACK)
             ts_by_four = ts_row[:].rearrange("r (p t) -> r p t", t=PACK)
-            if u == 0:
-                turned_g[j] = psum_bank(TURNED_G_BANK[j], [P, PACK, P])
             nc.vector.scalar_tensor_tensor(g_words[u][j][:].rearrange("r (p v) -> r p v", v=2),
                                            by_four[:, :, 2 * u:2 * u + 2], factor[j][:, 1:2],
                                            ts_by_four[:, :, 2 * u:2 * u + 2], ALU.mult, ALU.mult)
+
+        def turn_g(j, u):
+            if u == 0:
+                turned_g[j] = psum_bank(TURNED_G_BANK[j], [P, PACK, P])
             nc.tensor.transpose(turned_g[j][:, u, :], g_words[u][j][:].bitcast(F32), ident[:])
 
-        terms = [tiles("term%d_" % k, [P, PACK, P], F32) for k in range(2)]
+        terms = [[placed([P, PACK, P], F32, "term%d_%d" % (k, j), TERM_AT[k][j]) for j in range(4)] for k in range(2)]
 
         def make_term_factors(j):
             nc.vector.tensor_tensor(factor[j][:], inverse[j][:], signed_wu[:, j, :], ALU.mult)
 
-        def turn_term(j, k, engine):
-            dealt = terms[k][j][:].rearrange("r t (c m) -> r c t m", m=4)
-            source = (e, f)[k][j][:].rearrange("r (c m t) -> r c t m", m=4, t=PACK)
+        def invert_sum(j, k):
+            nc.vector.reciprocal(inverse[j][:, k:k + 1], stats[j][:, k:k + 1])
+
+        def make_term_factor(j, k):
+            nc.scalar.activation(factor[j][:, k:k + 1], signed_wu[:, j, k:k + 1], ACT.Copy, scale=inverse[j][:, k:k + 1])
+
+        def scale_term(j, k, engine):
+            dealt = terms[k][j][:].rearrange("r t p -> r p t")
+            source = (e, f)[k][j][:].rearrange("r (p t) -> r p t", t=PACK)
             if engine == "scalar":
                 nc.scalar.activation(dealt, source, ACT.Copy, scale=factor[j][:, k:k + 1])
             else:
                 nc.vector.tensor_scalar(dealt, source, factor[j][:, k:k + 1], None, ALU.mult)
+
+        def turn_term(j, k):
             if k == 0:
                 turned_g[j] = psum_bank(TURNED_G_BANK[j], [P, PACK, P])
             for t in range(PACK):
@@ -300,8 +339,10 @@ def tile_attend_grag_q_kernel(tc, xT, dT, us, ts, lk, wt, offs, out):
             nc.scalar.copy(g_grouped[j][:].bitcast(F32).rearrange("p (r u) -> p r u", u=2),
                            turned_g[j][:, 0:2, :].rearrange("p u r -> p r u"))
 
-        def product(j):
+        def quantize_g(j):
             nc.vector.quantize_mx(out=g_codes[j][:].bitcast(E5M2X4), scales=g_scales[j][:], in_=g_grouped[j][:])
+
+        def product(j):
             sums[j] = psum_bank(PRODUCT_BANK[j], [P, D])
             nc.tensor.matmul_mx(out=sums[j][:], lhsT=g_codes[j][:].bitcast(E5M2X4), lhsT_scale=g_scales[j][:],
                                 rhs=dt_codes[:].bitcast(E4M3X4), rhs_scale=dt_scales[:], start=True, stop=True)
@@ -309,7 +350,7 @@ def tile_attend_grag_q_kernel(tc, xT, dT, us, ts, lk, wt, offs, out):
         def store(j):
             in_order = sums[j][:].rearrange("r (t q) -> r q t", t=PACK)
             rows = slice(j * P, (j + 1) * P)
-            if j < ROW_TILES - 1:
+            if j != LAST:
                 nc.scalar.copy(staged[j][:], in_order)
                 nc.sync.dma_start(out[rows, :], staged[j][:].rearrange("r q t -> r (q t)"))
             else:
@@ -320,65 +361,88 @@ def tile_attend_grag_q_kernel(tc, xT, dT, us, ts, lk, wt, offs, out):
                                       staged[j][:, qs, :].rearrange("r q t -> r (q t)"))
 
         group_x(0)
-        group_x(1)
-        group_x(2)
-        group_x(3)
-        group_turned_plane(turned_plane2, 2)
         quantize_d(0)
         quantize_x(0)
         quantize_d(1)
+        group_x(1)
         quantize_x(1)
+        quantize_turned_planes(0)
         score_half_by_rows(0, 0)
         score_half_by_rows(0, 1)
-        quantize_x(2)
         score_by_rows(1)
-        quantize_x(3)
-        row_minimum(0)
-        row_minimum(1)
-        quantize_turned_planes(0)
+        group_x(2)
+        quantize_x(2)
         score_by_slots(2)
-        exponentials(0)
+        row_minimum(0)
+        group_x(3)
+        group_turned_plane(turned_plane[2], 2)
+        nc.scalar.copy(ts_places[:], ts_places_bank[:, :, 0])
+        pick_plane(3)
+        quantize_x(3)
         score_by_slots(3)
-        exponentials(1)
-        weigh(0)
+        scale_by_rows(1)
+        exponentials(0)
+        scale_by_slots(2)
         turn_scores(2)
+        scale_by_slots(3)
         turn_scores(3)
-        exponentials(2)
-        exponentials(3)
-        turned_plane3 = turn_woven_plane(3)
-        group_turned_plane(turned_plane3, 3)
-        invert(0)
-        weigh(1)
-        make_term_factors(0)
-        invert(1)
-        weigh(2)
-        make_term_factors(1)
-        weigh(3)
-        turn_term(0, 0, "scalar")
-        turn_term(0, 1, "scalar")
-        turn_term(1, 0, "scalar")
-        turn_term(1, 1, "scalar")
-        invert(2)
+        turn_picked_plane(3)
         quantize_turned_planes(1)
+        row_minimum(1)
+        invert_sum(0, 0)
+        weigh(0)
+        make_term_factor(0, 0)
+        exponentials(1)
+        invert_sum(0, 1)
+        scale_turned_scores(2)
+        scale_term(0, 0, "scalar")
+        turn_term(0, 0)
+        make_term_factor(0, 1)
+        scale_turned_scores(3)
+        exponentials(2)
+        weigh(1)
+        invert_sum(2, 0)
+        exponentials(3)
+        make_term_factor(2, 0)
+        scale_term(0, 1, "scalar")
+        turn_term(0, 1)
+        weigh(2)
+        invert(1)
+        weigh(3)
+        scale_term(2, 0, "scalar")
+        turn_term(2, 0)
+        make_factors(1)
+        invert_sum(2, 1)
+        make_term_factor(2, 1)
+        group_turned_plane(turned_plane[3], 3)
+        subtract(1)
         invert(3)
-        make_factors(2)
-        make_factors(3)
-        quantize_turned_planes(2)
-        subtract(2)
+        scale_term(2, 1, "scalar")
+        turn_term(2, 1)
         round_turned_g(0)
-        round_g(2, 0)
-        round_g(2, 1)
-        group_g(2)
+        make_factors(3)
+        round_g(1, 0)
+        turn_g(1, 0)
+        round_g(1, 1)
+        turn_g(1, 1)
+        quantize_turned_planes(2)
+        quantize_g(0)
         product(0)
+        group_g(1)
         subtract(3)
-        round_turned_g(1)
+        round_turned_g(2)
         round_g(3, 0)
+        turn_g(3, 0)
         round_g(3, 1)
-        group_g(3)
-        product(2)
-        product(1)
-        product(3)
+        turn_g(3, 1)
         store(0)
-        store(2)
+        quantize_g(1)
+        product(1)
+        group_g(3)
+        quantize_g(2)
+        product(2)
+        quantize_g(3)
+        product(3)
         store(1)
+        store(2)
         store(3)

@@ -331,9 +331,9 @@ def tile_attend_grag_q_kernel(tc, xT, dT, us, ts, lk, wt, offs, out):
                                  start=(k == 0 and t == 0), stop=(k == 1 and t == PACK - 1))
 
         def round_turned_g(j):
-            nc.vector.tensor_tensor(g_grouped[j][:].rearrange("p (r t) -> p r t", t=PACK),
-                                    turned_g[j][:].rearrange("p t r -> p r t"),
-                                    ts_places[:].unsqueeze(1).to_broadcast([P, P, PACK]), ALU.mult)
+            nc.vector.tensor_tensor(g_grouped[j][:].rearrange("p (c m t) -> p c t m", m=2, t=PACK),
+                                    turned_g[j][:].rearrange("p t (c m) -> p c t m", m=2),
+                                    ts_places[:].unsqueeze(1).unsqueeze(3).to_broadcast([P, P // 2, PACK, 2]), ALU.mult)
 
         def group_g(j):
             nc.scalar.copy(g_grouped[j][:].bitcast(F32).rearrange("p (r u) -> p r u", u=2),

@@ -125,8 +125,8 @@ def tile_attend_grag_q_kernel(tc, xT, dT, us, ts, lk, wt, offs, out):
 
         def group_turned_plane(bank, t):
             grouped = dt_grouped[max(t - 1, 0)][:, P * PACK:] if t == 1 else dt_grouped[max(t - 1, 0)][:, :P * PACK]
-            nc.scalar.copy(grouped.bitcast(F32).rearrange("p (q u) -> p q u", u=2),
-                           bank[:, 0:2, :].rearrange("p u q -> p q u"))
+            nc.scalar.copy(grouped.bitcast(F32).rearrange("p (c m u) -> p c u m", m=2, u=2),
+                           bank[:, 0:2, :].rearrange("p u (c m) -> p c u m", m=2))
 
         d_planes01 = placed([P, 2, SLOTS], BF16, "d_planes01", D_PLANES01_AT)
         nc.vector.tensor_copy(d_planes01[:, 0, :], d_window[0][:].indirect(offsets[:]))
@@ -316,8 +316,8 @@ def tile_attend_grag_q_kernel(tc, xT, dT, us, ts, lk, wt, offs, out):
             nc.scalar.activation(factor[j][:, k:k + 1], signed_wu[:, j, k:k + 1], ACT.Copy, scale=inverse[j][:, k:k + 1])
 
         def scale_term(j, k, engine):
-            dealt = terms[k][j][:].rearrange("r t p -> r p t")
-            source = (e, f)[k][j][:].rearrange("r (p t) -> r p t", t=PACK)
+            dealt = terms[k][j][:].rearrange("r t (c m) -> r c t m", m=2)
+            source = (e, f)[k][j][:].rearrange("r (c m t) -> r c t m", m=2, t=PACK)
             if engine == "scalar":
                 nc.scalar.activation(dealt, source, ACT.Copy, scale=factor[j][:, k:k + 1])
             else:
@@ -336,8 +336,8 @@ def tile_attend_grag_q_kernel(tc, xT, dT, us, ts, lk, wt, offs, out):
                                     ts_places[:].unsqueeze(1).unsqueeze(3).to_broadcast([P, P // 2, PACK, 2]), ALU.mult)
 
         def group_g(j):
-            nc.scalar.copy(g_grouped[j][:].bitcast(F32).rearrange("p (r u) -> p r u", u=2),
-                           turned_g[j][:, 0:2, :].rearrange("p u r -> p r u"))
+            nc.scalar.copy(g_grouped[j][:].bitcast(F32).rearrange("p (c m u) -> p c u m", m=2, u=2),
+                           turned_g[j][:, 0:2, :].rearrange("p u (c m) -> p c u m", m=2))
 
         def quantize_g(j):
             nc.vector.quantize_mx(out=g_codes[j][:].bitcast(E5M2X4), scales=g_scales[j][:], in_=g_grouped[j][:])
@@ -348,15 +348,17 @@ def tile_attend_grag_q_kernel(tc, xT, dT, us, ts, lk, wt, offs, out):
                                 rhs=dt_codes[:].bitcast(E4M3X4), rhs_scale=dt_scales[:], start=True, stop=True)
 
         def store(j):
-            in_order = sums[j][:].rearrange("r (t q) -> r q t", t=PACK)
+            in_order = sums[j][:].rearrange("r (t c m) -> r c t m", t=PACK, m=2)
+            in_pairs = staged[j][:].rearrange("r (c m) t -> r c t m", m=2)
             rows = slice(j * P, (j + 1) * P)
             if j != LAST:
-                nc.scalar.copy(staged[j][:], in_order)
+                nc.scalar.copy(in_pairs, in_order)
                 nc.sync.dma_start(out[rows, :], staged[j][:].rearrange("r q t -> r (q t)"))
             else:
                 for half in range(2):
                     qs = slice(half * P // 2, (half + 1) * P // 2)
-                    nc.vector.tensor_copy(staged[j][:, qs, :], in_order[:, qs, :])
+                    cs = slice(half * P // 4, (half + 1) * P // 4)
+                    nc.vector.tensor_copy(in_pairs[:, cs], in_order[:, cs])
                     nc.sync.dma_start(out[rows, half * D // 2:(half + 1) * D // 2],
                                       staged[j][:, qs, :].rearrange("r q t -> r (q t)"))
 

@@ -82,13 +82,14 @@ def tile_attend_grag_q_kernel(tc, xT, dT, us, ts, lk, wt, offs, out):
         offsets = keep.tile([P, SLOTS // OFFSETS_PER_COLUMN], U16, name="offsets")
         d_planes = dT.rearrange("(p t) n -> t p n", t=PACK)
         d_window = [placed([P, DOCS], F32, "d_window%d" % t, D_WINDOW_AT[t]) for t in range(PACK)]
-        ts_seed = keep.tile([P, DOCS // P], F32, name="ts_seed")
+        ts_window = keep.tile([P, DOCS], F32, name="ts_window")
+        nc.vector.memset(ts_window[0:P - 1, :], 0.0)
         uw_rows = keep.tile([P, P], F32, name="uw_rows")
         nc.gpsimd.memset(uw_rows[:], 0.0)
 
-        nc.sync.dma_start(ts_seed[:], ts[0].rearrange("(p c) -> p c", p=P))
-        nc.sync.dma_start(d_window[0][:], d_planes[0])
         nc.sync.dma_start(offsets[:], offs)
+        nc.sync.dma_start(ts_window[P - 1:P, :], ts[0:1, :])
+        nc.sync.dma_start(d_window[0][:], d_planes[0])
         nc.sync.dma_start(uw_rows[0:ROW_TILES, :], us.rearrange("(j p) o -> j (p o)", p=P))
         nc.sync.dma_start(uw_rows[ROW_TILES:2 * ROW_TILES, :], wt.rearrange("(j p) o -> j (p o)", p=P))
         for t in range(1, PACK):
@@ -99,15 +100,6 @@ def tile_attend_grag_q_kernel(tc, xT, dT, us, ts, lk, wt, offs, out):
 
         one = keep.tile([P, 1], F32, name="one")
         nc.scalar.activation(one[:], ident[:, 0:1], ACT.Exp, scale=0.0)
-
-        ts_window = placed([P, DOCS], F32, "ts_window", TS_WINDOW_AT)
-        ts_window_parts = ts_window[:].rearrange("m (p b c) -> m b p c", b=DOCS // P // BANK_BLOCKS, c=BANK_BLOCKS)
-        for b in range(DOCS // P // BANK_BLOCKS):
-            bank = psum_bank(b, [P, BANK_BLOCKS, P])
-            for c in range(BANK_BLOCKS):
-                col = BANK_BLOCKS * b + c
-                nc.tensor.transpose(bank[:, c, :], ts_seed[:, col:col + 1].to_broadcast([P, P]), ident[:])
-            nc.scalar.activation(ts_window_parts[:, b], bank[:].rearrange("m c p -> m p c"), ACT.Copy)
 
         dt_codes = placed([P, D], U32, "dt_codes", DT_CODES_AT)
         dt_scales = keep.tile([P, D], U8, name="dt_scales", align_bytes=64)
@@ -128,11 +120,26 @@ def tile_attend_grag_q_kernel(tc, xT, dT, us, ts, lk, wt, offs, out):
             nc.scalar.copy(grouped.bitcast(F32).rearrange("p (c m u) -> p c u m", m=2, u=2),
                            bank[:, 0:2, :].rearrange("p u (c m) -> p c u m", m=2))
 
+        ts_listed = keep.tile([P, SLOTS], F32, name="ts_listed")
+        nc.vector.tensor_copy(ts_listed[:], ts_window[:].indirect(offsets[:]))
+        bank = psum_bank(5, [P, BANK_BLOCKS, P])
+        for s in range(SLOT_TILES):
+            nc.tensor.transpose(bank[:, s, :], ts_listed[:, s * P:(s + 1) * P], ident[:])
+        ts_col = keep.tile([P, SLOT_TILES], F32, name="ts_col")
+        nc.scalar.copy(ts_col[:], bank[:, :, P - 1])
+        bank = psum_bank(2, [P, SLOT_TILES, P])
+        for s in range(SLOT_TILES):
+            nc.tensor.transpose(bank[:, s, :], ts_col[:, s:s + 1].to_broadcast([P, P]), ident[:])
+        ts_row = keep.tile([P, SLOTS], F32, name="ts_row")
+        nc.scalar.copy(ts_row[:], bank[:].rearrange("m s p -> m (s p)"))
+        ts_places_bank = psum_bank(5, [P, BANK_BLOCKS, P])
+        for t in range(PACK):
+            nc.tensor.transpose(ts_places_bank[:, t, :], ts_listed[:, t:SLOTS:PACK], ident[:])
+        ts_places = keep.tile([P, PACK], F32, name="ts_places")
+        nc.scalar.copy(ts_places[:], ts_places_bank[:, :, P - 1])
         d_planes01 = placed([P, 2, SLOTS], BF16, "d_planes01", D_PLANES01_AT)
         nc.vector.tensor_copy(d_planes01[:, 0, :], d_window[0][:].indirect(offsets[:]))
-        ts_row = placed([P, SLOTS], F32, "ts_row", TS_ROW_AT)
-        nc.vector.tensor_copy(ts_row[:], ts_window[:].indirect(offsets[:]))
-        d_grouped = placed([P, SLOTS, PACK], BF16, "d_grouped", D_GROUPED_AT)
+        d_grouped = keep.tile([P, SLOTS, PACK], BF16, name="d_grouped", align_bytes=64)
         bank = psum_bank(PLANE_BANK[0], [P, BANK_BLOCKS, P])
         turn_plane(d_planes01[:, 0, :], bank)
         group_turned_plane(bank, 0)
@@ -163,11 +170,6 @@ def tile_attend_grag_q_kernel(tc, xT, dT, us, ts, lk, wt, offs, out):
             for k, signed_us in enumerate((uw, neg_us)):
                 nc.scalar.activation(signed_wu[:, j, k:k + 1], uw[:, ROW_TILES + j:ROW_TILES + j + 1], ACT.Copy,
                                      scale=signed_us[:, j:j + 1])
-        bank = psum_bank(5, [P, BANK_BLOCKS, P])
-        for s in range(SLOT_TILES):
-            nc.tensor.transpose(bank[:, s, :], ts_row[:, s * P:(s + 1) * P], ident[:])
-        ts_col = placed([P, SLOT_TILES], F32, "ts_col", TS_COL_AT)
-        nc.scalar.copy(ts_col[:], bank[:, :, 0])
 
         woven_plane = {}
         turned_plane = {}
@@ -186,10 +188,6 @@ def tile_attend_grag_q_kernel(tc, xT, dT, us, ts, lk, wt, offs, out):
             nc.sync.dma_start(lk_rows[j][:], lk[j * P:(j + 1) * P, :])
         pick_plane(2)
         turn_picked_plane(2)
-        ts_places_bank = psum_bank(6, [P, BANK_BLOCKS, P])
-        for t in range(PACK):
-            nc.tensor.transpose(ts_places_bank[:, t, :], ts_row[:, t:SLOTS:PACK], ident[:])
-        ts_places = placed([P, PACK], F32, "ts_places", TS_PLACES_AT)
         half_columns = HALF // OFFSETS_PER_COLUMN
         for half in range(2):
             nc.vector.tensor_copy(d_grouped[:, half * HALF:(half + 1) * HALF, 3],
@@ -378,7 +376,6 @@ def tile_attend_grag_q_kernel(tc, xT, dT, us, ts, lk, wt, offs, out):
         row_minimum(0)
         group_x(3)
         group_turned_plane(turned_plane[2], 2)
-        nc.scalar.copy(ts_places[:], ts_places_bank[:, :, 0])
         pick_plane(3)
         quantize_x(3)
         score_by_slots(3)

@@ -56,6 +56,7 @@ TURNED_SCORE_BANK = (None, None, 2, 1)
 TURNED_G_BANK = (4, 6, 0, 2)
 PRODUCT_BANK = (3, 4, 7, 1)
 
+WARM_UP_BANK = 5
 ADDED = (0, 2,)
 PAIRED = (1, 3,)
 LAST = 3
@@ -345,6 +346,11 @@ def tile_attend_grag_q_kernel(tc, xT, dT, us, ts, lk, wt, offs, out):
             nc.tensor.matmul_mx(out=sums[j][:], lhsT=g_codes[j][:].bitcast(E5M2X4), lhsT_scale=g_scales[j][:],
                                 rhs=dt_codes[:].bitcast(E4M3X4), rhs_scale=dt_scales[:], start=True, stop=True)
 
+        def warm_up(j):
+            nc.tensor.matmul_mx(out=psum_bank(WARM_UP_BANK, [P, D])[:], lhsT=g_codes[j][:].bitcast(E5M2X4),
+                                lhsT_scale=g_scales[j][:], rhs=dt_codes[:].bitcast(E4M3X4), rhs_scale=dt_scales[:],
+                                start=True, stop=True)
+
         def store(j):
             in_order = sums[j][:].rearrange("r (t c m) -> r c t m", t=PACK, m=2)
             in_pairs = staged[j][:].rearrange("r (c m) t -> r c t m", m=2)
@@ -427,6 +433,7 @@ def tile_attend_grag_q_kernel(tc, xT, dT, us, ts, lk, wt, offs, out):
         quantize_turned_planes(2)
         quantize_g(0)
         product(0)
+        warm_up(0)
         group_g(1)
         subtract(3)
         round_turned_g(2)

@@ -26,40 +26,39 @@ HALF = SLOTS // 2
 OFFSETS_PER_COLUMN = 16
 BANK_BLOCKS = 4
 
-X_SPANS = tuple((j * P, (j + 1) * P) for j in range(ROW_TILES))
-
-D_WINDOW_AT = (0, 8, 18, 34)
-X_RAW_AT = (8.5, 10.5, 12.5, 14.5)
-LK_AT = (18, 20, 22, 24)
-TS_WINDOW_AT = 26
-D_GROUPED_AT = 26
-Z_AT = (42, 14, 42, 14)
-SCALED_AT = (None, None, 58, 44)
-D_PLANES01_AT = 60
-TS_COL_AT = 60
-TS_PLACES_AT = 52
-TERM_AT = ((62, 64, 70, 84), (68, 66, 72, 86))
-STAGED_AT = (74, 76, 78, 80)
-G_WORDS_AT = ((88, 89, 82, 83), (88.5, 89.5, 82.5, 83.5))
-D_CODES_AT = 8.5
-TS_ROW_AT = 0
-X_GROUPED_AT = (50, 51, 52, 53)
-DT_CODES_AT = 10.5
-D_PLANE_AT = {2: 30, 3: 16}
-DT_GROUPED_AT = (55, 12.5, 14)
-DT_GROUPS = ((0, 1), (2,), (3,))
-
 BANK_BYTES = 2048
+KIB = 1024
+
+ADDED = (0, 2)
+PAIRED = (1, 3)
+BY_SLOTS = (2, 3)
+LAST = 3
+COPIED_BY_VECTOR = 1
+TURNED_GROUPS = ((0, 1), (2,), (3,))
+
+WINDOW1_AT = 0
+X_RAW_AT = (0, 2, 4, 6)
+D_CODES_AT = 0
+DT_CODES_AT = 2
+TURNED_PLANE2_AT = 4
+NEG_Z13_AT = 5.5
+PLANE3_AT = 7.5
+TURNED_PLANE3_AT = 5.5
+WINDOW2_AT = 9
+LK_AT = (9, 11, 13, 15)
+NEG_Z02_AT = 17
+LAST_WORDS_AT = 19
+STAGED2_AT = 19
+
+TS_COL_BANK, TS_ROW_BANK, TS_PLACES_BANK, UW_BANK = 5, 2, 5, 4
 PLANE_BANK = (0, 1, 7, 5)
-SCORE_BANK = (None, 2, 3, 5)
-TURNED_SCORE_BANK = (None, None, 2, 1)
+FIRST_SCORE_BANK = (0, 1)
+SCORE_BANK = {1: 2, 2: 3, 3: 5}
+TURNED_SCORE_BANK = {2: 2, 3: 1}
 TURNED_G_BANK = (4, 6, 0, 2)
 PRODUCT_BANK = (3, 4, 7, 1)
-
 WARM_UP_BANK = 5
-ADDED = (0, 2,)
-PAIRED = (1, 3,)
-LAST = 3
+
 FLOPS = 2 * 2 * R * SLOTS * D
 BYTES = 4 * (D * R + D * DOCS + R * SLOTS + R * D + DOCS + 2 * R) + 2 * P * SLOTS // OFFSETS_PER_COLUMN
 
@@ -71,18 +70,20 @@ def tile_attend_grag_q_kernel(tc, xT, dT, us, ts, lk, wt, offs, out):
         reused = ctx.enter_context(tc.tile_pool(name="reused", bufs=1))
         psum = ctx.enter_context(tc.psum_pool(name="psum", bufs=1))
 
-        banks = []
-
-        def psum_bank(n, shape):
-            banks.append(psum.tile(shape, F32, name="bank%d_%d" % (n, len(banks)), offset=n * BANK_BYTES))
-            return banks[-1]
+        def psum_bank(name, n, shape):
+            return psum.tile(shape, F32, name=name, offset=n * BANK_BYTES)
 
         def placed(shape, dtype, name, kib):
-            return reused.tile(shape, dtype, name=name, align_bytes=64, offset=int(kib * 1024))
+            return reused.tile(shape, dtype, name=name, align_bytes=64, offset=int(kib * KIB))
+
+        def tiles(name, shape, dtype, which=range(ROW_TILES)):
+            return {j: keep.tile(shape, dtype, name="%s%d" % (name, j), align_bytes=64) for j in which}
 
         offsets = keep.tile([P, SLOTS // OFFSETS_PER_COLUMN], U16, name="offsets")
         d_planes = dT.rearrange("(p t) n -> t p n", t=PACK)
-        d_window = [placed([P, DOCS], F32, "d_window%d" % t, D_WINDOW_AT[t]) for t in range(PACK)]
+        d_window = tiles("d_window", [P, DOCS], F32, (0, 3))
+        d_window[1] = placed([P, DOCS], F32, "d_window1", WINDOW1_AT)
+        d_window[2] = placed([P, DOCS], F32, "d_window2", WINDOW2_AT)
         ts_window = keep.tile([P, DOCS], F32, name="ts_window")
         nc.vector.memset(ts_window[0:P - 1, :], 0.0)
         uw_rows = keep.tile([P, P], F32, name="uw_rows")
@@ -104,59 +105,63 @@ def tile_attend_grag_q_kernel(tc, xT, dT, us, ts, lk, wt, offs, out):
 
         dt_codes = placed([P, D], U32, "dt_codes", DT_CODES_AT)
         dt_scales = keep.tile([P, D], U8, name="dt_scales", align_bytes=64)
-        dt_grouped = [placed([P, len(group) * P * PACK], BF16, "dt_grouped%d" % n, DT_GROUPED_AT[n])
-                      for n, group in enumerate(DT_GROUPS)]
+        dt_grouped = [keep.tile([P, 2 * P * PACK], BF16, name="dt_grouped01", align_bytes=64),
+                      placed([P, P * PACK], BF16, "dt_grouped2", TURNED_PLANE2_AT),
+                      placed([P, P * PACK], BF16, "dt_grouped3", TURNED_PLANE3_AT)]
+        dt_plane = [tile[:, n * P * PACK:(n + 1) * P * PACK]
+                    for group, tile in zip(TURNED_GROUPS, dt_grouped) for n in range(len(group))]
+        turned_plane = {}
 
         def quantize_turned_planes(n):
-            cols = slice(DT_GROUPS[n][0] * P, (DT_GROUPS[n][-1] + 1) * P)
+            cols = slice(TURNED_GROUPS[n][0] * P, (TURNED_GROUPS[n][-1] + 1) * P)
             nc.vector.quantize_mx(out=dt_codes[:, cols].bitcast(E4M3X4), scales=dt_scales[:, cols], in_=dt_grouped[n][:])
 
-        def turn_plane(plane, bank):
+        def turn_plane(plane, t):
             words = plane.bitcast(F32)
+            turned_plane[t] = psum_bank("turned_plane%d" % t, PLANE_BANK[t], [P, BANK_BLOCKS, P])
             for u in range(2):
-                nc.tensor.transpose(bank[:, u, :], words[:, u:HALF:2], ident[:])
+                nc.tensor.transpose(turned_plane[t][:, u, :], words[:, u:HALF:2], ident[:])
 
-        def group_turned_plane(bank, t):
-            grouped = dt_grouped[max(t - 1, 0)][:, P * PACK:] if t == 1 else dt_grouped[max(t - 1, 0)][:, :P * PACK]
+        def interleave_words(grouped, bank):
             nc.scalar.copy(grouped.bitcast(F32).rearrange("p (c m u) -> p c u m", m=2, u=2),
                            bank[:, 0:2, :].rearrange("p u (c m) -> p c u m", m=2))
 
+        def group_turned_plane(t):
+            interleave_words(dt_plane[t], turned_plane[t])
+
         ts_listed = keep.tile([P, SLOTS], F32, name="ts_listed")
         nc.vector.tensor_copy(ts_listed[:], ts_window[:].indirect(offsets[:]))
-        bank = psum_bank(5, [P, BANK_BLOCKS, P])
+        bank = psum_bank("ts_col_bank", TS_COL_BANK, [P, SLOT_TILES, P])
         for s in range(SLOT_TILES):
             nc.tensor.transpose(bank[:, s, :], ts_listed[:, s * P:(s + 1) * P], ident[:])
         ts_col = keep.tile([P, SLOT_TILES], F32, name="ts_col")
         nc.scalar.copy(ts_col[:], bank[:, :, P - 1])
-        bank = psum_bank(2, [P, SLOT_TILES, P])
+        bank = psum_bank("ts_row_bank", TS_ROW_BANK, [P, SLOT_TILES, P])
         for s in range(SLOT_TILES):
             nc.tensor.transpose(bank[:, s, :], ts_col[:, s:s + 1].to_broadcast([P, P]), ident[:])
         ts_row = keep.tile([P, SLOTS], F32, name="ts_row")
         nc.scalar.copy(ts_row[:], bank[:].rearrange("m s p -> m (s p)"))
-        ts_places_bank = psum_bank(5, [P, BANK_BLOCKS, P])
+        bank = psum_bank("ts_places_bank", TS_PLACES_BANK, [P, PACK, P])
         for t in range(PACK):
-            nc.tensor.transpose(ts_places_bank[:, t, :], ts_listed[:, t:SLOTS:PACK], ident[:])
+            nc.tensor.transpose(bank[:, t, :], ts_listed[:, t:SLOTS:PACK], ident[:])
         ts_places = keep.tile([P, PACK], F32, name="ts_places")
-        nc.scalar.copy(ts_places[:], ts_places_bank[:, :, P - 1])
-        d_planes01 = placed([P, 2, SLOTS], BF16, "d_planes01", D_PLANES01_AT)
-        nc.vector.tensor_copy(d_planes01[:, 0, :], d_window[0][:].indirect(offsets[:]))
+        nc.scalar.copy(ts_places[:], bank[:, :, P - 1])
+
+        d_planes01 = keep.tile([P, 2, SLOTS], BF16, name="d_planes01", align_bytes=64)
         d_grouped = keep.tile([P, SLOTS, PACK], BF16, name="d_grouped", align_bytes=64)
-        bank = psum_bank(PLANE_BANK[0], [P, BANK_BLOCKS, P])
-        turn_plane(d_planes01[:, 0, :], bank)
-        group_turned_plane(bank, 0)
+        nc.vector.tensor_copy(d_planes01[:, 0, :], d_window[0][:].indirect(offsets[:]))
+        turn_plane(d_planes01[:, 0, :], 0)
+        group_turned_plane(0)
         nc.vector.tensor_copy(d_planes01[:, 1, :], d_window[1][:].indirect(offsets[:]))
         x_planes = xT.rearrange("(p t) r -> p t r", t=PACK)
-        x_raw = []
-        for n, (first, end) in enumerate(X_SPANS):
-            span = placed([P, PACK, end - first], F32, "x_raw%d" % n, X_RAW_AT[n])
-            nc.sync.dma_start(span[:], x_planes[:, :, first:end])
-            x_raw.extend(span[:, :, k:k + P] for k in range(0, end - first, P))
-        bank = psum_bank(PLANE_BANK[1], [P, BANK_BLOCKS, P])
-        turn_plane(d_planes01[:, 1, :], bank)
-        group_turned_plane(bank, 1)
+        x_raw = [placed([P, PACK, P], F32, "x_raw%d" % j, X_RAW_AT[j]) for j in range(ROW_TILES)]
+        for j in range(ROW_TILES):
+            nc.sync.dma_start(x_raw[j][:], x_planes[:, :, j * P:(j + 1) * P])
+        turn_plane(d_planes01[:, 1, :], 1)
+        group_turned_plane(1)
         nc.scalar.copy(d_grouped[:, :, 0:2], d_planes01[:].rearrange("p t i -> p i t"))
 
-        bank = psum_bank(4, [P, BANK_BLOCKS, P])
+        bank = psum_bank("uw_bank", UW_BANK, [P, BANK_BLOCKS, P])
         nc.tensor.transpose(bank[:, 0, :], uw_rows[:], ident[:])
         uw = keep.tile([P, 2 * ROW_TILES], F32, name="uw")
         nc.scalar.copy(uw[:], bank[:, 0, 0:2 * ROW_TILES])
@@ -166,29 +171,24 @@ def tile_attend_grag_q_kernel(tc, xT, dT, us, ts, lk, wt, offs, out):
         for j in PAIRED:
             nc.scalar.activation(stats[j][:, 2:3], uw[:, ROW_TILES + j:ROW_TILES + j + 1], ACT.Copy,
                                  scale=uw[:, j:j + 1])
-        signed_wu = keep.tile([P, 4, 2], F32, name="signed_wu")
+        signed_wu = keep.tile([P, ROW_TILES, 2], F32, name="signed_wu")
         for j in ADDED:
             for k, signed_us in enumerate((uw, neg_us)):
                 nc.scalar.activation(signed_wu[:, j, k:k + 1], uw[:, ROW_TILES + j:ROW_TILES + j + 1], ACT.Copy,
                                      scale=signed_us[:, j:j + 1])
 
-        woven_plane = {}
-        turned_plane = {}
+        picked_plane = {2: keep.tile([P, SLOTS], BF16, name="d_plane2", align_bytes=64),
+                        3: placed([P, SLOTS], BF16, "d_plane3", PLANE3_AT)}
 
         def pick_plane(t):
-            woven_plane[t] = placed([P, SLOTS], BF16, "d_plane%d" % t, D_PLANE_AT[t])
-            nc.scalar.copy(woven_plane[t][:], d_grouped[:, :, t])
-
-        def turn_picked_plane(t):
-            turned_plane[t] = psum_bank(PLANE_BANK[t], [P, BANK_BLOCKS, P])
-            turn_plane(woven_plane[t][:], turned_plane[t])
+            nc.scalar.copy(picked_plane[t][:], d_grouped[:, :, t])
 
         nc.vector.tensor_copy(d_grouped[:, :, 2], d_window[2][:].indirect(offsets[:]))
         lk_rows = [placed([P, SLOTS], F32, "lk_rows%d" % j, LK_AT[j]) for j in range(ROW_TILES)]
         for j in range(ROW_TILES):
             nc.sync.dma_start(lk_rows[j][:], lk[j * P:(j + 1) * P, :])
         pick_plane(2)
-        turn_picked_plane(2)
+        turn_plane(picked_plane[2][:], 2)
         half_columns = HALF // OFFSETS_PER_COLUMN
         for half in range(2):
             nc.vector.tensor_copy(d_grouped[:, half * HALF:(half + 1) * HALF, 3],
@@ -202,31 +202,33 @@ def tile_attend_grag_q_kernel(tc, xT, dT, us, ts, lk, wt, offs, out):
             nc.vector.quantize_mx(out=d_codes[:, cols].bitcast(E4M3X4), scales=d_scales[:, cols],
                                   in_=d_grouped[:, cols, :].rearrange("p i t -> p (i t)"))
 
-        def tiles(name, shape, dtype):
-            return [keep.tile(shape, dtype, name="%s%d" % (name, j), align_bytes=64) for j in range(ROW_TILES)]
-
-        x_grouped = [placed([P, P, PACK], BF16, "x_grouped%d" % j, X_GROUPED_AT[j]) for j in range(ROW_TILES)]
+        x_grouped = tiles("x_grouped", [P, P, PACK], BF16)
         x_codes = tiles("x_codes", [P, P], U32)
         x_scales = tiles("x_scales", [P, P], U8)
-        scaled = {j: placed([P, SLOT_TILES, P], F32, "scaled%d" % j, SCALED_AT[j]) for j in (2, 3)}
-        z = [placed([P, SLOTS], F32, "z%d" % j, Z_AT[j]) for j in range(ROW_TILES)]
+        scaled = tiles("scaled", [P, SLOT_TILES, P], F32, BY_SLOTS)
+        neg_z = [placed([P, SLOTS], F32, "neg_z%d" % j, (NEG_Z02_AT, NEG_Z13_AT)[j % 2]) for j in range(ROW_TILES)]
         neg_max = tiles("neg_max", [P, 1], F32)
         e = tiles("e", [P, SLOTS], F32)
         f = tiles("f", [P, SLOTS], F32)
         inverse = tiles("inverse", [P, 2], F32)
         factor = tiles("factor", [P, 2], F32)
-        difference = tiles("difference", [P, SLOTS], F32)
-        g_words = [{j: placed([P, HALF], BF16, "g_words%d_%d" % (u, j), G_WORDS_AT[u][j]) for j in range(4)} for u in range(2)]
+        terms = [tiles("term%d_" % k, [P, PACK, P], F32, ADDED) for k in range(2)]
+        difference = tiles("difference", [P, SLOTS], F32, PAIRED)
+        g_words = [tiles("g_words0_", [P, HALF], BF16, PAIRED), tiles("g_words1_", [P, HALF], BF16, PAIRED[:-1])]
+        g_words[1][LAST] = placed([P, HALF], BF16, "g_words1_%d" % LAST, LAST_WORDS_AT)
         g_grouped = tiles("g_grouped", [P, P * PACK], BF16)
         g_codes = tiles("g_codes", [P, P], U32)
         g_scales = tiles("g_scales", [P, P], U8)
-        staged = [placed([P, P, PACK], F32, "staged%d" % j, STAGED_AT[j]) for j in range(ROW_TILES)]
+        staged = tiles("staged", [P, P, PACK], F32, (0, 1, 3))
+        staged[2] = placed([P, P, PACK], F32, "staged2", STAGED2_AT)
+        scores = {}
+        turned_scores = {}
         turned_g = {}
         sums = {}
 
         def group_x(j):
             nc.scalar.copy(x_grouped[j][:].rearrange("p (c m) t -> p c t m", m=4),
-                           x_raw[j].rearrange("p t (c m) -> p c t m", m=4))
+                           x_raw[j][:].rearrange("p t (c m) -> p c t m", m=4))
 
         def quantize_x(j):
             nc.vector.quantize_mx(out=x_codes[j][:].bitcast(E4M3X4), scales=x_scales[j][:],
@@ -234,28 +236,25 @@ def tile_attend_grag_q_kernel(tc, xT, dT, us, ts, lk, wt, offs, out):
 
         def score_half_by_rows(j, half):
             cols = slice(half * HALF, (half + 1) * HALF)
-            a = psum_bank(half, [P, HALF])
+            a = psum_bank("first_scores%d" % half, FIRST_SCORE_BANK[half], [P, HALF])
             nc.tensor.matmul_mx(out=a[:], lhsT=x_codes[j][:].bitcast(E4M3X4), lhsT_scale=x_scales[j][:],
                                 rhs=d_codes[:, cols].bitcast(E4M3X4), rhs_scale=d_scales[:, cols],
                                 start=True, stop=True)
-            nc.vector.scalar_tensor_tensor(z[j][:, cols], a[:], neg_us[:, j:j + 1], ts_row[:, cols], ALU.mult, ALU.mult)
+            nc.vector.scalar_tensor_tensor(neg_z[j][:, cols], a[:], neg_us[:, j:j + 1], ts_row[:, cols], ALU.mult, ALU.mult)
 
         def row_minimum(j):
-            nc.vector.tensor_reduce(neg_max[j][:], z[j][:], AX.X, ALU.min)
-
-        scores = {}
-        turned_scores = {}
+            nc.vector.tensor_reduce(neg_max[j][:], neg_z[j][:], AX.X, ALU.min)
 
         def score_by_rows(j):
-            scores[j] = psum_bank(SCORE_BANK[j], [P, SLOTS])
+            scores[j] = psum_bank("scores%d" % j, SCORE_BANK[j], [P, SLOTS])
             nc.tensor.matmul_mx(out=scores[j][:], lhsT=x_codes[j][:].bitcast(E4M3X4), lhsT_scale=x_scales[j][:],
                                 rhs=d_codes[:].bitcast(E4M3X4), rhs_scale=d_scales[:], start=True, stop=True)
 
         def scale_by_rows(j):
-            nc.vector.scalar_tensor_tensor(z[j][:], scores[j][:], neg_us[:, j:j + 1], ts_row[:], ALU.mult, ALU.mult)
+            nc.vector.scalar_tensor_tensor(neg_z[j][:], scores[j][:], neg_us[:, j:j + 1], ts_row[:], ALU.mult, ALU.mult)
 
         def score_by_slots(j):
-            scores[j] = psum_bank(SCORE_BANK[j], [P, SLOT_TILES, P])
+            scores[j] = psum_bank("scores%d" % j, SCORE_BANK[j], [P, SLOT_TILES, P])
             for s in range(SLOT_TILES):
                 cols = slice(s * P, (s + 1) * P)
                 nc.tensor.matmul_mx(out=scores[j][:, s, :], lhsT=d_codes[:, cols].bitcast(E4M3X4),
@@ -267,16 +266,16 @@ def tile_attend_grag_q_kernel(tc, xT, dT, us, ts, lk, wt, offs, out):
                 nc.scalar.activation(scaled[j][:, s, :], scores[j][:, s, :], ACT.Copy, scale=ts_col[:, s:s + 1])
 
         def turn_scores(j):
-            turned_scores[j] = psum_bank(TURNED_SCORE_BANK[j], [P, SLOTS])
+            turned_scores[j] = psum_bank("turned_scores%d" % j, TURNED_SCORE_BANK[j], [P, SLOTS])
             for s in range(SLOT_TILES):
                 nc.tensor.transpose(turned_scores[j][:, s * P:(s + 1) * P], scaled[j][:, s, :], ident[:])
 
         def scale_turned_scores(j):
-            nc.vector.tensor_scalar(z[j][:], turned_scores[j][:], neg_us[:, j:j + 1], None, ALU.mult, ALU.min,
+            nc.vector.tensor_scalar(neg_z[j][:], turned_scores[j][:], neg_us[:, j:j + 1], None, ALU.mult, ALU.min,
                                     accum_out=neg_max[j][:])
 
         def exponentials(j):
-            nc.scalar.activation(e[j][:], z[j][:], ACT.Exp, bias=neg_max[j][:], scale=-1.0, accum_out=stats[j][:, 0:1])
+            nc.scalar.activation(e[j][:], neg_z[j][:], ACT.Exp, bias=neg_max[j][:], scale=-1.0, accum_out=stats[j][:, 0:1])
 
         def weigh(j):
             nc.vector.scalar_tensor_tensor(f[j][:], e[j][:], one[:], lk_rows[j][:], ALU.mult, ALU.mult,
@@ -300,13 +299,8 @@ def tile_attend_grag_q_kernel(tc, xT, dT, us, ts, lk, wt, offs, out):
 
         def turn_g(j, u):
             if u == 0:
-                turned_g[j] = psum_bank(TURNED_G_BANK[j], [P, PACK, P])
+                turned_g[j] = psum_bank("turned_g%d" % j, TURNED_G_BANK[j], [P, PACK, P])
             nc.tensor.transpose(turned_g[j][:, u, :], g_words[u][j][:].bitcast(F32), ident[:])
-
-        terms = [[placed([P, PACK, P], F32, "term%d_%d" % (k, j), TERM_AT[k][j]) for j in range(4)] for k in range(2)]
-
-        def make_term_factors(j):
-            nc.vector.tensor_tensor(factor[j][:], inverse[j][:], signed_wu[:, j, :], ALU.mult)
 
         def invert_sum(j, k):
             nc.vector.reciprocal(inverse[j][:, k:k + 1], stats[j][:, k:k + 1])
@@ -314,17 +308,14 @@ def tile_attend_grag_q_kernel(tc, xT, dT, us, ts, lk, wt, offs, out):
         def make_term_factor(j, k):
             nc.scalar.activation(factor[j][:, k:k + 1], signed_wu[:, j, k:k + 1], ACT.Copy, scale=inverse[j][:, k:k + 1])
 
-        def scale_term(j, k, engine):
+        def scale_term(j, k):
             dealt = terms[k][j][:].rearrange("r t (c m) -> r c t m", m=2)
             source = (e, f)[k][j][:].rearrange("r (c m t) -> r c t m", m=2, t=PACK)
-            if engine == "scalar":
-                nc.scalar.activation(dealt, source, ACT.Copy, scale=factor[j][:, k:k + 1])
-            else:
-                nc.vector.tensor_scalar(dealt, source, factor[j][:, k:k + 1], None, ALU.mult)
+            nc.scalar.activation(dealt, source, ACT.Copy, scale=factor[j][:, k:k + 1])
 
         def turn_term(j, k):
             if k == 0:
-                turned_g[j] = psum_bank(TURNED_G_BANK[j], [P, PACK, P])
+                turned_g[j] = psum_bank("turned_g%d" % j, TURNED_G_BANK[j], [P, PACK, P])
             for t in range(PACK):
                 nc.tensor.matmul(turned_g[j][:, t, :], terms[k][j][:, t, :], ident[:], is_transpose=True,
                                  start=(k == 0 and t == 0), stop=(k == 1 and t == PACK - 1))
@@ -335,36 +326,38 @@ def tile_attend_grag_q_kernel(tc, xT, dT, us, ts, lk, wt, offs, out):
                                     ts_places[:].unsqueeze(1).unsqueeze(3).to_broadcast([P, P // 2, PACK, 2]), ALU.mult)
 
         def group_g(j):
-            nc.scalar.copy(g_grouped[j][:].bitcast(F32).rearrange("p (c m u) -> p c u m", m=2, u=2),
-                           turned_g[j][:, 0:2, :].rearrange("p u (c m) -> p c u m", m=2))
+            interleave_words(g_grouped[j][:], turned_g[j])
 
         def quantize_g(j):
             nc.vector.quantize_mx(out=g_codes[j][:].bitcast(E5M2X4), scales=g_scales[j][:], in_=g_grouped[j][:])
 
         def product(j):
-            sums[j] = psum_bank(PRODUCT_BANK[j], [P, D])
+            sums[j] = psum_bank("sums%d" % j, PRODUCT_BANK[j], [P, D])
             nc.tensor.matmul_mx(out=sums[j][:], lhsT=g_codes[j][:].bitcast(E5M2X4), lhsT_scale=g_scales[j][:],
                                 rhs=dt_codes[:].bitcast(E4M3X4), rhs_scale=dt_scales[:], start=True, stop=True)
 
         def warm_up(j):
-            nc.tensor.matmul_mx(out=psum_bank(WARM_UP_BANK, [P, D])[:], lhsT=g_codes[j][:].bitcast(E5M2X4),
-                                lhsT_scale=g_scales[j][:], rhs=dt_codes[:].bitcast(E4M3X4), rhs_scale=dt_scales[:],
-                                start=True, stop=True)
+            unread = psum_bank("unread", WARM_UP_BANK, [P, D])
+            nc.tensor.matmul_mx(out=unread[:], lhsT=g_codes[j][:].bitcast(E5M2X4), lhsT_scale=g_scales[j][:],
+                                rhs=dt_codes[:].bitcast(E4M3X4), rhs_scale=dt_scales[:], start=True, stop=True)
 
         def store(j):
             in_order = sums[j][:].rearrange("r (t c m) -> r c t m", t=PACK, m=2)
             in_pairs = staged[j][:].rearrange("r (c m) t -> r c t m", m=2)
             rows = slice(j * P, (j + 1) * P)
-            if j != LAST:
-                nc.scalar.copy(in_pairs, in_order)
-                nc.sync.dma_start(out[rows, :], staged[j][:].rearrange("r q t -> r (q t)"))
-            else:
+            if j == LAST:
                 for half in range(2):
-                    qs = slice(half * P // 2, (half + 1) * P // 2)
-                    cs = slice(half * P // 4, (half + 1) * P // 4)
-                    nc.vector.tensor_copy(in_pairs[:, cs], in_order[:, cs])
+                    pairs = slice(half * P // 4, (half + 1) * P // 4)
+                    words = slice(half * P // 2, (half + 1) * P // 2)
+                    nc.vector.tensor_copy(in_pairs[:, pairs], in_order[:, pairs])
                     nc.sync.dma_start(out[rows, half * D // 2:(half + 1) * D // 2],
-                                      staged[j][:, qs, :].rearrange("r q t -> r (q t)"))
+                                      staged[j][:, words, :].rearrange("r q t -> r (q t)"))
+            else:
+                if j == COPIED_BY_VECTOR:
+                    nc.vector.tensor_copy(in_pairs, in_order)
+                else:
+                    nc.scalar.copy(in_pairs, in_order)
+                nc.sync.dma_start(out[rows, :], staged[j][:].rearrange("r q t -> r (q t)"))
 
         group_x(0)
         quantize_d(0)
@@ -381,7 +374,7 @@ def tile_attend_grag_q_kernel(tc, xT, dT, us, ts, lk, wt, offs, out):
         score_by_slots(2)
         row_minimum(0)
         group_x(3)
-        group_turned_plane(turned_plane[2], 2)
+        group_turned_plane(2)
         pick_plane(3)
         quantize_x(3)
         score_by_slots(3)
@@ -391,7 +384,7 @@ def tile_attend_grag_q_kernel(tc, xT, dT, us, ts, lk, wt, offs, out):
         turn_scores(2)
         scale_by_slots(3)
         turn_scores(3)
-        turn_picked_plane(3)
+        turn_plane(picked_plane[3][:], 3)
         quantize_turned_planes(1)
         row_minimum(1)
         invert_sum(0, 0)
@@ -400,7 +393,7 @@ def tile_attend_grag_q_kernel(tc, xT, dT, us, ts, lk, wt, offs, out):
         exponentials(1)
         invert_sum(0, 1)
         scale_turned_scores(2)
-        scale_term(0, 0, "scalar")
+        scale_term(0, 0)
         turn_term(0, 0)
         make_term_factor(0, 1)
         scale_turned_scores(3)
@@ -409,20 +402,20 @@ def tile_attend_grag_q_kernel(tc, xT, dT, us, ts, lk, wt, offs, out):
         invert_sum(2, 0)
         exponentials(3)
         make_term_factor(2, 0)
-        scale_term(0, 1, "scalar")
+        scale_term(0, 1)
         turn_term(0, 1)
         weigh(2)
         invert(1)
         weigh(3)
-        scale_term(2, 0, "scalar")
+        scale_term(2, 0)
         turn_term(2, 0)
         make_factors(1)
         invert_sum(2, 1)
         make_term_factor(2, 1)
-        group_turned_plane(turned_plane[3], 3)
+        group_turned_plane(3)
         subtract(1)
         invert(3)
-        scale_term(2, 1, "scalar")
+        scale_term(2, 1)
         turn_term(2, 1)
         round_turned_g(0)
         make_factors(3)
@@ -447,8 +440,8 @@ def tile_attend_grag_q_kernel(tc, xT, dT, us, ts, lk, wt, offs, out):
         group_g(3)
         quantize_g(2)
         product(2)
+        store(1)
         quantize_g(3)
         product(3)
-        store(1)
         store(2)
         store(3)

@@ -23,6 +23,8 @@ DOCS = 2048
 ROW_TILES = R // P
 SLOT_TILES = SLOTS // P
 HALF = SLOTS // 2
+HALF_D = D // 2
+QUARTER = HALF_D // PACK
 OFFSETS_PER_COLUMN = 16
 BANK_BLOCKS = 4
 
@@ -56,7 +58,8 @@ FIRST_SCORE_BANK = (0, 1)
 SCORE_BANK = {1: 2, 2: 3, 3: 5}
 TURNED_SCORE_BANK = {2: 2, 3: 1}
 TURNED_G_BANK = (4, 6, 0, 2)
-PRODUCT_BANK = (3, 4, 7, 1)
+PRODUCT_BANK = (3, 4, 7)
+LAST_PRODUCT_BANK = (1, 6)
 WARM_UP_BANK = 5
 
 FLOPS = 2 * 2 * R * SLOTS * D
@@ -103,18 +106,19 @@ def tile_attend_grag_q_kernel(tc, xT, dT, us, ts, lk, wt, offs, out):
         one = keep.tile([P, 1], F32, name="one")
         nc.scalar.activation(one[:], ident[:, 0:1], ACT.Exp, scale=0.0)
 
-        dt_codes = placed([P, D], U32, "dt_codes", DT_CODES_AT)
-        dt_scales = keep.tile([P, D], U8, name="dt_scales", align_bytes=64)
-        dt_grouped = [keep.tile([P, 2 * P * PACK], BF16, name="dt_grouped01", align_bytes=64),
-                      placed([P, P * PACK], BF16, "dt_grouped2", TURNED_PLANE2_AT),
-                      placed([P, P * PACK], BF16, "dt_grouped3", TURNED_PLANE3_AT)]
-        dt_plane = [tile[:, n * P * PACK:(n + 1) * P * PACK]
-                    for group, tile in zip(TURNED_GROUPS, dt_grouped) for n in range(len(group))]
+        dt_codes = placed([P, 2, PACK * QUARTER], U32, "dt_codes", DT_CODES_AT)
+        dt_scales = keep.tile([P, 2, PACK * QUARTER], U8, name="dt_scales", align_bytes=64)
+        dt_grouped = [keep.tile([P, 2, 2, QUARTER * PACK], BF16, name="dt_grouped01", align_bytes=64),
+                      placed([P, 2, 1, QUARTER * PACK], BF16, "dt_grouped2", TURNED_PLANE2_AT),
+                      placed([P, 2, 1, QUARTER * PACK], BF16, "dt_grouped3", TURNED_PLANE3_AT)]
+        dt_plane = [tile[:, :, v, :] for group, tile in zip(TURNED_GROUPS, dt_grouped) for v in range(len(group))]
         turned_plane = {}
 
         def quantize_turned_planes(n):
-            cols = slice(TURNED_GROUPS[n][0] * P, (TURNED_GROUPS[n][-1] + 1) * P)
-            nc.vector.quantize_mx(out=dt_codes[:, cols].bitcast(E4M3X4), scales=dt_scales[:, cols], in_=dt_grouped[n][:])
+            cols = slice(TURNED_GROUPS[n][0] * QUARTER, (TURNED_GROUPS[n][-1] + 1) * QUARTER)
+            for h in range(2):
+                nc.vector.quantize_mx(out=dt_codes[:, h, cols].bitcast(E4M3X4), scales=dt_scales[:, h, cols],
+                                      in_=dt_grouped[n][:, h].rearrange("p v x -> p (v x)"))
 
         def turn_plane(plane, t):
             words = plane.bitcast(F32)
@@ -127,7 +131,8 @@ def tile_attend_grag_q_kernel(tc, xT, dT, us, ts, lk, wt, offs, out):
                            bank[:, 0:2, :].rearrange("p u (c m) -> p c u m", m=2))
 
         def group_turned_plane(t):
-            interleave_words(dt_plane[t], turned_plane[t])
+            nc.scalar.copy(dt_plane[t].bitcast(F32).rearrange("p h (c m u) -> p h c u m", m=2, u=2),
+                           turned_plane[t][:, 0:2, :].rearrange("p u (h c m) -> p h c u m", h=2, m=2))
 
         ts_listed = keep.tile([P, SLOTS], F32, name="ts_listed")
         nc.vector.tensor_copy(ts_listed[:], ts_window[:].indirect(offsets[:]))
@@ -219,8 +224,9 @@ def tile_attend_grag_q_kernel(tc, xT, dT, us, ts, lk, wt, offs, out):
         g_grouped = tiles("g_grouped", [P, P * PACK], BF16)
         g_codes = tiles("g_codes", [P, P], U32)
         g_scales = tiles("g_scales", [P, P], U8)
-        staged = tiles("staged", [P, P, PACK], F32, (0, 1, 3))
-        staged[2] = placed([P, P, PACK], F32, "staged2", STAGED2_AT)
+        staged = tiles("staged", [P, D], F32, (0, 1))
+        staged[2] = placed([P, D], F32, "staged2", STAGED2_AT)
+        staged_half = tiles("staged_half", [P, HALF_D], F32, range(2))
         scores = {}
         turned_scores = {}
         turned_g = {}
@@ -334,30 +340,29 @@ def tile_attend_grag_q_kernel(tc, xT, dT, us, ts, lk, wt, offs, out):
         def product(j):
             sums[j] = psum_bank("sums%d" % j, PRODUCT_BANK[j], [P, D])
             nc.tensor.matmul_mx(out=sums[j][:], lhsT=g_codes[j][:].bitcast(E5M2X4), lhsT_scale=g_scales[j][:],
-                                rhs=dt_codes[:].bitcast(E4M3X4), rhs_scale=dt_scales[:], start=True, stop=True)
+                                rhs=dt_codes[:].rearrange("p h x -> p (h x)").bitcast(E4M3X4),
+                                rhs_scale=dt_scales[:].rearrange("p h x -> p (h x)"), start=True, stop=True)
 
         def warm_up(j):
             unread = psum_bank("unread", WARM_UP_BANK, [P, D])
             nc.tensor.matmul_mx(out=unread[:], lhsT=g_codes[j][:].bitcast(E5M2X4), lhsT_scale=g_scales[j][:],
-                                rhs=dt_codes[:].bitcast(E4M3X4), rhs_scale=dt_scales[:], start=True, stop=True)
+                                rhs=dt_codes[:].rearrange("p h x -> p (h x)").bitcast(E4M3X4),
+                                rhs_scale=dt_scales[:].rearrange("p h x -> p (h x)"), start=True, stop=True)
 
         def store(j):
-            in_order = sums[j][:].rearrange("r (t c m) -> r c t m", t=PACK, m=2)
-            in_pairs = staged[j][:].rearrange("r (c m) t -> r c t m", m=2)
-            rows = slice(j * P, (j + 1) * P)
-            if j == LAST:
-                for half in range(2):
-                    pairs = slice(half * P // 4, (half + 1) * P // 4)
-                    words = slice(half * P // 2, (half + 1) * P // 2)
-                    nc.vector.tensor_copy(in_pairs[:, pairs], in_order[:, pairs])
-                    nc.sync.dma_start(out[rows, half * D // 2:(half + 1) * D // 2],
-                                      staged[j][:, words, :].rearrange("r q t -> r (q t)"))
-            else:
-                if j == COPIED_BY_VECTOR:
-                    nc.vector.tensor_copy(in_pairs, in_order)
-                else:
-                    nc.scalar.copy(in_pairs, in_order)
-                nc.sync.dma_start(out[rows, :], staged[j][:].rearrange("r q t -> r (q t)"))
+            copy_out = nc.vector.tensor_copy if j == COPIED_BY_VECTOR else nc.scalar.copy
+            copy_out(staged[j][:].rearrange("r (h c m t) -> r h c t m", h=2, m=2, t=PACK),
+                     sums[j][:].rearrange("r (h t c m) -> r h c t m", h=2, t=PACK, m=2))
+            nc.sync.dma_start(out[j * P:(j + 1) * P, :], staged[j][:])
+
+        def last_product_and_store():
+            for h, copy_out in enumerate((nc.vector.tensor_copy, nc.scalar.copy)):
+                bank = psum_bank("last_sums%d" % h, LAST_PRODUCT_BANK[h], [P, HALF_D])
+                nc.tensor.matmul_mx(out=bank[:], lhsT=g_codes[LAST][:].bitcast(E5M2X4), lhsT_scale=g_scales[LAST][:],
+                                    rhs=dt_codes[:, h].bitcast(E4M3X4), rhs_scale=dt_scales[:, h], start=True, stop=True)
+                copy_out(staged_half[h][:].rearrange("r (c m t) -> r c t m", m=2, t=PACK),
+                         bank[:].rearrange("r (t c m) -> r c t m", t=PACK, m=2))
+                nc.sync.dma_start(out[LAST * P:(LAST + 1) * P, h * HALF_D:(h + 1) * HALF_D], staged_half[h][:])
 
         group_x(0)
         quantize_d(0)
@@ -442,6 +447,5 @@ def tile_attend_grag_q_kernel(tc, xT, dT, us, ts, lk, wt, offs, out):
         product(2)
         store(1)
         quantize_g(3)
-        product(3)
         store(2)
-        store(3)
+        last_product_and_store()

@@ -164,7 +164,8 @@ def tile_attend_grag_q_kernel(tc, xT, dT, us, ts, lk, wt, offs, out):
             nc.sync.dma_start(x_raw[j][:], x_planes[:, :, j * P:(j + 1) * P])
         turn_plane(d_planes01[:, 1, :], 1)
         group_turned_plane(1)
-        nc.scalar.copy(d_grouped[:, :, 0:2], d_planes01[:].rearrange("p t i -> p i t"))
+        nc.scalar.copy(d_grouped[:, :, 0:2].rearrange("p (c m) t -> p c t m", m=4),
+                       d_planes01[:].rearrange("p t (c m) -> p c t m", m=4))
 
         bank = psum_bank("uw_bank", UW_BANK, [P, BANK_BLOCKS, P])
         nc.tensor.transpose(bank[:, 0, :], uw_rows[:], ident[:])
@@ -217,7 +218,7 @@ def tile_attend_grag_q_kernel(tc, xT, dT, us, ts, lk, wt, offs, out):
         f = tiles("f", [P, SLOTS], F32)
         inverse = tiles("inverse", [P, 2], F32)
         factor = tiles("factor", [P, 2], F32)
-        terms = [tiles("term%d_" % k, [P, PACK, P], F32, ADDED) for k in range(2)]
+        terms = [tiles("term%d_" % k, [P, 2, P, 2], F32, ADDED) for k in range(2)]
         difference = tiles("difference", [P, SLOTS], F32, PAIRED)
         g_words = [tiles("g_words0_", [P, HALF], BF16, PAIRED), tiles("g_words1_", [P, HALF], BF16, PAIRED[:-1])]
         g_words[1][LAST] = placed([P, HALF], BF16, "g_words1_%d" % LAST, LAST_WORDS_AT)
@@ -315,15 +316,14 @@ def tile_attend_grag_q_kernel(tc, xT, dT, us, ts, lk, wt, offs, out):
             nc.scalar.activation(factor[j][:, k:k + 1], signed_wu[:, j, k:k + 1], ACT.Copy, scale=inverse[j][:, k:k + 1])
 
         def scale_term(j, k):
-            dealt = terms[k][j][:].rearrange("r t (c m) -> r c t m", m=2)
-            source = (e, f)[k][j][:].rearrange("r (c m t) -> r c t m", m=2, t=PACK)
-            nc.scalar.activation(dealt, source, ACT.Copy, scale=factor[j][:, k:k + 1])
+            source = (e, f)[k][j][:].rearrange("r (p u v) -> r u p v", u=2, v=2)
+            nc.scalar.activation(terms[k][j][:], source, ACT.Copy, scale=factor[j][:, k:k + 1])
 
         def turn_term(j, k):
             if k == 0:
                 turned_g[j] = psum_bank("turned_g%d" % j, TURNED_G_BANK[j], [P, PACK, P])
             for t in range(PACK):
-                nc.tensor.matmul(turned_g[j][:, t, :], terms[k][j][:, t, :], ident[:], is_transpose=True,
+                nc.tensor.matmul(turned_g[j][:, t, :], terms[k][j][:, t // 2, :, t % 2], ident[:], is_transpose=True,
                                  start=(k == 0 and t == 0), stop=(k == 1 and t == PACK - 1))
 
         def round_turned_g(j):

@@ -34,8 +34,7 @@ KIB = 1024
 ADDED = (0, 2)
 PAIRED = (1, 3)
 BY_SLOTS = (2, 3)
-LAST = 3
-COPIED_BY_VECTOR = 1
+IN_HALVES = (2, 3)
 TURNED_GROUPS = ((0, 1), (2,), (3,))
 
 WINDOW1_AT = 0
@@ -49,8 +48,7 @@ TURNED_PLANE3_AT = 5.5
 WINDOW2_AT = 9
 LK_AT = (9, 11, 13, 15)
 NEG_Z02_AT = 17
-LAST_WORDS_AT = 19
-STAGED2_AT = 19
+F_AT = {1: 19, 3: 21}
 
 TS_COL_BANK, TS_ROW_BANK, TS_PLACES_BANK, UW_BANK = 5, 2, 5, 4
 PLANE_BANK = (0, 1, 7, 5)
@@ -58,9 +56,8 @@ FIRST_SCORE_BANK = (0, 1)
 SCORE_BANK = {1: 2, 2: 3, 3: 5}
 TURNED_SCORE_BANK = {2: 2, 3: 1}
 TURNED_G_BANK = (4, 6, 0, 2)
-PRODUCT_BANK = (3, 4, 7)
-LAST_PRODUCT_BANK = (1, 6)
-WARM_UP_BANK = 5
+PRODUCT_BANK = (3, 4)
+HALF_PRODUCT_BANK = {2: (7, 6), 3: (1, 3)}
 
 FLOPS = 2 * 2 * R * SLOTS * D
 BYTES = 4 * (D * R + D * DOCS + R * SLOTS + R * D + DOCS + 2 * R) + 2 * P * SLOTS // OFFSETS_PER_COLUMN
@@ -215,19 +212,21 @@ def tile_attend_grag_q_kernel(tc, xT, dT, us, ts, lk, wt, offs, out):
         neg_z = [placed([P, SLOTS], F32, "neg_z%d" % j, (NEG_Z02_AT, NEG_Z13_AT)[j % 2]) for j in range(ROW_TILES)]
         neg_max = tiles("neg_max", [P, 1], F32)
         e = tiles("e", [P, SLOTS], F32)
-        f = tiles("f", [P, SLOTS], F32)
+        f = tiles("f", [P, SLOTS], F32, ADDED)
+        for j in PAIRED:
+            f[j] = placed([P, SLOTS], F32, "f%d" % j, F_AT[j])
         inverse = tiles("inverse", [P, 2], F32)
         factor = tiles("factor", [P, 2], F32)
         terms = [tiles("term%d_" % k, [P, 2, P, 2], F32, ADDED) for k in range(2)]
         difference = tiles("difference", [P, SLOTS], F32, PAIRED)
-        g_words = [tiles("g_words0_", [P, HALF], BF16, PAIRED), tiles("g_words1_", [P, HALF], BF16, PAIRED[:-1])]
-        g_words[1][LAST] = placed([P, HALF], BF16, "g_words1_%d" % LAST, LAST_WORDS_AT)
-        g_grouped = tiles("g_grouped", [P, P * PACK], BF16)
+        g_words = [tiles("g_words%d_" % u, [P, HALF], BF16, PAIRED) for u in range(2)]
+        g_grouped = tiles("g_grouped", [P, P * PACK], BF16, PAIRED)
+        for j in ADDED:
+            g_grouped[j] = placed([P, P * PACK], BF16, "g_grouped%d" % j, F_AT[j + 1])
         g_codes = tiles("g_codes", [P, P], U32)
         g_scales = tiles("g_scales", [P, P], U8)
         staged = tiles("staged", [P, D], F32, (0, 1))
-        staged[2] = placed([P, D], F32, "staged2", STAGED2_AT)
-        staged_half = tiles("staged_half", [P, HALF_D], F32, range(2))
+        staged_half = {j: tiles("staged_half%d_" % j, [P, HALF_D], F32, range(2)) for j in IN_HALVES}
         scores = {}
         turned_scores = {}
         turned_g = {}
@@ -343,26 +342,19 @@ def tile_attend_grag_q_kernel(tc, xT, dT, us, ts, lk, wt, offs, out):
                                 rhs=dt_codes[:].rearrange("p h x -> p (h x)").bitcast(E4M3X4),
                                 rhs_scale=dt_scales[:].rearrange("p h x -> p (h x)"), start=True, stop=True)
 
-        def warm_up(j):
-            unread = psum_bank("unread", WARM_UP_BANK, [P, D])
-            nc.tensor.matmul_mx(out=unread[:], lhsT=g_codes[j][:].bitcast(E5M2X4), lhsT_scale=g_scales[j][:],
-                                rhs=dt_codes[:].rearrange("p h x -> p (h x)").bitcast(E4M3X4),
-                                rhs_scale=dt_scales[:].rearrange("p h x -> p (h x)"), start=True, stop=True)
-
         def store(j):
-            copy_out = nc.vector.tensor_copy if j == COPIED_BY_VECTOR else nc.scalar.copy
-            copy_out(staged[j][:].rearrange("r (h c m t) -> r h c t m", h=2, m=2, t=PACK),
-                     sums[j][:].rearrange("r (h t c m) -> r h c t m", h=2, t=PACK, m=2))
+            nc.scalar.copy(staged[j][:].rearrange("r (h c m t) -> r h c t m", h=2, m=2, t=PACK),
+                           sums[j][:].rearrange("r (h t c m) -> r h c t m", h=2, t=PACK, m=2))
             nc.sync.dma_start(out[j * P:(j + 1) * P, :], staged[j][:])
 
-        def last_product_and_store():
+        def product_and_store_in_halves(j):
             for h, copy_out in enumerate((nc.vector.tensor_copy, nc.scalar.copy)):
-                bank = psum_bank("last_sums%d" % h, LAST_PRODUCT_BANK[h], [P, HALF_D])
-                nc.tensor.matmul_mx(out=bank[:], lhsT=g_codes[LAST][:].bitcast(E5M2X4), lhsT_scale=g_scales[LAST][:],
+                bank = psum_bank("sums%d_%d" % (j, h), HALF_PRODUCT_BANK[j][h], [P, HALF_D])
+                nc.tensor.matmul_mx(out=bank[:], lhsT=g_codes[j][:].bitcast(E5M2X4), lhsT_scale=g_scales[j][:],
                                     rhs=dt_codes[:, h].bitcast(E4M3X4), rhs_scale=dt_scales[:, h], start=True, stop=True)
-                copy_out(staged_half[h][:].rearrange("r (c m t) -> r c t m", m=2, t=PACK),
+                copy_out(staged_half[j][h][:].rearrange("r (c m t) -> r c t m", m=2, t=PACK),
                          bank[:].rearrange("r (t c m) -> r c t m", t=PACK, m=2))
-                nc.sync.dma_start(out[LAST * P:(LAST + 1) * P, h * HALF_D:(h + 1) * HALF_D], staged_half[h][:])
+                nc.sync.dma_start(out[j * P:(j + 1) * P, h * HALF_D:(h + 1) * HALF_D], staged_half[j][h][:])
 
         group_x(0)
         quantize_d(0)
@@ -421,31 +413,29 @@ def tile_attend_grag_q_kernel(tc, xT, dT, us, ts, lk, wt, offs, out):
         subtract(1)
         invert(3)
         scale_term(2, 1)
-        turn_term(2, 1)
-        round_turned_g(0)
-        make_factors(3)
+        quantize_turned_planes(2)
         round_g(1, 0)
         turn_g(1, 0)
         round_g(1, 1)
         turn_g(1, 1)
-        quantize_turned_planes(2)
+        turn_term(2, 1)
+        round_turned_g(0)
+        make_factors(3)
+        group_g(1)
         quantize_g(0)
         product(0)
-        warm_up(0)
-        group_g(1)
         subtract(3)
-        round_turned_g(2)
+        quantize_g(1)
+        product(1)
         round_g(3, 0)
         turn_g(3, 0)
         round_g(3, 1)
         turn_g(3, 1)
+        round_turned_g(2)
         store(0)
-        quantize_g(1)
-        product(1)
         group_g(3)
-        quantize_g(2)
-        product(2)
         store(1)
+        quantize_g(2)
         quantize_g(3)
-        store(2)
-        last_product_and_store()
+        product_and_store_in_halves(2)
+        product_and_store_in_halves(3)

@@ -123,9 +123,9 @@ def tile_attend_grag_q_kernel(tc, xT, dT, us, ts, lk, wt, offs, out):
             for u in range(2):
                 nc.tensor.transpose(turned_plane[t][:, u, :], words[:, u:HALF:2], ident[:])
 
-        def interleave_words(grouped, bank):
-            nc.scalar.copy(grouped.bitcast(F32).rearrange("p (c m u) -> p c u m", m=2, u=2),
-                           bank[:, 0:2, :].rearrange("p u (c m) -> p c u m", m=2))
+        def interleave_words(copy, grouped, bank):
+            copy(grouped.bitcast(F32).rearrange("p (c m u) -> p c u m", m=2, u=2),
+                 bank[:, 0:2, :].rearrange("p u (c m) -> p c u m", m=2))
 
         def group_turned_plane(t):
             nc.scalar.copy(dt_plane[t].bitcast(F32).rearrange("p h (c m u) -> p h c u m", m=2, u=2),
@@ -331,7 +331,7 @@ def tile_attend_grag_q_kernel(tc, xT, dT, us, ts, lk, wt, offs, out):
                                     ts_places[:].unsqueeze(1).unsqueeze(3).to_broadcast([P, P // 2, PACK, 2]), ALU.mult)
 
         def group_g(j):
-            interleave_words(g_grouped[j][:], turned_g[j])
+            interleave_words(nc.vector.tensor_copy if j == PAIRED[-1] else nc.scalar.copy, g_grouped[j][:], turned_g[j])
 
         def quantize_g(j):
             nc.vector.quantize_mx(out=g_codes[j][:].bitcast(E5M2X4), scales=g_scales[j][:], in_=g_grouped[j][:])
@@ -342,10 +342,19 @@ def tile_attend_grag_q_kernel(tc, xT, dT, us, ts, lk, wt, offs, out):
                                 rhs=dt_codes[:].rearrange("p h x -> p (h x)").bitcast(E4M3X4),
                                 rhs_scale=dt_scales[:].rearrange("p h x -> p (h x)"), start=True, stop=True)
 
+        def warm_up(j):
+            unread = psum_bank("unread", TURNED_G_BANK[j], [P, SLOTS])
+            nc.tensor.matmul_mx(out=unread[:], lhsT=x_codes[j][:].bitcast(E4M3X4), lhsT_scale=x_scales[j][:],
+                                rhs=d_codes[:].bitcast(E4M3X4), rhs_scale=d_scales[:], start=True, stop=True)
+
         def store(j):
-            nc.scalar.copy(staged[j][:].rearrange("r (h c m t) -> r h c t m", h=2, m=2, t=PACK),
-                           sums[j][:].rearrange("r (h t c m) -> r h c t m", h=2, t=PACK, m=2))
-            nc.sync.dma_start(out[j * P:(j + 1) * P, :], staged[j][:])
+            parts = 2 if j == 0 else 1
+            for part in range(parts):
+                halves = slice(part * 2 // parts, (part + 1) * 2 // parts)
+                cols = slice(part * D // parts, (part + 1) * D // parts)
+                nc.scalar.copy(staged[j][:].rearrange("r (h c m t) -> r h c t m", h=2, m=2, t=PACK)[:, halves],
+                               sums[j][:].rearrange("r (h t c m) -> r h c t m", h=2, t=PACK, m=2)[:, halves])
+                nc.sync.dma_start(out[j * P:(j + 1) * P, cols], staged[j][:, cols])
 
         def product_and_store_in_halves(j):
             for h, copy_out in enumerate((nc.vector.tensor_copy, nc.scalar.copy)):
@@ -416,15 +425,16 @@ def tile_attend_grag_q_kernel(tc, xT, dT, us, ts, lk, wt, offs, out):
         quantize_turned_planes(2)
         round_g(1, 0)
         turn_g(1, 0)
+        make_factors(3)
         round_g(1, 1)
         turn_g(1, 1)
         turn_term(2, 1)
         round_turned_g(0)
-        make_factors(3)
+        warm_up(0)
         group_g(1)
+        subtract(3)
         quantize_g(0)
         product(0)
-        subtract(3)
         quantize_g(1)
         product(1)
         round_g(3, 0)
@@ -433,9 +443,9 @@ def tile_attend_grag_q_kernel(tc, xT, dT, us, ts, lk, wt, offs, out):
         turn_g(3, 1)
         round_turned_g(2)
         store(0)
-        group_g(3)
         store(1)
         quantize_g(2)
+        group_g(3)
         quantize_g(3)
         product_and_store_in_halves(2)
         product_and_store_in_halves(3)

@@ -34,7 +34,7 @@ KIB = 1024
 ADDED = (0, 2)
 PAIRED = (1, 3)
 BY_SLOTS = (2, 3)
-IN_HALVES = (2, 3)
+IN_HALVES = (3,)
 TURNED_GROUPS = ((0, 1), (2,), (3,))
 
 WINDOW1_AT = 0
@@ -56,8 +56,8 @@ FIRST_SCORE_BANK = (0, 1)
 SCORE_BANK = {1: 2, 2: 3, 3: 5}
 TURNED_SCORE_BANK = {2: 2, 3: 1}
 TURNED_G_BANK = (4, 6, 0, 2)
-PRODUCT_BANK = (3, 4)
-HALF_PRODUCT_BANK = {2: (7, 6), 3: (1, 3)}
+PRODUCT_BANK = (3, 4, 7)
+HALF_PRODUCT_BANK = {3: (1, 6)}
 
 FLOPS = 2 * 2 * R * SLOTS * D
 BYTES = 4 * (D * R + D * DOCS + R * SLOTS + R * D + DOCS + 2 * R) + 2 * P * SLOTS // OFFSETS_PER_COLUMN
@@ -223,9 +223,10 @@ def tile_attend_grag_q_kernel(tc, xT, dT, us, ts, lk, wt, offs, out):
         g_grouped = tiles("g_grouped", [P, P * PACK], BF16, PAIRED)
         for j in ADDED:
             g_grouped[j] = placed([P, P * PACK], BF16, "g_grouped%d" % j, F_AT[j + 1])
+        g_places = keep.tile([P, PACK, P], BF16, name="g_places", align_bytes=64)
         g_codes = tiles("g_codes", [P, P], U32)
         g_scales = tiles("g_scales", [P, P], U8)
-        staged = tiles("staged", [P, D], F32, (0, 1))
+        staged = tiles("staged", [P, D], F32, (0, 1, 2))
         staged_half = {j: tiles("staged_half%d_" % j, [P, HALF_D], F32, range(2)) for j in IN_HALVES}
         scores = {}
         turned_scores = {}
@@ -330,6 +331,14 @@ def tile_attend_grag_q_kernel(tc, xT, dT, us, ts, lk, wt, offs, out):
                                     turned_g[j][:].rearrange("p t (c m) -> p c t m", m=2),
                                     ts_places[:].unsqueeze(1).unsqueeze(3).to_broadcast([P, P // 2, PACK, 2]), ALU.mult)
 
+        def round_turned_g_by_places(j):
+            for t in range(PACK):
+                nc.scalar.activation(g_places[:, t, :], turned_g[j][:, t, :], ACT.Copy, scale=ts_places[:, t:t + 1])
+
+        def weave_places(j):
+            nc.vector.tensor_copy(g_grouped[j][:].rearrange("p (c m t) -> p c t m", m=4, t=PACK),
+                                  g_places[:].rearrange("p t (c m) -> p c t m", m=4))
+
         def group_g(j):
             interleave_words(nc.vector.tensor_copy if j == PAIRED[-1] else nc.scalar.copy, g_grouped[j][:], turned_g[j])
 
@@ -348,12 +357,10 @@ def tile_attend_grag_q_kernel(tc, xT, dT, us, ts, lk, wt, offs, out):
                                 rhs=d_codes[:].bitcast(E4M3X4), rhs_scale=d_scales[:], start=True, stop=True)
 
         def store(j):
-            parts = 2 if j == 0 else 1
-            for part in range(parts):
-                halves = slice(part * 2 // parts, (part + 1) * 2 // parts)
-                cols = slice(part * D // parts, (part + 1) * D // parts)
-                nc.scalar.copy(staged[j][:].rearrange("r (h c m t) -> r h c t m", h=2, m=2, t=PACK)[:, halves],
-                               sums[j][:].rearrange("r (h t c m) -> r h c t m", h=2, t=PACK, m=2)[:, halves])
+            for h in range(2):
+                cols = slice(h * HALF_D, (h + 1) * HALF_D)
+                nc.scalar.copy(staged[j][:, cols].rearrange("r (c m t) -> r c t m", m=2, t=PACK),
+                               sums[j][:, cols].rearrange("r (t c m) -> r c t m", t=PACK, m=2))
                 nc.sync.dma_start(out[j * P:(j + 1) * P, cols], staged[j][:, cols])
 
         def product_and_store_in_halves(j):
@@ -432,6 +439,7 @@ def tile_attend_grag_q_kernel(tc, xT, dT, us, ts, lk, wt, offs, out):
         round_turned_g(0)
         warm_up(0)
         group_g(1)
+        round_turned_g_by_places(2)
         subtract(3)
         quantize_g(0)
         product(0)
@@ -441,11 +449,12 @@ def tile_attend_grag_q_kernel(tc, xT, dT, us, ts, lk, wt, offs, out):
         turn_g(3, 0)
         round_g(3, 1)
         turn_g(3, 1)
-        round_turned_g(2)
+        weave_places(2)
         store(0)
         store(1)
         quantize_g(2)
+        product(2)
         group_g(3)
         quantize_g(3)
-        product_and_store_in_halves(2)
+        store(2)
         product_and_store_in_halves(3)

@@ -351,11 +351,6 @@ def tile_attend_grag_q_kernel(tc, xT, dT, us, ts, lk, wt, offs, out):
                                 rhs=dt_codes[:].rearrange("p h x -> p (h x)").bitcast(E4M3X4),
                                 rhs_scale=dt_scales[:].rearrange("p h x -> p (h x)"), start=True, stop=True)
 
-        def warm_up(j):
-            unread = psum_bank("unread", TURNED_G_BANK[j], [P, SLOTS])
-            nc.tensor.matmul_mx(out=unread[:], lhsT=x_codes[j][:].bitcast(E4M3X4), lhsT_scale=x_scales[j][:],
-                                rhs=d_codes[:].bitcast(E4M3X4), rhs_scale=d_scales[:], start=True, stop=True)
-
         def store(j):
             for h in range(2):
                 cols = slice(h * HALF_D, (h + 1) * HALF_D)
@@ -437,7 +432,6 @@ def tile_attend_grag_q_kernel(tc, xT, dT, us, ts, lk, wt, offs, out):
         turn_g(1, 1)
         turn_term(2, 1)
         round_turned_g(0)
-        warm_up(0)
         group_g(1)
         round_turned_g_by_places(2)
         subtract(3)

@@ -59,6 +59,8 @@ TURNED_G_BANK = (4, 6, 0, 2)
 PRODUCT_BANK = (3, 4, 7)
 HALF_PRODUCT_BANK = {3: (1, 6)}
 
+WARM_UP_COLUMNS = (slice(0, HALF), slice(HALF, HALF + P))
+
 FLOPS = 2 * 2 * R * SLOTS * D
 BYTES = 4 * (D * R + D * DOCS + R * SLOTS + R * D + DOCS + 2 * R) + 2 * P * SLOTS // OFFSETS_PER_COLUMN
 
@@ -351,6 +353,13 @@ def tile_attend_grag_q_kernel(tc, xT, dT, us, ts, lk, wt, offs, out):
                                 rhs=dt_codes[:].rearrange("p h x -> p (h x)").bitcast(E4M3X4),
                                 rhs_scale=dt_scales[:].rearrange("p h x -> p (h x)"), start=True, stop=True)
 
+        def warm_up(j):
+            unread = psum_bank("unread", TURNED_G_BANK[j], [P, SLOTS])
+            for cols in WARM_UP_COLUMNS:
+                nc.tensor.matmul_mx(out=unread[:, cols], lhsT=x_codes[j][:].bitcast(E4M3X4), lhsT_scale=x_scales[j][:],
+                                    rhs=d_codes[:, cols].bitcast(E4M3X4), rhs_scale=d_scales[:, cols],
+                                    start=True, stop=True)
+
         def store(j):
             for h in range(2):
                 cols = slice(h * HALF_D, (h + 1) * HALF_D)
@@ -432,6 +441,7 @@ def tile_attend_grag_q_kernel(tc, xT, dT, us, ts, lk, wt, offs, out):
         turn_g(1, 1)
         turn_term(2, 1)
         round_turned_g(0)
+        warm_up(0)
         group_g(1)
         round_turned_g_by_places(2)
         subtract(3)

@@ -34,7 +34,7 @@ KIB = 1024
 ADDED = (0, 2)
 PAIRED = (1, 3)
 BY_SLOTS = (2, 3)
-IN_HALVES = (3,)
+IN_HALVES = (2, 3)
 TURNED_GROUPS = ((0, 1), (2,), (3,))
 
 WINDOW1_AT = 0
@@ -56,8 +56,8 @@ FIRST_SCORE_BANK = (0, 1)
 SCORE_BANK = {1: 2, 2: 3, 3: 5}
 TURNED_SCORE_BANK = {2: 2, 3: 1}
 TURNED_G_BANK = (4, 6, 0, 2)
-PRODUCT_BANK = (3, 4, 7)
-HALF_PRODUCT_BANK = {3: (1, 6)}
+PRODUCT_BANK = (3, 4)
+HALF_PRODUCT_BANK = {2: (7, 5), 3: (1, 6)}
 
 WARM_UP_COLUMNS = (slice(0, HALF), slice(HALF, HALF + P))
 
@@ -222,13 +222,14 @@ def tile_attend_grag_q_kernel(tc, xT, dT, us, ts, lk, wt, offs, out):
         terms = [tiles("term%d_" % k, [P, 2, P, 2], F32, ADDED) for k in range(2)]
         difference = tiles("difference", [P, SLOTS], F32, PAIRED)
         g_words = [tiles("g_words%d_" % u, [P, HALF], BF16, PAIRED) for u in range(2)]
-        g_grouped = tiles("g_grouped", [P, P * PACK], BF16, PAIRED)
+        g_grouped = tiles("g_grouped", [P, P * PACK], BF16, PAIRED[:-1])
+        last_grouped = tiles("last_grouped", [P, P // 2 * PACK], BF16, range(2))
         for j in ADDED:
             g_grouped[j] = placed([P, P * PACK], BF16, "g_grouped%d" % j, F_AT[j + 1])
         g_places = keep.tile([P, PACK, P], BF16, name="g_places", align_bytes=64)
         g_codes = tiles("g_codes", [P, P], U32)
         g_scales = tiles("g_scales", [P, P], U8)
-        staged = tiles("staged", [P, D], F32, (0, 1, 2))
+        staged = tiles("staged", [P, D], F32, (0, 1))
         staged_half = {j: tiles("staged_half%d_" % j, [P, HALF_D], F32, range(2)) for j in IN_HALVES}
         scores = {}
         turned_scores = {}
@@ -342,7 +343,16 @@ def tile_attend_grag_q_kernel(tc, xT, dT, us, ts, lk, wt, offs, out):
                                   g_places[:].rearrange("p t (c m) -> p c t m", m=4))
 
         def group_g(j):
-            interleave_words(nc.vector.tensor_copy if j == PAIRED[-1] else nc.scalar.copy, g_grouped[j][:], turned_g[j])
+            interleave_words(nc.scalar.copy, g_grouped[j][:], turned_g[j][:])
+
+        def group_and_quantize_last(j):
+            for half in range(2):
+                interleave_words(nc.vector.tensor_copy, last_grouped[half][:],
+                                 turned_g[j][:, :, half * (P // 2):(half + 1) * (P // 2)])
+            for half in range(2):
+                cols = slice(half * (P // 2), (half + 1) * (P // 2))
+                nc.vector.quantize_mx(out=g_codes[j][:, cols].bitcast(E5M2X4), scales=g_scales[j][:, cols],
+                                      in_=last_grouped[half][:])
 
         def quantize_g(j):
             nc.vector.quantize_mx(out=g_codes[j][:].bitcast(E5M2X4), scales=g_scales[j][:], in_=g_grouped[j][:])
@@ -367,14 +377,16 @@ def tile_attend_grag_q_kernel(tc, xT, dT, us, ts, lk, wt, offs, out):
                                sums[j][:, cols].rearrange("r (t c m) -> r c t m", t=PACK, m=2))
                 nc.sync.dma_start(out[j * P:(j + 1) * P, cols], staged[j][:, cols])
 
-        def product_and_store_in_halves(j):
-            for h, copy_out in enumerate((nc.vector.tensor_copy, nc.scalar.copy)):
-                bank = psum_bank("sums%d_%d" % (j, h), HALF_PRODUCT_BANK[j][h], [P, HALF_D])
-                nc.tensor.matmul_mx(out=bank[:], lhsT=g_codes[j][:].bitcast(E5M2X4), lhsT_scale=g_scales[j][:],
+        def product_in_halves(j):
+            for h in range(2):
+                sums[j, h] = psum_bank("sums%d_%d" % (j, h), HALF_PRODUCT_BANK[j][h], [P, HALF_D])
+                nc.tensor.matmul_mx(out=sums[j, h][:], lhsT=g_codes[j][:].bitcast(E5M2X4), lhsT_scale=g_scales[j][:],
                                     rhs=dt_codes[:, h].bitcast(E4M3X4), rhs_scale=dt_scales[:, h], start=True, stop=True)
-                copy_out(staged_half[j][h][:].rearrange("r (c m t) -> r c t m", m=2, t=PACK),
-                         bank[:].rearrange("r (t c m) -> r c t m", t=PACK, m=2))
-                nc.sync.dma_start(out[j * P:(j + 1) * P, h * HALF_D:(h + 1) * HALF_D], staged_half[j][h][:])
+
+        def store_half(j, h, copy_out):
+            copy_out(staged_half[j][h][:].rearrange("r (c m t) -> r c t m", m=2, t=PACK),
+                     sums[j, h][:].rearrange("r (t c m) -> r c t m", t=PACK, m=2))
+            nc.sync.dma_start(out[j * P:(j + 1) * P, h * HALF_D:(h + 1) * HALF_D], staged_half[j][h][:])
 
         group_x(0)
         quantize_d(0)
@@ -457,8 +469,10 @@ def tile_attend_grag_q_kernel(tc, xT, dT, us, ts, lk, wt, offs, out):
         store(0)
         store(1)
         quantize_g(2)
-        product(2)
-        group_g(3)
-        quantize_g(3)
-        store(2)
-        product_and_store_in_halves(3)
+        product_in_halves(2)
+        group_and_quantize_last(3)
+        store_half(2, 0, nc.scalar.copy)
+        product_in_halves(3)
+        store_half(2, 1, nc.vector.tensor_copy)
+        store_half(3, 0, nc.scalar.copy)
+        store_half(3, 1, nc.vector.tensor_copy)

@@ -219,7 +219,7 @@ def tile_attend_grag_q_kernel(tc, xT, dT, us, ts, lk, wt, offs, out):
             f[j] = placed([P, SLOTS], F32, "f%d" % j, F_AT[j])
         inverse = tiles("inverse", [P, 2], F32)
         factor = tiles("factor", [P, 2], F32)
-        terms = [tiles("term%d_" % k, [P, 2, P, 2], F32, ADDED) for k in range(2)]
+        terms = [tiles("term%d_" % k, [P, PACK, P], F32, ADDED) for k in range(2)]
         difference = tiles("difference", [P, SLOTS], F32, PAIRED)
         g_words = [tiles("g_words%d_" % u, [P, HALF], BF16, PAIRED) for u in range(2)]
         g_grouped = tiles("g_grouped", [P, P * PACK], BF16, PAIRED[:-1])
@@ -319,14 +319,14 @@ def tile_attend_grag_q_kernel(tc, xT, dT, us, ts, lk, wt, offs, out):
             nc.scalar.activation(factor[j][:, k:k + 1], signed_wu[:, j, k:k + 1], ACT.Copy, scale=inverse[j][:, k:k + 1])
 
         def scale_term(j, k):
-            source = (e, f)[k][j][:].rearrange("r (p u v) -> r u p v", u=2, v=2)
-            nc.scalar.activation(terms[k][j][:], source, ACT.Copy, scale=factor[j][:, k:k + 1])
+            source = (e, f)[k][j][:].rearrange("r (p t) -> r p t", t=PACK)
+            nc.scalar.activation(terms[k][j][:].rearrange("r t p -> r p t"), source, ACT.Copy, scale=factor[j][:, k:k + 1])
 
         def turn_term(j, k):
             if k == 0:
                 turned_g[j] = psum_bank("turned_g%d" % j, TURNED_G_BANK[j], [P, PACK, P])
             for t in range(PACK):
-                nc.tensor.matmul(turned_g[j][:, t, :], terms[k][j][:, t // 2, :, t % 2], ident[:], is_transpose=True,
+                nc.tensor.matmul(turned_g[j][:, t, :], terms[k][j][:, t, :], ident[:], is_transpose=True,
                                  start=(k == 0 and t == 0), stop=(k == 1 and t == PACK - 1))
 
         def round_turned_g(j):

@@ -44,10 +44,11 @@ DT_CODES_AT = 2
 TURNED_PLANE2_AT = 4
 NEG_Z13_AT = 5.5
 PLANE3_AT = 7.5
-TURNED_PLANE3_AT = 5.5
+F2_AT = TURNED_PLANE3_AT = 23
 WINDOW2_AT = 9
 LK_AT = (9, 11, 13, 15)
 NEG_Z02_AT = 17
+DIFFERENCE1_AT = 15
 F_AT = {1: 19, 3: 21}
 
 TS_COL_BANK, TS_ROW_BANK, TS_PLACES_BANK, UW_BANK = 5, 2, 5, 4
@@ -214,13 +215,15 @@ def tile_attend_grag_q_kernel(tc, xT, dT, us, ts, lk, wt, offs, out):
         neg_z = [placed([P, SLOTS], F32, "neg_z%d" % j, (NEG_Z02_AT, NEG_Z13_AT)[j % 2]) for j in range(ROW_TILES)]
         neg_max = tiles("neg_max", [P, 1], F32)
         e = tiles("e", [P, SLOTS], F32)
-        f = tiles("f", [P, SLOTS], F32, ADDED)
+        f = tiles("f", [P, SLOTS], F32, (0,))
+        f[2] = placed([P, SLOTS], F32, "f2", F2_AT)
         for j in PAIRED:
             f[j] = placed([P, SLOTS], F32, "f%d" % j, F_AT[j])
         inverse = tiles("inverse", [P, 2], F32)
         factor = tiles("factor", [P, 2], F32)
         terms = [tiles("term%d_" % k, [P, PACK, P], F32, ADDED) for k in range(2)]
-        difference = tiles("difference", [P, SLOTS], F32, PAIRED)
+        difference = tiles("difference", [P, SLOTS], F32, (3,))
+        difference[1] = placed([P, SLOTS], F32, "difference1", DIFFERENCE1_AT)
         g_words = [tiles("g_words%d_" % u, [P, HALF], BF16, PAIRED) for u in range(2)]
         g_grouped = tiles("g_grouped", [P, P * PACK], BF16, PAIRED[:-1])
         last_grouped = tiles("last_grouped", [P, P // 2 * PACK], BF16, range(2))
@@ -441,11 +444,10 @@ def tile_attend_grag_q_kernel(tc, xT, dT, us, ts, lk, wt, offs, out):
         make_factors(1)
         invert_sum(2, 1)
         make_term_factor(2, 1)
-        group_turned_plane(3)
         subtract(1)
         invert(3)
         scale_term(2, 1)
-        quantize_turned_planes(2)
+        group_turned_plane(3)
         round_g(1, 0)
         turn_g(1, 0)
         make_factors(3)
@@ -453,6 +455,7 @@ def tile_attend_grag_q_kernel(tc, xT, dT, us, ts, lk, wt, offs, out):
         turn_g(1, 1)
         turn_term(2, 1)
         round_turned_g(0)
+        quantize_turned_planes(2)
         warm_up(0)
         group_g(1)
         round_turned_g_by_places(2)

@@ -152,20 +152,25 @@ def tile_attend_grag_q_kernel(tc, xT, dT, us, ts, lk, wt, offs, out):
         ts_places = keep.tile([P, PACK], F32, name="ts_places")
         nc.scalar.copy(ts_places[:], bank[:, :, P - 1])
 
-        d_planes01 = keep.tile([P, 2, SLOTS], BF16, name="d_planes01", align_bytes=64)
+        picked_plane = tiles("d_plane", [P, SLOTS], BF16, (0, 1, 2))
+        picked_plane[3] = placed([P, SLOTS], BF16, "d_plane3", PLANE3_AT)
         d_grouped = keep.tile([P, SLOTS, PACK], BF16, name="d_grouped", align_bytes=64)
-        nc.vector.tensor_copy(d_planes01[:, 0, :], d_window[0][:].indirect(offsets[:]))
-        turn_plane(d_planes01[:, 0, :], 0)
+
+        def pick_plane(t):
+            nc.scalar.copy(picked_plane[t][:], d_grouped[:, :, t])
+
+        nc.vector.tensor_copy(d_grouped[:, :, 0], d_window[0][:].indirect(offsets[:]))
+        pick_plane(0)
+        turn_plane(picked_plane[0][:], 0)
         group_turned_plane(0)
-        nc.vector.tensor_copy(d_planes01[:, 1, :], d_window[1][:].indirect(offsets[:]))
+        nc.vector.tensor_copy(d_grouped[:, :, 1], d_window[1][:].indirect(offsets[:]))
         x_planes = xT.rearrange("(p t) r -> p t r", t=PACK)
         x_raw = [placed([P, PACK, P], F32, "x_raw%d" % j, X_RAW_AT[j]) for j in range(ROW_TILES)]
         for j in range(ROW_TILES):
             nc.sync.dma_start(x_raw[j][:], x_planes[:, :, j * P:(j + 1) * P])
-        turn_plane(d_planes01[:, 1, :], 1)
+        pick_plane(1)
+        turn_plane(picked_plane[1][:], 1)
         group_turned_plane(1)
-        nc.scalar.copy(d_grouped[:, :, 0:2].rearrange("p (c m) t -> p c t m", m=4),
-                       d_planes01[:].rearrange("p t (c m) -> p c t m", m=4))
 
         bank = psum_bank("uw_bank", UW_BANK, [P, BANK_BLOCKS, P])
         nc.tensor.transpose(bank[:, 0, :], uw_rows[:], ident[:])
@@ -182,12 +187,6 @@ def tile_attend_grag_q_kernel(tc, xT, dT, us, ts, lk, wt, offs, out):
             for k, signed_us in enumerate((uw, neg_us)):
                 nc.scalar.activation(signed_wu[:, j, k:k + 1], uw[:, ROW_TILES + j:ROW_TILES + j + 1], ACT.Copy,
                                      scale=signed_us[:, j:j + 1])
-
-        picked_plane = {2: keep.tile([P, SLOTS], BF16, name="d_plane2", align_bytes=64),
-                        3: placed([P, SLOTS], BF16, "d_plane3", PLANE3_AT)}
-
-        def pick_plane(t):
-            nc.scalar.copy(picked_plane[t][:], d_grouped[:, :, t])
 
         nc.vector.tensor_copy(d_grouped[:, :, 2], d_window[2][:].indirect(offsets[:]))
         lk_rows = [placed([P, SLOTS], F32, "lk_rows%d" % j, LK_AT[j]) for j in range(ROW_TILES)]

from contextlib import ExitStack

import concourse.mybir as mybir
from concourse.masks import make_identity

F32 = mybir.dt.float32
BF16 = mybir.dt.bfloat16
U32 = mybir.dt.uint32
U16 = mybir.dt.uint16
U8 = mybir.dt.uint8
E4M3X4 = mybir.dt.float8_e4m3fn_x4
E5M2X4 = mybir.dt.float8_e5m2_x4
ALU = mybir.AluOpType
ACT = mybir.ActivationFunctionType
AX = mybir.AxisListType

P = 128
PACK = 4
D = 512
R = 512
SLOTS = 512
DOCS = 2048
ROW_TILES = R // P
SLOT_TILES = SLOTS // P
HALF = SLOTS // 2
HALF_D = D // 2
QUARTER = HALF_D // PACK
OFFSETS_PER_COLUMN = 16
BANK_BLOCKS = 4

BANK_BYTES = 2048
KIB = 1024

ADDED = (0, 2)
PAIRED = (1, 3)
BY_SLOTS = (2, 3)
IN_HALVES = (2, 3)
TURNED_GROUPS = ((0, 1), (2,), (3,))

WINDOW1_AT = 0
X_RAW_AT = (0, 2, 4, 6)
D_CODES_AT = 0
DT_CODES_AT = 2
TURNED_PLANE2_AT = 4
NEG_Z13_AT = 5.5
PLANE3_AT = 7.5
F2_AT = TURNED_PLANE3_AT = 23
WINDOW2_AT = 9
LK_AT = (9, 11, 13, 15)
NEG_Z02_AT = 17
DIFFERENCE1_AT = 15
F_AT = {1: 19, 3: 21}

TS_COL_BANK, TS_ROW_BANK, TS_PLACES_BANK, UW_BANK = 5, 2, 5, 4
PLANE_BANK = (0, 1, 7, 5)
FIRST_SCORE_BANK = (0, 1)
SCORE_BANK = {1: 2, 2: 3, 3: 5}
TURNED_SCORE_BANK = {2: 2, 3: 1}
TURNED_G_BANK = (4, 6, 0, 2)
PRODUCT_BANK = (3, 4)
HALF_PRODUCT_BANK = {2: (7, 5), 3: (1, 6)}

WARM_UP_COLUMNS = (slice(0, HALF), slice(HALF, HALF + P))

FLOPS = 2 * 2 * R * SLOTS * D
BYTES = 4 * (D * R + D * DOCS + R * SLOTS + R * D + DOCS + 2 * R) + 2 * P * SLOTS // OFFSETS_PER_COLUMN


def tile_attend_grag_q_kernel(tc, xT, dT, us, ts, lk, wt, offs, out):
    nc = tc.nc
    with ExitStack() as ctx:
        keep = ctx.enter_context(tc.tile_pool(name="keep", bufs=1))
        reused = ctx.enter_context(tc.tile_pool(name="reused", bufs=1))
        psum = ctx.enter_context(tc.psum_pool(name="psum", bufs=1))

        def psum_bank(name, n, shape):
            return psum.tile(shape, F32, name=name, offset=n * BANK_BYTES)

        def placed(shape, dtype, name, kib):
            return reused.tile(shape, dtype, name=name, align_bytes=64, offset=int(kib * KIB))

        def tiles(name, shape, dtype, which=range(ROW_TILES)):
            return {j: keep.tile(shape, dtype, name="%s%d" % (name, j), align_bytes=64) for j in which}

        offsets = keep.tile([P, SLOTS // OFFSETS_PER_COLUMN], U16, name="offsets")
        d_planes = dT.rearrange("(p t) n -> t p n", t=PACK)
        d_window = tiles("d_window", [P, DOCS], F32, (0, 3))
        d_window[1] = placed([P, DOCS], F32, "d_window1", WINDOW1_AT)
        d_window[2] = placed([P, DOCS], F32, "d_window2", WINDOW2_AT)
        ts_window = keep.tile([P, DOCS], F32, name="ts_window")
        nc.vector.memset(ts_window[0:P - 1, :], 0.0)
        uw_rows = keep.tile([P, P], F32, name="uw_rows")
        nc.gpsimd.memset(uw_rows[:], 0.0)

        nc.sync.dma_start(offsets[:], offs)
        nc.sync.dma_start(ts_window[P - 1:P, :], ts[0:1, :])
        nc.sync.dma_start(d_window[0][:], d_planes[0])
        nc.sync.dma_start(uw_rows[0:ROW_TILES, :], us.rearrange("(j p) o -> j (p o)", p=P))
        nc.sync.dma_start(uw_rows[ROW_TILES:2 * ROW_TILES, :], wt.rearrange("(j p) o -> j (p o)", p=P))
        for t in range(1, PACK):
            nc.sync.dma_start(d_window[t][:], d_planes[t])

        ident = keep.tile([P, P], F32, name="ident")
        make_identity(nc, ident[:])

        one = keep.tile([P, 1], F32, name="one")
        nc.scalar.activation(one[:], ident[:, 0:1], ACT.Exp, scale=0.0)

        dt_codes = placed([P, 2, PACK * QUARTER], U32, "dt_codes", DT_CODES_AT)
        dt_scales = keep.tile([P, 2, PACK * QUARTER], U8, name="dt_scales", align_bytes=64)
        dt_grouped = [keep.tile([P, 2, 2, QUARTER * PACK], BF16, name="dt_grouped01", align_bytes=64),
                      placed([P, 2, 1, QUARTER * PACK], BF16, "dt_grouped2", TURNED_PLANE2_AT),
                      placed([P, 2, 1, QUARTER * PACK], BF16, "dt_grouped3", TURNED_PLANE3_AT)]
        dt_plane = [tile[:, :, v, :] for group, tile in zip(TURNED_GROUPS, dt_grouped) for v in range(len(group))]
        turned_plane = {}

        def quantize_turned_planes(n):
            cols = slice(TURNED_GROUPS[n][0] * QUARTER, (TURNED_GROUPS[n][-1] + 1) * QUARTER)
            for h in range(2):
                nc.vector.quantize_mx(out=dt_codes[:, h, cols].bitcast(E4M3X4), scales=dt_scales[:, h, cols],
                                      in_=dt_grouped[n][:, h].rearrange("p v x -> p (v x)"))

        def turn_plane(plane, t):
            words = plane.bitcast(F32)
            turned_plane[t] = psum_bank("turned_plane%d" % t, PLANE_BANK[t], [P, BANK_BLOCKS, P])
            for u in range(2):
                nc.tensor.transpose(turned_plane[t][:, u, :], words[:, u:HALF:2], ident[:])

        def interleave_words(copy, grouped, bank):
            copy(grouped.bitcast(F32).rearrange("p (c m u) -> p c u m", m=2, u=2),
                 bank[:, 0:2, :].rearrange("p u (c m) -> p c u m", m=2))

        def group_turned_plane(t):
            nc.scalar.copy(dt_plane[t].bitcast(F32).rearrange("p h (c m u) -> p h c u m", m=2, u=2),
                           turned_plane[t][:, 0:2, :].rearrange("p u (h c m) -> p h c u m", h=2, m=2))

        ts_listed = keep.tile([P, SLOTS], F32, name="ts_listed")
        nc.vector.tensor_copy(ts_listed[:], ts_window[:].indirect(offsets[:]))
        bank = psum_bank("ts_col_bank", TS_COL_BANK, [P, SLOT_TILES, P])
        for s in range(SLOT_TILES):
            nc.tensor.transpose(bank[:, s, :], ts_listed[:, s * P:(s + 1) * P], ident[:])
        ts_col = keep.tile([P, SLOT_TILES], F32, name="ts_col")
        nc.scalar.copy(ts_col[:], bank[:, :, P - 1])
        bank = psum_bank("ts_row_bank", TS_ROW_BANK, [P, SLOT_TILES, P])
        for s in range(SLOT_TILES):
            nc.tensor.transpose(bank[:, s, :], ts_col[:, s:s + 1].to_broadcast([P, P]), ident[:])
        ts_row = keep.tile([P, SLOTS], F32, name="ts_row")
        nc.scalar.copy(ts_row[:], bank[:].rearrange("m s p -> m (s p)"))
        bank = psum_bank("ts_places_bank", TS_PLACES_BANK, [P, PACK, P])
        for t in range(PACK):
            nc.tensor.transpose(bank[:, t, :], ts_listed[:, t:SLOTS:PACK], ident[:])
        ts_places = keep.tile([P, PACK], F32, name="ts_places")
        nc.scalar.copy(ts_places[:], bank[:, :, P - 1])

        picked_plane = tiles("d_plane", [P, SLOTS], BF16, (0, 1, 2))
        picked_plane[3] = placed([P, SLOTS], BF16, "d_plane3", PLANE3_AT)
        d_grouped = keep.tile([P, SLOTS, PACK], BF16, name="d_grouped", align_bytes=64)

        def pick_plane(t):
            nc.scalar.copy(picked_plane[t][:], d_grouped[:, :, t])

        nc.vector.tensor_copy(d_grouped[:, :, 0], d_window[0][:].indirect(offsets[:]))
        pick_plane(0)
        turn_plane(picked_plane[0][:], 0)
        group_turned_plane(0)
        nc.vector.tensor_copy(d_grouped[:, :, 1], d_window[1][:].indirect(offsets[:]))
        x_planes = xT.rearrange("(p t) r -> p t r", t=PACK)
        x_raw = [placed([P, PACK, P], F32, "x_raw%d" % j, X_RAW_AT[j]) for j in range(ROW_TILES)]
        for j in range(ROW_TILES):
            nc.sync.dma_start(x_raw[j][:], x_planes[:, :, j * P:(j + 1) * P])
        pick_plane(1)
        turn_plane(picked_plane[1][:], 1)
        group_turned_plane(1)

        bank = psum_bank("uw_bank", UW_BANK, [P, BANK_BLOCKS, P])
        nc.tensor.transpose(bank[:, 0, :], uw_rows[:], ident[:])
        uw = keep.tile([P, 2 * ROW_TILES], F32, name="uw")
        nc.scalar.copy(uw[:], bank[:, 0, 0:2 * ROW_TILES])
        neg_us = keep.tile([P, ROW_TILES], F32, name="neg_us")
        nc.scalar.activation(neg_us[:], uw[:, 0:ROW_TILES], ACT.Copy, scale=-1.0)
        stats = [keep.tile([P, 3], F32, name="stats%d" % j) for j in range(ROW_TILES)]
        for j in PAIRED:
            nc.scalar.activation(stats[j][:, 2:3], uw[:, ROW_TILES + j:ROW_TILES + j + 1], ACT.Copy,
                                 scale=uw[:, j:j + 1])
        signed_wu = keep.tile([P, ROW_TILES, 2], F32, name="signed_wu")
        for j in ADDED:
            for k, signed_us in enumerate((uw, neg_us)):
                nc.scalar.activation(signed_wu[:, j, k:k + 1], uw[:, ROW_TILES + j:ROW_TILES + j + 1], ACT.Copy,
                                     scale=signed_us[:, j:j + 1])

        nc.vector.tensor_copy(d_grouped[:, :, 2], d_window[2][:].indirect(offsets[:]))
        lk_rows = [placed([P, SLOTS], F32, "lk_rows%d" % j, LK_AT[j]) for j in range(ROW_TILES)]
        for j in range(ROW_TILES):
            nc.sync.dma_start(lk_rows[j][:], lk[j * P:(j + 1) * P, :])
        pick_plane(2)
        turn_plane(picked_plane[2][:], 2)
        half_columns = HALF // OFFSETS_PER_COLUMN
        for half in range(2):
            nc.vector.tensor_copy(d_grouped[:, half * HALF:(half + 1) * HALF, 3],
                                  d_window[3][:].indirect(offsets[:, half * half_columns:(half + 1) * half_columns]))

        d_codes = placed([P, SLOTS], U32, "d_codes", D_CODES_AT)
        d_scales = keep.tile([P, SLOTS], U8, name="d_scales", align_bytes=64)

        def quantize_d(half):
            cols = slice(half * HALF, (half + 1) * HALF)
            nc.vector.quantize_mx(out=d_codes[:, cols].bitcast(E4M3X4), scales=d_scales[:, cols],
                                  in_=d_grouped[:, cols, :].rearrange("p i t -> p (i t)"))

        x_grouped = tiles("x_grouped", [P, P, PACK], BF16)
        x_codes = tiles("x_codes", [P, P], U32)
        x_scales = tiles("x_scales", [P, P], U8)
        scaled = tiles("scaled", [P, SLOT_TILES, P], F32, BY_SLOTS)
        neg_z = [placed([P, SLOTS], F32, "neg_z%d" % j, (NEG_Z02_AT, NEG_Z13_AT)[j % 2]) for j in range(ROW_TILES)]
        neg_max = tiles("neg_max", [P, 1], F32)
        e = tiles("e", [P, SLOTS], F32)
        f = tiles("f", [P, SLOTS], F32, (0,))
        f[2] = placed([P, SLOTS], F32, "f2", F2_AT)
        for j in PAIRED:
            f[j] = placed([P, SLOTS], F32, "f%d" % j, F_AT[j])
        inverse = tiles("inverse", [P, 2], F32)
        factor = tiles("factor", [P, 2], F32)
        terms = [tiles("term%d_" % k, [P, PACK, P], F32, ADDED) for k in range(2)]
        difference = tiles("difference", [P, SLOTS], F32, (3,))
        difference[1] = placed([P, SLOTS], F32, "difference1", DIFFERENCE1_AT)
        g_words = [tiles("g_words%d_" % u, [P, HALF], BF16, PAIRED) for u in range(2)]
        g_grouped = tiles("g_grouped", [P, P * PACK], BF16, PAIRED[:-1])
        last_grouped = tiles("last_grouped", [P, P // 2 * PACK], BF16, range(2))
        for j in ADDED:
            g_grouped[j] = placed([P, P * PACK], BF16, "g_grouped%d" % j, F_AT[j + 1])
        g_places = keep.tile([P, PACK, P], BF16, name="g_places", align_bytes=64)
        g_codes = tiles("g_codes", [P, P], U32)
        g_scales = tiles("g_scales", [P, P], U8)
        staged = tiles("staged", [P, D], F32, (0, 1))
        staged_half = {j: tiles("staged_half%d_" % j, [P, HALF_D], F32, range(2)) for j in IN_HALVES}
        scores = {}
        turned_scores = {}
        turned_g = {}
        sums = {}

        def group_x(j):
            nc.scalar.copy(x_grouped[j][:].rearrange("p (c m) t -> p c t m", m=4),
                           x_raw[j][:].rearrange("p t (c m) -> p c t m", m=4))

        def quantize_x(j):
            nc.vector.quantize_mx(out=x_codes[j][:].bitcast(E4M3X4), scales=x_scales[j][:],
                                  in_=x_grouped[j][:].rearrange("p r t -> p (r t)"))

        def score_half_by_rows(j, half):
            cols = slice(half * HALF, (half + 1) * HALF)
            a = psum_bank("first_scores%d" % half, FIRST_SCORE_BANK[half], [P, HALF])
            nc.tensor.matmul_mx(out=a[:], lhsT=x_codes[j][:].bitcast(E4M3X4), lhsT_scale=x_scales[j][:],
                                rhs=d_codes[:, cols].bitcast(E4M3X4), rhs_scale=d_scales[:, cols],
                                start=True, stop=True)
            nc.vector.scalar_tensor_tensor(neg_z[j][:, cols], a[:], neg_us[:, j:j + 1], ts_row[:, cols], ALU.mult, ALU.mult)

        def row_minimum(j):
            nc.vector.tensor_reduce(neg_max[j][:], neg_z[j][:], AX.X, ALU.min)

        def score_by_rows(j):
            scores[j] = psum_bank("scores%d" % j, SCORE_BANK[j], [P, SLOTS])
            nc.tensor.matmul_mx(out=scores[j][:], lhsT=x_codes[j][:].bitcast(E4M3X4), lhsT_scale=x_scales[j][:],
                                rhs=d_codes[:].bitcast(E4M3X4), rhs_scale=d_scales[:], start=True, stop=True)

        def scale_by_rows(j):
            nc.vector.scalar_tensor_tensor(neg_z[j][:], scores[j][:], neg_us[:, j:j + 1], ts_row[:], ALU.mult, ALU.mult)

        def score_by_slots(j):
            scores[j] = psum_bank("scores%d" % j, SCORE_BANK[j], [P, SLOT_TILES, P])
            for s in range(SLOT_TILES):
                cols = slice(s * P, (s + 1) * P)
                nc.tensor.matmul_mx(out=scores[j][:, s, :], lhsT=d_codes[:, cols].bitcast(E4M3X4),
                                    lhsT_scale=d_scales[:, cols], rhs=x_codes[j][:].bitcast(E4M3X4),
                                    rhs_scale=x_scales[j][:], start=True, stop=True)

        def scale_by_slots(j):
            for s in range(SLOT_TILES):
                nc.scalar.activation(scaled[j][:, s, :], scores[j][:, s, :], ACT.Copy, scale=ts_col[:, s:s + 1])

        def turn_scores(j):
            turned_scores[j] = psum_bank("turned_scores%d" % j, TURNED_SCORE_BANK[j], [P, SLOTS])
            for s in range(SLOT_TILES):
                nc.tensor.transpose(turned_scores[j][:, s * P:(s + 1) * P], scaled[j][:, s, :], ident[:])

        def scale_turned_scores(j):
            nc.vector.tensor_scalar(neg_z[j][:], turned_scores[j][:], neg_us[:, j:j + 1], None, ALU.mult, ALU.min,
                                    accum_out=neg_max[j][:])

        def exponentials(j):
            nc.scalar.activation(e[j][:], neg_z[j][:], ACT.Exp, bias=neg_max[j][:], scale=-1.0, accum_out=stats[j][:, 0:1])

        def weigh(j):
            nc.vector.scalar_tensor_tensor(f[j][:], e[j][:], one[:], lk_rows[j][:], ALU.mult, ALU.mult,
                                           accum_out=stats[j][:, 1:2])

        def invert(j):
            nc.vector.reciprocal(inverse[j][:], stats[j][:, 0:2])

        def make_factors(j):
            nc.vector.tensor_tensor(factor[j][:], inverse[j][:], stats[j][:, 1:3], ALU.mult)

        def subtract(j):
            nc.vector.scalar_tensor_tensor(difference[j][:], e[j][:], factor[j][:, 0:1], f[j][:], ALU.mult, ALU.subtract)

        def round_g(j, u):
            by_four = difference[j][:].rearrange("r (p t) -> r p t", t=PACK)
            ts_by_four = ts_row[:].rearrange("r (p t) -> r p t", t=PACK)
            nc.vector.scalar_tensor_tensor(g_words[u][j][:].rearrange("r (p v) -> r p v", v=2),
                                           by_four[:, :, 2 * u:2 * u + 2], factor[j][:, 1:2],
                                           ts_by_four[:, :, 2 * u:2 * u + 2], ALU.mult, ALU.mult)

        def turn_g(j, u):
            if u == 0:
                turned_g[j] = psum_bank("turned_g%d" % j, TURNED_G_BANK[j], [P, PACK, P])
            nc.tensor.transpose(turned_g[j][:, u, :], g_words[u][j][:].bitcast(F32), ident[:])

        def invert_sum(j, k):
            nc.vector.reciprocal(inverse[j][:, k:k + 1], stats[j][:, k:k + 1])

        def make_term_factor(j, k):
            nc.scalar.activation(factor[j][:, k:k + 1], signed_wu[:, j, k:k + 1], ACT.Copy, scale=inverse[j][:, k:k + 1])

        def scale_term(j, k):
            source = (e, f)[k][j][:].rearrange("r (p t) -> r p t", t=PACK)
            nc.scalar.activation(terms[k][j][:].rearrange("r t p -> r p t"), source, ACT.Copy, scale=factor[j][:, k:k + 1])

        def turn_term(j, k):
            if k == 0:
                turned_g[j] = psum_bank("turned_g%d" % j, TURNED_G_BANK[j], [P, PACK, P])
            for t in range(PACK):
                nc.tensor.matmul(turned_g[j][:, t, :], terms[k][j][:, t, :], ident[:], is_transpose=True,
                                 start=(k == 0 and t == 0), stop=(k == 1 and t == PACK - 1))

        def round_turned_g(j):
            nc.vector.tensor_tensor(g_grouped[j][:].rearrange("p (c m t) -> p c t m", m=2, t=PACK),
                                    turned_g[j][:].rearrange("p t (c m) -> p c t m", m=2),
                                    ts_places[:].unsqueeze(1).unsqueeze(3).to_broadcast([P, P // 2, PACK, 2]), ALU.mult)

        def round_turned_g_by_places(j):
            for t in range(PACK):
                nc.scalar.activation(g_places[:, t, :], turned_g[j][:, t, :], ACT.Copy, scale=ts_places[:, t:t + 1])

        def weave_places(j):
            nc.vector.tensor_copy(g_grouped[j][:].rearrange("p (c m t) -> p c t m", m=4, t=PACK),
                                  g_places[:].rearrange("p t (c m) -> p c t m", m=4))

        def group_g(j):
            interleave_words(nc.scalar.copy, g_grouped[j][:], turned_g[j][:])

        def group_and_quantize_last(j):
            for half in range(2):
                interleave_words(nc.vector.tensor_copy, last_grouped[half][:],
                                 turned_g[j][:, :, half * (P // 2):(half + 1) * (P // 2)])
            for half in range(2):
                cols = slice(half * (P // 2), (half + 1) * (P // 2))
                nc.vector.quantize_mx(out=g_codes[j][:, cols].bitcast(E5M2X4), scales=g_scales[j][:, cols],
                                      in_=last_grouped[half][:])

        def quantize_g(j):
            nc.vector.quantize_mx(out=g_codes[j][:].bitcast(E5M2X4), scales=g_scales[j][:], in_=g_grouped[j][:])

        def product(j):
            sums[j] = psum_bank("sums%d" % j, PRODUCT_BANK[j], [P, D])
            nc.tensor.matmul_mx(out=sums[j][:], lhsT=g_codes[j][:].bitcast(E5M2X4), lhsT_scale=g_scales[j][:],
                                rhs=dt_codes[:].rearrange("p h x -> p (h x)").bitcast(E4M3X4),
                                rhs_scale=dt_scales[:].rearrange("p h x -> p (h x)"), start=True, stop=True)

        def warm_up(j):
            unread = psum_bank("unread", TURNED_G_BANK[j], [P, SLOTS])
            for cols in WARM_UP_COLUMNS:
                nc.tensor.matmul_mx(out=unread[:, cols], lhsT=x_codes[j][:].bitcast(E4M3X4), lhsT_scale=x_scales[j][:],
                                    rhs=d_codes[:, cols].bitcast(E4M3X4), rhs_scale=d_scales[:, cols],
                                    start=True, stop=True)

        def store(j):
            for h in range(2):
                cols = slice(h * HALF_D, (h + 1) * HALF_D)
                nc.scalar.copy(staged[j][:, cols].rearrange("r (c m t) -> r c t m", m=2, t=PACK),
                               sums[j][:, cols].rearrange("r (t c m) -> r c t m", t=PACK, m=2))
                nc.sync.dma_start(out[j * P:(j + 1) * P, cols], staged[j][:, cols])

        def product_in_halves(j):
            for h in range(2):
                sums[j, h] = psum_bank("sums%d_%d" % (j, h), HALF_PRODUCT_BANK[j][h], [P, HALF_D])
                nc.tensor.matmul_mx(out=sums[j, h][:], lhsT=g_codes[j][:].bitcast(E5M2X4), lhsT_scale=g_scales[j][:],
                                    rhs=dt_codes[:, h].bitcast(E4M3X4), rhs_scale=dt_scales[:, h], start=True, stop=True)

        def store_half(j, h, copy_out):
            copy_out(staged_half[j][h][:].rearrange("r (c m t) -> r c t m", m=2, t=PACK),
                     sums[j, h][:].rearrange("r (t c m) -> r c t m", t=PACK, m=2))
            nc.sync.dma_start(out[j * P:(j + 1) * P, h * HALF_D:(h + 1) * HALF_D], staged_half[j][h][:])

        group_x(0)
        quantize_d(0)
        quantize_x(0)
        quantize_d(1)
        group_x(1)
        quantize_x(1)
        quantize_turned_planes(0)
        score_half_by_rows(0, 0)
        score_half_by_rows(0, 1)
        score_by_rows(1)
        group_x(2)
        quantize_x(2)
        score_by_slots(2)
        row_minimum(0)
        group_x(3)
        group_turned_plane(2)
        pick_plane(3)
        quantize_x(3)
        score_by_slots(3)
        scale_by_rows(1)
        exponentials(0)
        scale_by_slots(2)
        turn_scores(2)
        scale_by_slots(3)
        turn_scores(3)
        turn_plane(picked_plane[3][:], 3)
        quantize_turned_planes(1)
        row_minimum(1)
        invert_sum(0, 0)
        weigh(0)
        make_term_factor(0, 0)
        exponentials(1)
        invert_sum(0, 1)
        scale_turned_scores(2)
        scale_term(0, 0)
        turn_term(0, 0)
        make_term_factor(0, 1)
        scale_turned_scores(3)
        exponentials(2)
        weigh(1)
        invert_sum(2, 0)
        exponentials(3)
        make_term_factor(2, 0)
        scale_term(0, 1)
        turn_term(0, 1)
        weigh(2)
        invert(1)
        weigh(3)
        scale_term(2, 0)
        turn_term(2, 0)
        make_factors(1)
        invert_sum(2, 1)
        make_term_factor(2, 1)
        subtract(1)
        invert(3)
        scale_term(2, 1)
        group_turned_plane(3)
        round_g(1, 0)
        turn_g(1, 0)
        make_factors(3)
        round_g(1, 1)
        turn_g(1, 1)
        turn_term(2, 1)
        round_turned_g(0)
        quantize_turned_planes(2)
        warm_up(0)
        group_g(1)
        round_turned_g_by_places(2)
        subtract(3)
        quantize_g(0)
        product(0)
        quantize_g(1)
        product(1)
        round_g(3, 0)
        turn_g(3, 0)
        round_g(3, 1)
        turn_g(3, 1)
        weave_places(2)
        store(0)
        store(1)
        quantize_g(2)
        product_in_halves(2)
        group_and_quantize_last(3)
        store_half(2, 0, nc.scalar.copy)
        product_in_halves(3)
        store_half(2, 1, nc.vector.tensor_copy)
        store_half(3, 0, nc.scalar.copy)
        store_half(3, 1, nc.vector.tensor_copy)
